import numpy as np
import ml_dtypes


def mxq(x, axis, fmt="e4m3"):
    dtype, down = {"e4m3": (ml_dtypes.float8_e4m3fn, 7), "e5m2": (ml_dtypes.float8_e5m2, 14)}[fmt]
    v = np.moveaxis(np.asarray(x, np.float32).astype(ml_dtypes.bfloat16).astype(np.float64), axis, -1)
    blocks = v.reshape(v.shape[:-1] + (-1, 32))
    amax = np.abs(blocks).max(-1, keepdims=True)
    byte = np.maximum(np.where(amax > 0, np.frexp(amax)[1] - 1 + 127, 0) - down, 1)
    scale = np.exp2(byte - 127.0)
    codes = (blocks / scale).astype(np.float32).astype(dtype).astype(np.float64)
    return np.moveaxis((codes * scale).reshape(v.shape), -1, axis)


WIDE = False


def mx_kscale(k):
    if not WIDE:
        return np.ones(k)
    levels = np.array([18, -18])
    if k % 512:
        return np.exp2(np.random.permutation(np.resize(levels, k // 32))).repeat(32)
    a = np.empty((k // 512, 16))
    for p in range(k // 512):
        a[p, :8] = np.random.permutation(np.resize(levels, 8))
        for g in range(8):
            far = levels[np.abs(levels - a[p, g]) >= 10]
            a[p, g + 8] = far[np.random.randint(len(far))]
    return np.exp2(a.ravel()).repeat(32)


def f64(x):
    return np.asarray(x).astype(np.float64)


def striped(idx):
    return np.tile(np.asarray(idx).reshape(-1, 16).T, (8, 1)).astype(np.uint16)


def unstriped(offs):
    return offs[:16].T.reshape(-1).astype(np.int64)

def planes(y):
    n, m = y.shape
    v = y.astype(np.float32).astype(ml_dtypes.bfloat16).astype(np.float64).reshape(n // 32, 32, m)
    top = np.abs(v).max(1)
    byte = np.clip(np.where(top > 0, np.frexp(top)[1] - 1 + 127 - 7, 1), 1, 254)
    codes = (v * np.exp2(127.0 - byte)[:, None, :]).reshape(n, m).astype(np.float32).astype(ml_dtypes.float8_e4m3fn).view(np.uint8)
    words = codes.reshape(n // 512, 128, 4, m).transpose(0, 1, 3, 2)
    return np.ascontiguousarray(words), np.ascontiguousarray(byte.astype(np.uint8).reshape(n // 512, 16, m))


def setup_inputs():
    n = np.random.standard_normal
    uni = np.random.uniform
    idx = np.random.permutation(2048)[:1024]
    bag = np.random.permutation(np.repeat(np.arange(512), 2))
    slot = np.argsort(bag, kind="stable")
    f_m = mx_kscale(512)
    return {
        "vT": (0.5 * n((512, 2048))).astype(np.float32),
        "W": (n((512, 512)) / np.sqrt(512) * f_m[:, None]).astype(np.float32),
        "dz": (n((512, 512)) / f_m[:, None]).astype(np.float32),
        "tw": np.tile(uni(0.75, 1.3, 2048), (128, 1)).astype(np.float32),
        "offs": striped(idx),
        "boffs": striped(bag),
        "soffs": striped(slot),
    }


def reference(vT, W, dz, tw, offs, boffs, soffs):
    idx = unstriped(offs)
    bag = unstriped(boffs)
    slot = unstriped(soffs)
    vT_c = f64(vT)[:, idx]
    vT_c_y = vT_c[:, slot]
    s = vT_c_y.reshape(512, 512, 2).sum(-1)
    dh = mxq(f64(W), 0, "e4m3").T @ mxq(f64(dz), 0, "e5m2")
    h = np.tanh(s)
    e = dh * (1.0 - np.square(h))
    e_c = e[:, bag]
    tw_c = f64(tw)[:1][:, idx]
    dv = tw_c * e_c
    out_0 = np.zeros((512, 2048))
    out_0[:, idx] = dv
    return (out_0,) + planes(out_0)

@@ -1,0 +1,189 @@
+from contextlib import ExitStack
+
+import concourse.mybir as mybir
+from concourse.masks import make_identity
+
+F32 = mybir.dt.float32
+BF16 = mybir.dt.bfloat16
+I32 = mybir.dt.int32
+U32 = mybir.dt.uint32
+U16 = mybir.dt.uint16
+U8 = mybir.dt.uint8
+E4M3X4 = mybir.dt.float8_e4m3fn_x4
+E5M2X4 = mybir.dt.float8_e5m2_x4
+ACT = mybir.ActivationFunctionType
+MULT = mybir.AluOpType.mult
+
+P = 128
+LANES = 4
+D = 512
+M = 512
+X = 512
+SLOTS = 1024
+T = 2048
+PER_COL = 16
+CHUNK = 512
+CHUNKS = T // CHUNK
+VECTOR_CHUNKS = 2
+ORDER = (2, 0, 1, 3)
+SLOT_PIECES = ((0, 512), (512, 1024))
+BAG_PIECES = ((0, 384), (384, 768), (768, 1024))
+
+FLOPS = 2 * M * D * X
+
+
+def tile_attend_gfm_mlp_pl_kernel(tc, vT, W, dz, tw, offs, boffs, soffs, out_0, out_1, out_2):
+    nc = tc.nc
+    with ExitStack() as ctx:
+        lists = ctx.enter_context(tc.tile_pool(name="lists", bufs=1))
+        keep = ctx.enter_context(tc.tile_pool(name="keep", bufs=1))
+        work = ctx.enter_context(tc.tile_pool(name="work", bufs=2))
+        psum_dh = ctx.enter_context(tc.psum_pool(name="psum_dh", bufs=1))
+        psum_turn = ctx.enter_context(tc.psum_pool(name="psum_turn", bufs=2))
+
+        vT_planes = vT.rearrange("(p t) c -> t p c", t=LANES)
+        out_planes = out_0.rearrange("(p t) c -> t p c", t=LANES)
+        out_words = out_1.rearrange("a p c l -> p (a c l)").bitcast(I32)
+        out_scales = out_2.rearrange("a f c -> (a f) c").bitcast(I32)
+
+        idx_list = lists.tile([P, SLOTS // PER_COL], U16, name="idx_list")
+        bag_list = lists.tile([P, SLOTS // PER_COL], U16, name="bag_list")
+        slot_list = lists.tile([P, SLOTS // PER_COL], U16, name="slot_list")
+        table = {t: keep.tile([P, T], F32, name=f"table{t}") for t in ORDER}
+        w_raw = keep.tile([P, LANES, D], F32, name="w_raw")
+        dz_raw = keep.tile([P, LANES, X], F32, name="dz_raw")
+        tw_all = keep.tile([P, T], F32, name="tw_all")
+
+        nc.sync.dma_start(idx_list[:], offs)
+        nc.sync.dma_start(table[ORDER[0]][:], vT_planes[ORDER[0]])
+        nc.sync.dma_start(slot_list[:], soffs)
+        nc.sync.dma_start(table[ORDER[1]][:], vT_planes[ORDER[1]])
+        nc.sync.dma_start(w_raw[:], W.rearrange("(p j) d -> p j d", j=LANES))
+        nc.sync.dma_start(dz_raw[:], dz.rearrange("(p j) x -> p j x", j=LANES))
+        nc.sync.dma_start(table[ORDER[2]][:], vT_planes[ORDER[2]])
+        nc.sync.dma_start(table[ORDER[3]][:], vT_planes[ORDER[3]])
+        nc.sync.dma_start(tw_all[:], tw)
+        nc.sync.dma_start(bag_list[:], boffs)
+
+        windows = [keep.tile([P, T], F32, name=f"window{i}") for i in range(2)]
+        for window in windows:
+            nc.vector.memset(window[:], 0.0)
+        identity = keep.tile([P, P], F32, name="identity")
+        make_identity(nc, identity[:])
+
+        w_bf = keep.tile([P, LANES * D], BF16, name="w_bf", align_bytes=64)
+        dz_bf = keep.tile([P, LANES * X], BF16, name="dz_bf", align_bytes=64)
+        w_codes = keep.tile([P, D], U32, name="w_codes", align_bytes=64)
+        w_scales = keep.tile([P, D], U8, name="w_scales", align_bytes=64)
+        dz_codes = keep.tile([P, X], U32, name="dz_codes", align_bytes=64)
+        dz_scales = keep.tile([P, X], U8, name="dz_scales", align_bytes=64)
+        dh = {t: psum_dh.tile([P, X], F32, name=f"dh{t}") for t in ORDER}
+
+        def dense_backward():
+            nc.scalar.copy(
+                w_bf[:].rearrange("p (t q j) -> p t q j", t=LANES, j=LANES),
+                w_raw[:].rearrange("p j (q t) -> p t q j", t=LANES),
+            )
+            nc.scalar.copy(dz_bf[:].rearrange("p (x j) -> p x j", j=LANES), dz_raw[:].rearrange("p j x -> p x j"))
+            nc.vector.quantize_mx(w_codes[:].bitcast(E4M3X4), w_scales[:], w_bf[:])
+            nc.vector.quantize_mx(dz_codes[:].bitcast(E5M2X4), dz_scales[:], dz_bf[:])
+            for t in ORDER:
+                cols = slice(t * P, (t + 1) * P)
+                nc.tensor.matmul_mx(
+                    dh[t][:],
+                    lhsT=w_codes[:, cols].bitcast(E4M3X4),
+                    lhsT_scale=w_scales[:, cols],
+                    rhs=dz_codes[:].bitcast(E5M2X4),
+                    rhs_scale=dz_scales[:],
+                    start=True,
+                    stop=True,
+                )
+
+        listed = {}
+        slope = {}
+        e = {}
+        e_listed = {}
+
+        def gather_table(t):
+            listed[t] = keep.tile([P, SLOTS], F32, name=f"listed{t}")
+            nc.vector.tensor_copy(listed[t][:], table[t][:].indirect(idx_list[:]))
+
+        def pool_bags(t):
+            pairs = work.tile([P, SLOTS], F32, name="pairs")
+            for a, b in SLOT_PIECES:
+                nc.vector.tensor_copy(pairs[:, a:b], listed[t][:].indirect(slot_list[:, a // PER_COL : b // PER_COL]))
+            s_turned = psum_turn.tile([P, X], F32, name="s_turned")
+            for blk in range(X // P):
+                for j in range(2):
+                    nc.tensor.matmul(
+                        s_turned[:, blk * P : (blk + 1) * P],
+                        lhsT=pairs[:, 2 * P * blk + j : 2 * P * (blk + 1) : 2],
+                        rhs=identity[:],
+                        is_transpose=True,
+                        start=(j == 0),
+                        stop=(j == 1),
+                    )
+            h_turned = work.tile([P, X], F32, name="h_turned")
+            nc.scalar.activation(h_turned[:], s_turned[:], ACT.Tanh)
+            h = psum_turn.tile([P, X], F32, name="h")
+            for blk in range(X // P):
+                cols = slice(blk * P, (blk + 1) * P)
+                nc.tensor.transpose(h[:, cols], h_turned[:, cols], identity[:])
+            h_squared = work.tile([P, X], F32, name="h_squared")
+            nc.scalar.activation(h_squared[:], h[:], ACT.Square)
+            slope[t] = keep.tile([P, X], F32, name=f"slope{t}")
+            nc.scalar.activation(slope[t][:], h_squared[:], ACT.Copy, bias=1.0, scale=-1.0)
+
+        def form_e(t):
+            e[t] = keep.tile([P, X], F32, name=f"e{t}")
+            nc.vector.tensor_tensor(e[t][:], dh[t][:], slope[t][:], MULT)
+
+        def gather_e(t):
+            e_listed[t] = work.tile([P, SLOTS], F32, name="e_listed")
+            for a, b in BAG_PIECES:
+                nc.vector.tensor_copy(e_listed[t][:, a:b], e[t][:].indirect(bag_list[:, a // PER_COL : b // PER_COL]))
+
+        rounded = [keep.tile([P, CHUNK, LANES], BF16, name=f"rounded{c}", align_bytes=64) for c in range(CHUNKS)]
+        words = [keep.tile([P, CHUNK], U32, name=f"words{c}", align_bytes=64) for c in range(CHUNKS)]
+        scales = keep.tile([P, T], U8, name="scales", align_bytes=64)
+        tw_listed = keep.tile([P, SLOTS], F32, name="tw_listed")
+
+        def scatter(i):
+            t = ORDER[i]
+            window = windows[i % 2]
+            nc.vector.tensor_tensor(window[:].indirect(idx_list[:]), e_listed[t][:], tw_listed[:], MULT)
+            nc.sync.dma_start(out_planes[t], window[:])
+            last = i == LANES - 1
+            for c in range(CHUNKS):
+                cols = slice(c * CHUNK, (c + 1) * CHUNK)
+                if last and c < VECTOR_CHUNKS:
+                    nc.vector.tensor_copy(rounded[c][:, :, t], window[:, cols])
+                else:
+                    nc.scalar.copy(rounded[c][:, :, t], window[:, cols])
+
+        gather_table(ORDER[0])
+        gather_table(ORDER[1])
+        pool_bags(ORDER[0])
+        dense_backward()
+        gather_table(ORDER[2])
+        pool_bags(ORDER[1])
+        gather_table(ORDER[3])
+        pool_bags(ORDER[2])
+        nc.vector.tensor_copy(tw_listed[:], tw_all[:].indirect(idx_list[:]))
+        pool_bags(ORDER[3])
+        for t in ORDER[:3]:
+            form_e(t)
+        gather_e(ORDER[0])
+        form_e(ORDER[3])
+        for i in range(LANES):
+            if i + 1 < LANES:
+                gather_e(ORDER[i + 1])
+            scatter(i)
+
+        for c in range(CHUNKS):
+            cols = slice(c * CHUNK, (c + 1) * CHUNK)
+            nc.vector.quantize_mx(words[c][:].bitcast(E4M3X4), scales[:, cols], rounded[c][:].rearrange("p c l -> p (c l)"))
+            nc.sync.dma_start(out_words[:, cols], words[c][:].bitcast(I32))
+        for q in range(4):
+            queue = nc.sync if q % 2 == 0 else nc.scalar
+            queue.dma_start(out_scales[4 * q : 4 * q + 4, :], scales[32 * q : 32 * q + 4, :].bitcast(I32))

@@ -22,10 +22,9 @@ X = 512
 SLOTS = 1024
 T = 2048
 PER_COL = 16
-CHUNK = 512
-CHUNKS = T // CHUNK
+CHUNKS = ((0, 512), (512, 1024), (1024, 1536), (1536, 1792), (1792, 2048))
 VECTOR_CHUNKS = 2
-ORDER = (2, 0, 1, 3)
+ORDER = (0, 3, 1, 2)
 SLOT_PIECES = ((0, 512), (512, 1024))
 BAG_PIECES = ((0, 384), (384, 768), (768, 1024))
 
@@ -50,14 +49,14 @@ def tile_attend_gfm_mlp_pl_kernel(tc, vT, W, dz, tw, offs, boffs, soffs, out_0, 
         bag_list = lists.tile([P, SLOTS // PER_COL], U16, name="bag_list")
         slot_list = lists.tile([P, SLOTS // PER_COL], U16, name="slot_list")
         table = {t: keep.tile([P, T], F32, name=f"table{t}") for t in ORDER}
-        w_raw = keep.tile([P, LANES, D], F32, name="w_raw")
-        dz_raw = keep.tile([P, LANES, X], F32, name="dz_raw")
+        w_raw = keep.tile([P, LANES, D], F32, name="w_raw", tag="w_slot")
+        dz_raw = keep.tile([P, LANES, X], F32, name="dz_raw", tag="dz_slot")
         tw_all = keep.tile([P, T], F32, name="tw_all")
 
         nc.sync.dma_start(idx_list[:], offs)
         nc.sync.dma_start(table[ORDER[0]][:], vT_planes[ORDER[0]])
-        nc.sync.dma_start(slot_list[:], soffs)
         nc.sync.dma_start(table[ORDER[1]][:], vT_planes[ORDER[1]])
+        nc.sync.dma_start(slot_list[:], soffs)
         nc.sync.dma_start(w_raw[:], W.rearrange("(p j) d -> p j d", j=LANES))
         nc.sync.dma_start(dz_raw[:], dz.rearrange("(p j) x -> p j x", j=LANES))
         nc.sync.dma_start(table[ORDER[2]][:], vT_planes[ORDER[2]])
@@ -109,7 +108,10 @@ def tile_attend_gfm_mlp_pl_kernel(tc, vT, W, dz, tw, offs, boffs, soffs, out_0, 
             nc.vector.tensor_copy(listed[t][:], table[t][:].indirect(idx_list[:]))
 
         def pool_bags(t):
-            pairs = work.tile([P, SLOTS], F32, name="pairs")
+            if t == ORDER[2]:
+                pairs = keep.tile([P, SLOTS], F32, name="pairs_held", tag="dz_slot")
+            else:
+                pairs = keep.tile([P, SLOTS], F32, name=f"pairs{t}")
             for a, b in SLOT_PIECES:
                 nc.vector.tensor_copy(pairs[:, a:b], listed[t][:].indirect(slot_list[:, a // PER_COL : b // PER_COL]))
             s_turned = psum_turn.tile([P, X], F32, name="s_turned")
@@ -123,7 +125,10 @@ def tile_attend_gfm_mlp_pl_kernel(tc, vT, W, dz, tw, offs, boffs, soffs, out_0, 
                         start=(j == 0),
                         stop=(j == 1),
                     )
-            h_turned = work.tile([P, X], F32, name="h_turned")
+            if t == ORDER[0]:
+                h_turned = keep.tile([P, X], F32, name="h_turned_held", tag="w_slot")
+            else:
+                h_turned = work.tile([P, X], F32, name="h_turned")
             nc.scalar.activation(h_turned[:], s_turned[:], ACT.Tanh)
             h = psum_turn.tile([P, X], F32, name="h")
             for blk in range(X // P):
@@ -143,8 +148,8 @@ def tile_attend_gfm_mlp_pl_kernel(tc, vT, W, dz, tw, offs, boffs, soffs, out_0, 
             for a, b in BAG_PIECES:
                 nc.vector.tensor_copy(e_listed[t][:, a:b], e[t][:].indirect(bag_list[:, a // PER_COL : b // PER_COL]))
 
-        rounded = [keep.tile([P, CHUNK, LANES], BF16, name=f"rounded{c}", align_bytes=64) for c in range(CHUNKS)]
-        words = [keep.tile([P, CHUNK], U32, name=f"words{c}", align_bytes=64) for c in range(CHUNKS)]
+        rounded = [keep.tile([P, b - a, LANES], BF16, name=f"rounded{a}", align_bytes=64) for a, b in CHUNKS]
+        words = [keep.tile([P, b - a], U32, name=f"words{a}", align_bytes=64) for a, b in CHUNKS]
         scales = keep.tile([P, T], U8, name="scales", align_bytes=64)
         tw_listed = keep.tile([P, SLOTS], F32, name="tw_listed")
 
@@ -154,8 +159,8 @@ def tile_attend_gfm_mlp_pl_kernel(tc, vT, W, dz, tw, offs, boffs, soffs, out_0, 
             nc.vector.tensor_tensor(window[:].indirect(idx_list[:]), e_listed[t][:], tw_listed[:], MULT)
             nc.sync.dma_start(out_planes[t], window[:])
             last = i == LANES - 1
-            for c in range(CHUNKS):
-                cols = slice(c * CHUNK, (c + 1) * CHUNK)
+            for c, (a, b) in enumerate(CHUNKS):
+                cols = slice(a, b)
                 if last and c < VECTOR_CHUNKS:
                     nc.vector.tensor_copy(rounded[c][:, :, t], window[:, cols])
                 else:
@@ -163,25 +168,26 @@ def tile_attend_gfm_mlp_pl_kernel(tc, vT, W, dz, tw, offs, boffs, soffs, out_0, 
 
         gather_table(ORDER[0])
         gather_table(ORDER[1])
-        pool_bags(ORDER[0])
         dense_backward()
-        gather_table(ORDER[2])
+        pool_bags(ORDER[0])
         pool_bags(ORDER[1])
+        gather_table(ORDER[2])
         gather_table(ORDER[3])
         pool_bags(ORDER[2])
-        nc.vector.tensor_copy(tw_listed[:], tw_all[:].indirect(idx_list[:]))
         pool_bags(ORDER[3])
-        for t in ORDER[:3]:
-            form_e(t)
+        nc.vector.tensor_copy(tw_listed[:], tw_all[:].indirect(idx_list[:]))
+        form_e(ORDER[0])
+        form_e(ORDER[1])
         gather_e(ORDER[0])
+        form_e(ORDER[2])
         form_e(ORDER[3])
         for i in range(LANES):
             if i + 1 < LANES:
                 gather_e(ORDER[i + 1])
             scatter(i)
 
-        for c in range(CHUNKS):
-            cols = slice(c * CHUNK, (c + 1) * CHUNK)
+        for c, (a, b) in enumerate(CHUNKS):
+            cols = slice(a, b)
             nc.vector.quantize_mx(words[c][:].bitcast(E4M3X4), scales[:, cols], rounded[c][:].rearrange("p c l -> p (c l)"))
             nc.sync.dma_start(out_words[:, cols], words[c][:].bitcast(I32))
         for q in range(4):

@@ -43,7 +43,7 @@ def tile_attend_gfm_mlp_pl_kernel(tc, vT, W, dz, tw, offs, boffs, soffs, out_0, 
         vT_planes = vT.rearrange("(p t) c -> t p c", t=LANES)
         out_planes = out_0.rearrange("(p t) c -> t p c", t=LANES)
         out_words = out_1.rearrange("a p c l -> p (a c l)").bitcast(I32)
-        out_scales = out_2.rearrange("a f c -> (a f) c").bitcast(I32)
+        out_scales = out_2.rearrange("a (q r) (j c) -> (a q) j r c", r=4, j=4).bitcast(I32)
 
         idx_list = lists.tile([P, SLOTS // PER_COL], U16, name="idx_list")
         bag_list = lists.tile([P, SLOTS // PER_COL], U16, name="bag_list")
@@ -65,10 +65,10 @@ def tile_attend_gfm_mlp_pl_kernel(tc, vT, W, dz, tw, offs, boffs, soffs, out_0, 
         nc.sync.dma_start(bag_list[:], boffs)
 
         windows = [keep.tile([P, T], F32, name=f"window{i}") for i in range(2)]
-        for window in windows:
-            nc.vector.memset(window[:], 0.0)
         identity = keep.tile([P, P], F32, name="identity")
         make_identity(nc, identity[:])
+        nc.vector.memset(windows[0][:], 0.0)
+        nc.gpsimd.memset(windows[1][:], 0.0)
 
         w_bf = keep.tile([P, LANES * D], BF16, name="w_bf", align_bytes=64)
         dz_bf = keep.tile([P, LANES * X], BF16, name="dz_bf", align_bytes=64)
@@ -77,6 +77,7 @@ def tile_attend_gfm_mlp_pl_kernel(tc, vT, W, dz, tw, offs, boffs, soffs, out_0, 
         dz_codes = keep.tile([P, X], U32, name="dz_codes", align_bytes=64)
         dz_scales = keep.tile([P, X], U8, name="dz_scales", align_bytes=64)
         dh = {t: psum_dh.tile([P, X], F32, name=f"dh{t}") for t in ORDER}
+        dh_sb = {t: keep.tile([P, X], F32, name=f"dh_sb{t}") for t in ORDER}
 
         def dense_backward():
             nc.scalar.copy(
@@ -97,6 +98,7 @@ def tile_attend_gfm_mlp_pl_kernel(tc, vT, W, dz, tw, offs, boffs, soffs, out_0, 
                     start=True,
                     stop=True,
                 )
+                nc.scalar.copy(dh_sb[t][:], dh[t][:])
 
         listed = {}
         slope = {}
@@ -140,8 +142,8 @@ def tile_attend_gfm_mlp_pl_kernel(tc, vT, W, dz, tw, offs, boffs, soffs, out_0, 
             nc.scalar.activation(slope[t][:], h_squared[:], ACT.Copy, bias=1.0, scale=-1.0)
 
         def form_e(t):
-            e[t] = keep.tile([P, X], F32, name=f"e{t}")
-            nc.vector.tensor_tensor(e[t][:], dh[t][:], slope[t][:], MULT)
+            e[t] = keep.tile([P, X], F32, name=f"e{t}", tag=f"e_slot{min(ORDER.index(t), 4 - ORDER.index(t))}")
+            nc.gpsimd.tensor_tensor(e[t][:], dh_sb[t][:], slope[t][:], MULT)
 
         def gather_e(t):
             e_listed[t] = work.tile([P, SLOTS], F32, name="e_listed")
@@ -150,7 +152,7 @@ def tile_attend_gfm_mlp_pl_kernel(tc, vT, W, dz, tw, offs, boffs, soffs, out_0, 
 
         rounded = [keep.tile([P, b - a, LANES], BF16, name=f"rounded{a}", align_bytes=64) for a, b in CHUNKS]
         words = [keep.tile([P, b - a], U32, name=f"words{a}", align_bytes=64) for a, b in CHUNKS]
-        scales = keep.tile([P, T], U8, name="scales", align_bytes=64)
+        scales = keep.tile([P, T // 4], U8, name="scales", align_bytes=64)
         tw_listed = keep.tile([P, SLOTS], F32, name="tw_listed")
 
         def scatter(i):
@@ -180,16 +182,17 @@ def tile_attend_gfm_mlp_pl_kernel(tc, vT, W, dz, tw, offs, boffs, soffs, out_0, 
         form_e(ORDER[1])
         gather_e(ORDER[0])
         form_e(ORDER[2])
-        form_e(ORDER[3])
         for i in range(LANES):
             if i + 1 < LANES:
                 gather_e(ORDER[i + 1])
+            if i == 0:
+                form_e(ORDER[3])
             scatter(i)
 
         for c, (a, b) in enumerate(CHUNKS):
             cols = slice(a, b)
-            nc.vector.quantize_mx(words[c][:].bitcast(E4M3X4), scales[:, cols], rounded[c][:].rearrange("p c l -> p (c l)"))
+            nc.vector.quantize_mx(words[c][:].bitcast(E4M3X4), scales[4 * (a // 512) : P, a % 512 : a % 512 + b - a], rounded[c][:].rearrange("p c l -> p (c l)"))
             nc.sync.dma_start(out_words[:, cols], words[c][:].bitcast(I32))
         for q in range(4):
             queue = nc.sync if q % 2 == 0 else nc.scalar
-            queue.dma_start(out_scales[4 * q : 4 * q + 4, :], scales[32 * q : 32 * q + 4, :].bitcast(I32))
+            queue.dma_start(out_scales[q], scales[32 * q : 32 * q + 16, :].bitcast(I32))

@@ -25,8 +25,7 @@ PER_COL = 16
 CHUNKS = ((0, 512), (512, 1024), (1024, 1536), (1536, 1792), (1792, 2048))
 VECTOR_CHUNKS = 2
 ORDER = (0, 3, 1, 2)
-SLOT_PIECES = ((0, 512), (512, 1024))
-BAG_PIECES = ((0, 384), (384, 768), (768, 1024))
+WINDOW = 1376
 
 FLOPS = 2 * M * D * X
 
@@ -53,8 +52,8 @@ def tile_attend_gfm_mlp_pl_kernel(tc, vT, W, dz, tw, offs, boffs, soffs, out_0, 
         dz_raw = keep.tile([P, LANES, X], F32, name="dz_raw", tag="dz_slot")
         tw_all = keep.tile([P, T], F32, name="tw_all")
 
-        nc.sync.dma_start(idx_list[:], offs)
         nc.sync.dma_start(table[ORDER[0]][:], vT_planes[ORDER[0]])
+        nc.sync.dma_start(idx_list[:], offs)
         nc.sync.dma_start(table[ORDER[1]][:], vT_planes[ORDER[1]])
         nc.sync.dma_start(slot_list[:], soffs)
         nc.sync.dma_start(w_raw[:], W.rearrange("(p j) d -> p j d", j=LANES))
@@ -68,7 +67,13 @@ def tile_attend_gfm_mlp_pl_kernel(tc, vT, W, dz, tw, offs, boffs, soffs, out_0, 
         identity = keep.tile([P, P], F32, name="identity")
         make_identity(nc, identity[:])
         nc.vector.memset(windows[0][:], 0.0)
+        listed = [keep.tile([P, SLOTS + WINDOW], F32, name=f"listed{i}") for i in range(2)]
+        e = [keep.tile([P, WINDOW], F32, name=f"e{i}") for i in range(2)]
+        for tile in listed:
+            nc.gpsimd.memset(tile[:, 2 * SLOTS :], 0.0)
         nc.gpsimd.memset(windows[1][:], 0.0)
+        for tile in e:
+            nc.gpsimd.memset(tile[:, X:], 0.0)
 
         w_bf = keep.tile([P, LANES * D], BF16, name="w_bf", align_bytes=64)
         dz_bf = keep.tile([P, LANES * X], BF16, name="dz_bf", align_bytes=64)
@@ -100,22 +105,20 @@ def tile_attend_gfm_mlp_pl_kernel(tc, vT, W, dz, tw, offs, boffs, soffs, out_0, 
                 )
                 nc.scalar.copy(dh_sb[t][:], dh[t][:])
 
-        listed = {}
         slope = {}
-        e = {}
         e_listed = {}
 
         def gather_table(t):
-            listed[t] = keep.tile([P, SLOTS], F32, name=f"listed{t}")
-            nc.vector.tensor_copy(listed[t][:], table[t][:].indirect(idx_list[:]))
+            pair, half = ORDER.index(t) // 2, 1 - ORDER.index(t) % 2
+            nc.vector.tensor_copy(listed[pair][:, half * SLOTS : (half + 1) * SLOTS], table[t][:].indirect(idx_list[:]))
 
         def pool_bags(t):
             if t == ORDER[2]:
                 pairs = keep.tile([P, SLOTS], F32, name="pairs_held", tag="dz_slot")
             else:
                 pairs = keep.tile([P, SLOTS], F32, name=f"pairs{t}")
-            for a, b in SLOT_PIECES:
-                nc.vector.tensor_copy(pairs[:, a:b], listed[t][:].indirect(slot_list[:, a // PER_COL : b // PER_COL]))
+            pair, half = ORDER.index(t) // 2, 1 - ORDER.index(t) % 2
+            nc.vector.tensor_copy(pairs[:], listed[pair][:, half * SLOTS : half * SLOTS + WINDOW].indirect(slot_list[:]))
             s_turned = psum_turn.tile([P, X], F32, name="s_turned")
             for blk in range(X // P):
                 for j in range(2):
@@ -142,13 +145,11 @@ def tile_attend_gfm_mlp_pl_kernel(tc, vT, W, dz, tw, offs, boffs, soffs, out_0, 
             nc.scalar.activation(slope[t][:], h_squared[:], ACT.Copy, bias=1.0, scale=-1.0)
 
         def form_e(t):
-            e[t] = keep.tile([P, X], F32, name=f"e{t}", tag=f"e_slot{min(ORDER.index(t), 4 - ORDER.index(t))}")
-            nc.gpsimd.tensor_tensor(e[t][:], dh_sb[t][:], slope[t][:], MULT)
+            nc.gpsimd.tensor_tensor(e[ORDER.index(t) % 2][:, :X], dh_sb[t][:], slope[t][:], MULT)
 
         def gather_e(t):
             e_listed[t] = work.tile([P, SLOTS], F32, name="e_listed")
-            for a, b in BAG_PIECES:
-                nc.vector.tensor_copy(e_listed[t][:, a:b], e[t][:].indirect(bag_list[:, a // PER_COL : b // PER_COL]))
+            nc.vector.tensor_copy(e_listed[t][:], e[ORDER.index(t) % 2][:].indirect(bag_list[:]))
 
         rounded = [keep.tile([P, b - a, LANES], BF16, name=f"rounded{a}", align_bytes=64) for a, b in CHUNKS]
         words = [keep.tile([P, b - a], U32, name=f"words{a}", align_bytes=64) for a, b in CHUNKS]

@@ -26,6 +26,7 @@ CHUNKS = ((0, 512), (512, 1024), (1024, 1536), (1536, 1792), (1792, 2048))
 VECTOR_CHUNKS = 2
 ORDER = (0, 3, 1, 2)
 WINDOW = 1376
+E_TILE = (0, 1, 2, 1)
 
 FLOPS = 2 * M * D * X
 
@@ -68,7 +69,7 @@ def tile_attend_gfm_mlp_pl_kernel(tc, vT, W, dz, tw, offs, boffs, soffs, out_0, 
         make_identity(nc, identity[:])
         nc.vector.memset(windows[0][:], 0.0)
         listed = [keep.tile([P, SLOTS + WINDOW], F32, name=f"listed{i}") for i in range(2)]
-        e = [keep.tile([P, WINDOW], F32, name=f"e{i}") for i in range(2)]
+        e = [keep.tile([P, WINDOW], F32, name=f"e{i}") for i in range(3)]
         for tile in listed:
             nc.gpsimd.memset(tile[:, 2 * SLOTS :], 0.0)
         nc.gpsimd.memset(windows[1][:], 0.0)
@@ -82,12 +83,12 @@ def tile_attend_gfm_mlp_pl_kernel(tc, vT, W, dz, tw, offs, boffs, soffs, out_0, 
         dz_codes = keep.tile([P, X], U32, name="dz_codes", align_bytes=64)
         dz_scales = keep.tile([P, X], U8, name="dz_scales", align_bytes=64)
         dh = {t: psum_dh.tile([P, X], F32, name=f"dh{t}") for t in ORDER}
-        dh_sb = {t: keep.tile([P, X], F32, name=f"dh_sb{t}") for t in ORDER}
+        dh_sb = {t: keep.tile([P, X], F32, name=f"dh_sb{t}") for t in ORDER[:3]}
 
         def dense_backward():
             nc.scalar.copy(
-                w_bf[:].rearrange("p (t q j) -> p t q j", t=LANES, j=LANES),
-                w_raw[:].rearrange("p j (q t) -> p t q j", t=LANES),
+                w_bf[:].rearrange("p (t q j) -> p q t j", t=LANES, j=LANES),
+                w_raw[:].rearrange("p j (q t) -> p q t j", t=LANES),
             )
             nc.scalar.copy(dz_bf[:].rearrange("p (x j) -> p x j", j=LANES), dz_raw[:].rearrange("p j x -> p x j"))
             nc.vector.quantize_mx(w_codes[:].bitcast(E4M3X4), w_scales[:], w_bf[:])
@@ -103,7 +104,8 @@ def tile_attend_gfm_mlp_pl_kernel(tc, vT, W, dz, tw, offs, boffs, soffs, out_0, 
                     start=True,
                     stop=True,
                 )
-                nc.scalar.copy(dh_sb[t][:], dh[t][:])
+                if t != ORDER[3]:
+                    nc.scalar.copy(dh_sb[t][:], dh[t][:])
 
         slope = {}
         e_listed = {}
@@ -145,11 +147,14 @@ def tile_attend_gfm_mlp_pl_kernel(tc, vT, W, dz, tw, offs, boffs, soffs, out_0, 
             nc.scalar.activation(slope[t][:], h_squared[:], ACT.Copy, bias=1.0, scale=-1.0)
 
         def form_e(t):
-            nc.gpsimd.tensor_tensor(e[ORDER.index(t) % 2][:, :X], dh_sb[t][:], slope[t][:], MULT)
+            if t == ORDER[3]:
+                nc.vector.tensor_tensor(e[E_TILE[ORDER.index(t)]][:, :X], dh[t][:], slope[t][:], MULT)
+            else:
+                nc.gpsimd.tensor_tensor(e[E_TILE[ORDER.index(t)]][:, :X], dh_sb[t][:], slope[t][:], MULT)
 
         def gather_e(t):
-            e_listed[t] = work.tile([P, SLOTS], F32, name="e_listed")
-            nc.vector.tensor_copy(e_listed[t][:], e[ORDER.index(t) % 2][:].indirect(bag_list[:]))
+            e_listed[t] = work.tile([P, SLOTS], F32, name="e_listed", bufs=3)
+            nc.vector.tensor_copy(e_listed[t][:], e[E_TILE[ORDER.index(t)]][:].indirect(bag_list[:]))
 
         rounded = [keep.tile([P, b - a, LANES], BF16, name=f"rounded{a}", align_bytes=64) for a, b in CHUNKS]
         words = [keep.tile([P, b - a], U32, name=f"words{a}", align_bytes=64) for a, b in CHUNKS]

@@ -26,7 +26,9 @@ CHUNKS = ((0, 512), (512, 1024), (1024, 1536), (1536, 1792), (1792, 2048))
 VECTOR_CHUNKS = 2
 ORDER = (0, 3, 1, 2)
 WINDOW = 1376
-E_TILE = (0, 1, 2, 1)
+TW_SPLIT = 1792
+LISTED_AT = (3 * SLOTS, 2 * SLOTS, SLOTS, 0)
+E_AT = (2 * X, 3 * X, X, 0)
 
 FLOPS = 2 * M * D * X
 
@@ -43,7 +45,7 @@ def tile_attend_gfm_mlp_pl_kernel(tc, vT, W, dz, tw, offs, boffs, soffs, out_0, 
         vT_planes = vT.rearrange("(p t) c -> t p c", t=LANES)
         out_planes = out_0.rearrange("(p t) c -> t p c", t=LANES)
         out_words = out_1.rearrange("a p c l -> p (a c l)").bitcast(I32)
-        out_scales = out_2.rearrange("a (q r) (j c) -> (a q) j r c", r=4, j=4).bitcast(I32)
+        out_scales = out_2.rearrange("a (q r) (j c) -> (a q) j r c", r=4, j=2).bitcast(I32)
 
         idx_list = lists.tile([P, SLOTS // PER_COL], U16, name="idx_list")
         bag_list = lists.tile([P, SLOTS // PER_COL], U16, name="bag_list")
@@ -60,21 +62,20 @@ def tile_attend_gfm_mlp_pl_kernel(tc, vT, W, dz, tw, offs, boffs, soffs, out_0, 
         nc.sync.dma_start(w_raw[:], W.rearrange("(p j) d -> p j d", j=LANES))
         nc.sync.dma_start(dz_raw[:], dz.rearrange("(p j) x -> p j x", j=LANES))
         nc.sync.dma_start(table[ORDER[2]][:], vT_planes[ORDER[2]])
+        nc.sync.dma_start(tw_all[:, :TW_SPLIT], tw[:, :TW_SPLIT])
         nc.sync.dma_start(table[ORDER[3]][:], vT_planes[ORDER[3]])
-        nc.sync.dma_start(tw_all[:], tw)
+        nc.sync.dma_start(tw_all[:, TW_SPLIT:], tw[:, TW_SPLIT:])
         nc.sync.dma_start(bag_list[:], boffs)
 
         windows = [keep.tile([P, T], F32, name=f"window{i}") for i in range(2)]
         identity = keep.tile([P, P], F32, name="identity")
         make_identity(nc, identity[:])
         nc.vector.memset(windows[0][:], 0.0)
-        listed = [keep.tile([P, SLOTS + WINDOW], F32, name=f"listed{i}") for i in range(2)]
-        e = [keep.tile([P, WINDOW], F32, name=f"e{i}") for i in range(3)]
-        for tile in listed:
-            nc.gpsimd.memset(tile[:, 2 * SLOTS :], 0.0)
+        listed = keep.tile([P, 3 * SLOTS + WINDOW], F32, name="listed")
+        e = keep.tile([P, 3 * X + WINDOW], F32, name="e")
+        nc.gpsimd.memset(listed[:, LANES * SLOTS :], 0.0)
         nc.gpsimd.memset(windows[1][:], 0.0)
-        for tile in e:
-            nc.gpsimd.memset(tile[:, X:], 0.0)
+        nc.gpsimd.memset(e[:, LANES * X :], 0.0)
 
         w_bf = keep.tile([P, LANES * D], BF16, name="w_bf", align_bytes=64)
         dz_bf = keep.tile([P, LANES * X], BF16, name="dz_bf", align_bytes=64)
@@ -83,15 +84,17 @@ def tile_attend_gfm_mlp_pl_kernel(tc, vT, W, dz, tw, offs, boffs, soffs, out_0, 
         dz_codes = keep.tile([P, X], U32, name="dz_codes", align_bytes=64)
         dz_scales = keep.tile([P, X], U8, name="dz_scales", align_bytes=64)
         dh = {t: psum_dh.tile([P, X], F32, name=f"dh{t}") for t in ORDER}
-        dh_sb = {t: keep.tile([P, X], F32, name=f"dh_sb{t}") for t in ORDER[:3]}
+        dh_sb = {t: keep.tile([P, X], F32, name=f"dh_sb{t}") for t in ORDER}
 
-        def dense_backward():
+        def quantise_w():
             nc.scalar.copy(
                 w_bf[:].rearrange("p (t q j) -> p q t j", t=LANES, j=LANES),
                 w_raw[:].rearrange("p j (q t) -> p q t j", t=LANES),
             )
-            nc.scalar.copy(dz_bf[:].rearrange("p (x j) -> p x j", j=LANES), dz_raw[:].rearrange("p j x -> p x j"))
             nc.vector.quantize_mx(w_codes[:].bitcast(E4M3X4), w_scales[:], w_bf[:])
+
+        def dense_backward():
+            nc.scalar.copy(dz_bf[:].rearrange("p (x j) -> p x j", j=LANES), dz_raw[:].rearrange("p j x -> p x j"))
             nc.vector.quantize_mx(dz_codes[:].bitcast(E5M2X4), dz_scales[:], dz_bf[:])
             for t in ORDER:
                 cols = slice(t * P, (t + 1) * P)
@@ -104,23 +107,22 @@ def tile_attend_gfm_mlp_pl_kernel(tc, vT, W, dz, tw, offs, boffs, soffs, out_0, 
                     start=True,
                     stop=True,
                 )
-                if t != ORDER[3]:
-                    nc.scalar.copy(dh_sb[t][:], dh[t][:])
+                nc.scalar.copy(dh_sb[t][:], dh[t][:])
 
         slope = {}
         e_listed = {}
 
         def gather_table(t):
-            pair, half = ORDER.index(t) // 2, 1 - ORDER.index(t) % 2
-            nc.vector.tensor_copy(listed[pair][:, half * SLOTS : (half + 1) * SLOTS], table[t][:].indirect(idx_list[:]))
+            at = LISTED_AT[ORDER.index(t)]
+            nc.vector.tensor_copy(listed[:, at : at + SLOTS], table[t][:].indirect(idx_list[:]))
 
         def pool_bags(t):
             if t == ORDER[2]:
-                pairs = keep.tile([P, SLOTS], F32, name="pairs_held", tag="dz_slot")
+                pairs = keep.tile([P, SLOTS], F32, name="pairs_third", tag="dz_slot")
             else:
                 pairs = keep.tile([P, SLOTS], F32, name=f"pairs{t}")
-            pair, half = ORDER.index(t) // 2, 1 - ORDER.index(t) % 2
-            nc.vector.tensor_copy(pairs[:], listed[pair][:, half * SLOTS : half * SLOTS + WINDOW].indirect(slot_list[:]))
+            at = LISTED_AT[ORDER.index(t)]
+            nc.vector.tensor_copy(pairs[:], listed[:, at : at + WINDOW].indirect(slot_list[:]))
             s_turned = psum_turn.tile([P, X], F32, name="s_turned")
             for blk in range(X // P):
                 for j in range(2):
@@ -141,24 +143,25 @@ def tile_attend_gfm_mlp_pl_kernel(tc, vT, W, dz, tw, offs, boffs, soffs, out_0, 
             for blk in range(X // P):
                 cols = slice(blk * P, (blk + 1) * P)
                 nc.tensor.transpose(h[:, cols], h_turned[:, cols], identity[:])
-            h_squared = work.tile([P, X], F32, name="h_squared")
+            if t == ORDER[3]:
+                h_squared = keep.tile([P, X], F32, name="h_squared_held", tag="rounded_slot", align_bytes=64)
+            else:
+                h_squared = work.tile([P, X], F32, name="h_squared")
             nc.scalar.activation(h_squared[:], h[:], ACT.Square)
             slope[t] = keep.tile([P, X], F32, name=f"slope{t}")
             nc.scalar.activation(slope[t][:], h_squared[:], ACT.Copy, bias=1.0, scale=-1.0)
 
         def form_e(t):
-            if t == ORDER[3]:
-                nc.vector.tensor_tensor(e[E_TILE[ORDER.index(t)]][:, :X], dh[t][:], slope[t][:], MULT)
-            else:
-                nc.gpsimd.tensor_tensor(e[E_TILE[ORDER.index(t)]][:, :X], dh_sb[t][:], slope[t][:], MULT)
+            at = E_AT[ORDER.index(t)]
+            nc.gpsimd.tensor_tensor(e[:, at : at + X], dh_sb[t][:], slope[t][:], MULT)
 
         def gather_e(t):
             e_listed[t] = work.tile([P, SLOTS], F32, name="e_listed", bufs=3)
-            nc.vector.tensor_copy(e_listed[t][:], e[E_TILE[ORDER.index(t)]][:].indirect(bag_list[:]))
+            at = E_AT[ORDER.index(t)]
+            nc.vector.tensor_copy(e_listed[t][:], e[:, at : at + WINDOW].indirect(bag_list[:]))
 
-        rounded = [keep.tile([P, b - a, LANES], BF16, name=f"rounded{a}", align_bytes=64) for a, b in CHUNKS]
         words = [keep.tile([P, b - a], U32, name=f"words{a}", align_bytes=64) for a, b in CHUNKS]
-        scales = keep.tile([P, T // 4], U8, name="scales", align_bytes=64)
+        scales = keep.tile([P, T // 2], U8, name="scales", align_bytes=64)
         tw_listed = keep.tile([P, SLOTS], F32, name="tw_listed")
 
         def scatter(i):
@@ -166,39 +169,40 @@ def tile_attend_gfm_mlp_pl_kernel(tc, vT, W, dz, tw, offs, boffs, soffs, out_0, 
             window = windows[i % 2]
             nc.vector.tensor_tensor(window[:].indirect(idx_list[:]), e_listed[t][:], tw_listed[:], MULT)
             nc.sync.dma_start(out_planes[t], window[:])
-            last = i == LANES - 1
-            for c, (a, b) in enumerate(CHUNKS):
-                cols = slice(a, b)
-                if last and c < VECTOR_CHUNKS:
-                    nc.vector.tensor_copy(rounded[c][:, :, t], window[:, cols])
-                else:
-                    nc.scalar.copy(rounded[c][:, :, t], window[:, cols])
+            if i < LANES - 1:
+                nc.scalar.copy(rounded[:, :, t], window[:])
+            else:
+                for c, (a, b) in enumerate(CHUNKS):
+                    cols = slice(a, b)
+                    if c < VECTOR_CHUNKS:
+                        nc.vector.tensor_copy(rounded[:, cols, t], window[:, cols])
+                    else:
+                        nc.scalar.copy(rounded[:, cols, t], window[:, cols])
 
         gather_table(ORDER[0])
         gather_table(ORDER[1])
+        quantise_w()
         dense_backward()
         pool_bags(ORDER[0])
         pool_bags(ORDER[1])
         gather_table(ORDER[2])
-        gather_table(ORDER[3])
         pool_bags(ORDER[2])
-        pool_bags(ORDER[3])
+        gather_table(ORDER[3])
         nc.vector.tensor_copy(tw_listed[:], tw_all[:].indirect(idx_list[:]))
-        form_e(ORDER[0])
-        form_e(ORDER[1])
+        pool_bags(ORDER[3])
+        for t in ORDER:
+            form_e(t)
+        rounded = keep.tile([P, T, LANES], BF16, name="rounded", tag="rounded_slot", align_bytes=64)
         gather_e(ORDER[0])
-        form_e(ORDER[2])
         for i in range(LANES):
             if i + 1 < LANES:
                 gather_e(ORDER[i + 1])
-            if i == 0:
-                form_e(ORDER[3])
             scatter(i)
 
         for c, (a, b) in enumerate(CHUNKS):
             cols = slice(a, b)
-            nc.vector.quantize_mx(words[c][:].bitcast(E4M3X4), scales[4 * (a // 512) : P, a % 512 : a % 512 + b - a], rounded[c][:].rearrange("p c l -> p (c l)"))
+            nc.vector.quantize_mx(words[c][:].bitcast(E4M3X4), scales[4 * (a // 1024) : P, a % 1024 : a % 1024 + b - a], rounded[:, cols, :].rearrange("p c l -> p (c l)"))
             nc.sync.dma_start(out_words[:, cols], words[c][:].bitcast(I32))
         for q in range(4):
             queue = nc.sync if q % 2 == 0 else nc.scalar
-            queue.dma_start(out_scales[q], scales[32 * q : 32 * q + 16, :].bitcast(I32))
+            queue.dma_start(out_scales[q], scales[32 * q : 32 * q + 8, :].bitcast(I32))

@@ -28,7 +28,7 @@ ORDER = (0, 3, 1, 2)
 WINDOW = 1376
 TW_SPLIT = 1792
 LISTED_AT = (3 * SLOTS, 2 * SLOTS, SLOTS, 0)
-E_AT = (2 * X, 3 * X, X, 0)
+E_AT = (X, 2 * X, 0)
 
 FLOPS = 2 * M * D * X
 
@@ -72,10 +72,10 @@ def tile_attend_gfm_mlp_pl_kernel(tc, vT, W, dz, tw, offs, boffs, soffs, out_0, 
         make_identity(nc, identity[:])
         nc.vector.memset(windows[0][:], 0.0)
         listed = keep.tile([P, 3 * SLOTS + WINDOW], F32, name="listed")
-        e = keep.tile([P, 3 * X + WINDOW], F32, name="e")
+        e = keep.tile([P, 2 * X + WINDOW], F32, name="e")
         nc.gpsimd.memset(listed[:, LANES * SLOTS :], 0.0)
         nc.gpsimd.memset(windows[1][:], 0.0)
-        nc.gpsimd.memset(e[:, LANES * X :], 0.0)
+        nc.gpsimd.memset(e[:, 3 * X :], 0.0)
 
         w_bf = keep.tile([P, LANES * D], BF16, name="w_bf", align_bytes=64)
         dz_bf = keep.tile([P, LANES * X], BF16, name="dz_bf", align_bytes=64)
@@ -123,7 +123,7 @@ def tile_attend_gfm_mlp_pl_kernel(tc, vT, W, dz, tw, offs, boffs, soffs, out_0, 
                 pairs = keep.tile([P, SLOTS], F32, name=f"pairs{t}")
             at = LISTED_AT[ORDER.index(t)]
             nc.vector.tensor_copy(pairs[:], listed[:, at : at + WINDOW].indirect(slot_list[:]))
-            s_turned = psum_turn.tile([P, X], F32, name="s_turned")
+            s_turned = psum_turn.tile([P, X], F32, name="s_turned", bufs=1)
             for blk in range(X // P):
                 for j in range(2):
                     nc.tensor.matmul(
@@ -151,14 +151,25 @@ def tile_attend_gfm_mlp_pl_kernel(tc, vT, W, dz, tw, offs, boffs, soffs, out_0, 
             slope[t] = keep.tile([P, X], F32, name=f"slope{t}")
             nc.scalar.activation(slope[t][:], h_squared[:], ACT.Copy, bias=1.0, scale=-1.0)
 
+        e_window = {}
+
         def form_e(t):
-            at = E_AT[ORDER.index(t)]
-            nc.gpsimd.tensor_tensor(e[:, at : at + X], dh_sb[t][:], slope[t][:], MULT)
+            if t == ORDER[3]:
+                e_last = keep.tile([P, WINDOW], F32, name="e_last", tag="first_listed_slot")
+                e_window[t] = e_last[:]
+            else:
+                at = E_AT[ORDER.index(t)]
+                e_window[t] = e[:, at : at + WINDOW]
+            nc.gpsimd.tensor_tensor(e_window[t][:, :X], dh_sb[t][:], slope[t][:], MULT)
+            if t == ORDER[3]:
+                nc.gpsimd.memset(e_window[t][:, X:], 0.0)
 
         def gather_e(t):
-            e_listed[t] = work.tile([P, SLOTS], F32, name="e_listed", bufs=3)
-            at = E_AT[ORDER.index(t)]
-            nc.vector.tensor_copy(e_listed[t][:], e[:, at : at + WINDOW].indirect(bag_list[:]))
+            if t == ORDER[0]:
+                e_listed[t] = keep.tile([P, SLOTS], F32, name="e_listed_first", tag="first_listed_slot")
+            else:
+                e_listed[t] = work.tile([P, SLOTS], F32, name="e_listed", bufs=3)
+            nc.vector.tensor_copy(e_listed[t][:], e_window[t].indirect(bag_list[:]))
 
         words = [keep.tile([P, b - a], U32, name=f"words{a}", align_bytes=64) for a, b in CHUNKS]
         scales = keep.tile([P, T // 2], U8, name="scales", align_bytes=64)
@@ -190,7 +201,7 @@ def tile_attend_gfm_mlp_pl_kernel(tc, vT, W, dz, tw, offs, boffs, soffs, out_0, 
         gather_table(ORDER[3])
         nc.vector.tensor_copy(tw_listed[:], tw_all[:].indirect(idx_list[:]))
         pool_bags(ORDER[3])
-        for t in ORDER:
+        for t in ORDER[:3]:
             form_e(t)
         rounded = keep.tile([P, T, LANES], BF16, name="rounded", tag="rounded_slot", align_bytes=64)
         gather_e(ORDER[0])
@@ -198,6 +209,8 @@ def tile_attend_gfm_mlp_pl_kernel(tc, vT, W, dz, tw, offs, boffs, soffs, out_0, 
             if i + 1 < LANES:
                 gather_e(ORDER[i + 1])
             scatter(i)
+            if i == 0:
+                form_e(ORDER[3])
 
         for c, (a, b) in enumerate(CHUNKS):
             cols = slice(a, b)

@@ -39,13 +39,12 @@ def tile_attend_gfm_mlp_pl_kernel(tc, vT, W, dz, tw, offs, boffs, soffs, out_0, 
         lists = ctx.enter_context(tc.tile_pool(name="lists", bufs=1))
         keep = ctx.enter_context(tc.tile_pool(name="keep", bufs=1))
         work = ctx.enter_context(tc.tile_pool(name="work", bufs=2))
-        psum_dh = ctx.enter_context(tc.psum_pool(name="psum_dh", bufs=1))
-        psum_turn = ctx.enter_context(tc.psum_pool(name="psum_turn", bufs=2))
+        psum = ctx.enter_context(tc.psum_pool(name="psum", bufs=1))
 
         vT_planes = vT.rearrange("(p t) c -> t p c", t=LANES)
         out_planes = out_0.rearrange("(p t) c -> t p c", t=LANES)
         out_words = out_1.rearrange("a p c l -> p (a c l)").bitcast(I32)
-        out_scales = out_2.rearrange("a (q r) (j c) -> (a q) j r c", r=4, j=2).bitcast(I32)
+        out_scales = out_2.rearrange("a (q r) (j c) -> (a q) j r c", r=4, j=4).bitcast(I32)
 
         idx_list = lists.tile([P, SLOTS // PER_COL], U16, name="idx_list")
         bag_list = lists.tile([P, SLOTS // PER_COL], U16, name="bag_list")
@@ -83,7 +82,6 @@ def tile_attend_gfm_mlp_pl_kernel(tc, vT, W, dz, tw, offs, boffs, soffs, out_0, 
         w_scales = keep.tile([P, D], U8, name="w_scales", align_bytes=64)
         dz_codes = keep.tile([P, X], U32, name="dz_codes", align_bytes=64)
         dz_scales = keep.tile([P, X], U8, name="dz_scales", align_bytes=64)
-        dh = {t: psum_dh.tile([P, X], F32, name=f"dh{t}") for t in ORDER}
         dh_sb = {t: keep.tile([P, X], F32, name=f"dh_sb{t}") for t in ORDER}
 
         def quantise_w():
@@ -93,13 +91,16 @@ def tile_attend_gfm_mlp_pl_kernel(tc, vT, W, dz, tw, offs, boffs, soffs, out_0, 
             )
             nc.vector.quantize_mx(w_codes[:].bitcast(E4M3X4), w_scales[:], w_bf[:])
 
-        def dense_backward():
+        def quantise_dz():
             nc.scalar.copy(dz_bf[:].rearrange("p (x j) -> p x j", j=LANES), dz_raw[:].rearrange("p j x -> p x j"))
             nc.vector.quantize_mx(dz_codes[:].bitcast(E5M2X4), dz_scales[:], dz_bf[:])
-            for t in ORDER:
+
+        def dense_backward():
+            for i, t in enumerate(ORDER):
                 cols = slice(t * P, (t + 1) * P)
+                dh = psum.tile([P, X], F32, name=f"dh{t}", tag=("second_sum", "second_h")[i % 2])
                 nc.tensor.matmul_mx(
-                    dh[t][:],
+                    dh[:],
                     lhsT=w_codes[:, cols].bitcast(E4M3X4),
                     lhsT_scale=w_scales[:, cols],
                     rhs=dz_codes[:].bitcast(E5M2X4),
@@ -107,7 +108,7 @@ def tile_attend_gfm_mlp_pl_kernel(tc, vT, W, dz, tw, offs, boffs, soffs, out_0, 
                     start=True,
                     stop=True,
                 )
-                nc.scalar.copy(dh_sb[t][:], dh[t][:])
+                nc.scalar.copy(dh_sb[t][:], dh[:])
 
         slope = {}
         e_listed = {}
@@ -123,7 +124,7 @@ def tile_attend_gfm_mlp_pl_kernel(tc, vT, W, dz, tw, offs, boffs, soffs, out_0, 
                 pairs = keep.tile([P, SLOTS], F32, name=f"pairs{t}")
             at = LISTED_AT[ORDER.index(t)]
             nc.vector.tensor_copy(pairs[:], listed[:, at : at + WINDOW].indirect(slot_list[:]))
-            s_turned = psum_turn.tile([P, X], F32, name="s_turned", bufs=1)
+            s_turned = psum.tile([P, X], F32, name=f"s_turned{t}", tag="second_sum" if t == ORDER[1] else "sum")
             for blk in range(X // P):
                 for j in range(2):
                     nc.tensor.matmul(
@@ -139,7 +140,7 @@ def tile_attend_gfm_mlp_pl_kernel(tc, vT, W, dz, tw, offs, boffs, soffs, out_0, 
             else:
                 h_turned = work.tile([P, X], F32, name="h_turned")
             nc.scalar.activation(h_turned[:], s_turned[:], ACT.Tanh)
-            h = psum_turn.tile([P, X], F32, name="h")
+            h = psum.tile([P, X], F32, name=f"h{t}", tag="second_h" if t == ORDER[1] else "h")
             for blk in range(X // P):
                 cols = slice(blk * P, (blk + 1) * P)
                 nc.tensor.transpose(h[:, cols], h_turned[:, cols], identity[:])
@@ -172,7 +173,7 @@ def tile_attend_gfm_mlp_pl_kernel(tc, vT, W, dz, tw, offs, boffs, soffs, out_0, 
             nc.vector.tensor_copy(e_listed[t][:], e_window[t].indirect(bag_list[:]))
 
         words = [keep.tile([P, b - a], U32, name=f"words{a}", align_bytes=64) for a, b in CHUNKS]
-        scales = keep.tile([P, T // 2], U8, name="scales", align_bytes=64)
+        scales = keep.tile([P, T // 4], U8, name="scales", align_bytes=64)
         tw_listed = keep.tile([P, SLOTS], F32, name="tw_listed")
 
         def scatter(i):
@@ -180,8 +181,11 @@ def tile_attend_gfm_mlp_pl_kernel(tc, vT, W, dz, tw, offs, boffs, soffs, out_0, 
             window = windows[i % 2]
             nc.vector.tensor_tensor(window[:].indirect(idx_list[:]), e_listed[t][:], tw_listed[:], MULT)
             nc.sync.dma_start(out_planes[t], window[:])
-            if i < LANES - 1:
+            if i < LANES - 2:
                 nc.scalar.copy(rounded[:, :, t], window[:])
+            elif i == LANES - 2:
+                for cols in (slice(0, T // 2), slice(T // 2, T)):
+                    nc.scalar.copy(rounded[:, cols, t], window[:, cols])
             else:
                 for c, (a, b) in enumerate(CHUNKS):
                     cols = slice(a, b)
@@ -193,9 +197,10 @@ def tile_attend_gfm_mlp_pl_kernel(tc, vT, W, dz, tw, offs, boffs, soffs, out_0, 
         gather_table(ORDER[0])
         gather_table(ORDER[1])
         quantise_w()
-        dense_backward()
+        quantise_dz()
         pool_bags(ORDER[0])
         pool_bags(ORDER[1])
+        dense_backward()
         gather_table(ORDER[2])
         pool_bags(ORDER[2])
         gather_table(ORDER[3])
@@ -214,8 +219,13 @@ def tile_attend_gfm_mlp_pl_kernel(tc, vT, W, dz, tw, offs, boffs, soffs, out_0, 
 
         for c, (a, b) in enumerate(CHUNKS):
             cols = slice(a, b)
-            nc.vector.quantize_mx(words[c][:].bitcast(E4M3X4), scales[4 * (a // 1024) : P, a % 1024 : a % 1024 + b - a], rounded[:, cols, :].rearrange("p c l -> p (c l)"))
+            for first in range(a, b, 256):
+                nc.vector.quantize_mx(
+                    words[c][:, first - a : first - a + 256].bitcast(E4M3X4),
+                    scales[4 * (first // 512) : P, first % 512 : first % 512 + 256],
+                    rounded[:, first : first + 256, :].rearrange("p c l -> p (c l)"),
+                )
             nc.sync.dma_start(out_words[:, cols], words[c][:].bitcast(I32))
         for q in range(4):
             queue = nc.sync if q % 2 == 0 else nc.scalar
-            queue.dma_start(out_scales[q], scales[32 * q : 32 * q + 8, :].bitcast(I32))
+            queue.dma_start(out_scales[q], scales[32 * q : 32 * q + 16, :].bitcast(I32))

@@ -28,7 +28,7 @@ ORDER = (0, 3, 1, 2)
 WINDOW = 1376
 TW_SPLIT = 1792
 LISTED_AT = (3 * SLOTS, 2 * SLOTS, SLOTS, 0)
-E_AT = (X, 2 * X, 0)
+E_AT = (3 * X, 4 * X, 2 * X, X)
 
 FLOPS = 2 * M * D * X
 
@@ -71,10 +71,10 @@ def tile_attend_gfm_mlp_pl_kernel(tc, vT, W, dz, tw, offs, boffs, soffs, out_0, 
         make_identity(nc, identity[:])
         nc.vector.memset(windows[0][:], 0.0)
         listed = keep.tile([P, 3 * SLOTS + WINDOW], F32, name="listed")
-        e = keep.tile([P, 2 * X + WINDOW], F32, name="e")
+        e = keep.tile([P, 4 * X + WINDOW], F32, name="e")
         nc.gpsimd.memset(listed[:, LANES * SLOTS :], 0.0)
+        nc.gpsimd.memset(e[:, 5 * X :], 0.0)
         nc.gpsimd.memset(windows[1][:], 0.0)
-        nc.gpsimd.memset(e[:, 3 * X :], 0.0)
 
         w_bf = keep.tile([P, LANES * D], BF16, name="w_bf", align_bytes=64)
         dz_bf = keep.tile([P, LANES * X], BF16, name="dz_bf", align_bytes=64)
@@ -152,25 +152,17 @@ def tile_attend_gfm_mlp_pl_kernel(tc, vT, W, dz, tw, offs, boffs, soffs, out_0, 
             slope[t] = keep.tile([P, X], F32, name=f"slope{t}")
             nc.scalar.activation(slope[t][:], h_squared[:], ACT.Copy, bias=1.0, scale=-1.0)
 
-        e_window = {}
-
         def form_e(t):
-            if t == ORDER[3]:
-                e_last = keep.tile([P, WINDOW], F32, name="e_last", tag="first_listed_slot")
-                e_window[t] = e_last[:]
-            else:
-                at = E_AT[ORDER.index(t)]
-                e_window[t] = e[:, at : at + WINDOW]
-            nc.gpsimd.tensor_tensor(e_window[t][:, :X], dh_sb[t][:], slope[t][:], MULT)
-            if t == ORDER[3]:
-                nc.gpsimd.memset(e_window[t][:, X:], 0.0)
+            at = E_AT[ORDER.index(t)]
+            nc.gpsimd.tensor_tensor(e[:, at : at + X], dh_sb[t][:], slope[t][:], MULT)
 
         def gather_e(t):
             if t == ORDER[0]:
-                e_listed[t] = keep.tile([P, SLOTS], F32, name="e_listed_first", tag="first_listed_slot")
+                e_listed[t] = e[:, :SLOTS]
             else:
-                e_listed[t] = work.tile([P, SLOTS], F32, name="e_listed", bufs=3)
-            nc.vector.tensor_copy(e_listed[t][:], e_window[t].indirect(bag_list[:]))
+                e_listed[t] = work.tile([P, SLOTS], F32, name="e_listed", bufs=3)[:]
+            at = E_AT[ORDER.index(t)]
+            nc.vector.tensor_copy(e_listed[t], e[:, at : at + WINDOW].indirect(bag_list[:]))
 
         words = [keep.tile([P, b - a], U32, name=f"words{a}", align_bytes=64) for a, b in CHUNKS]
         scales = keep.tile([P, T // 4], U8, name="scales", align_bytes=64)
@@ -179,7 +171,7 @@ def tile_attend_gfm_mlp_pl_kernel(tc, vT, W, dz, tw, offs, boffs, soffs, out_0, 
         def scatter(i):
             t = ORDER[i]
             window = windows[i % 2]
-            nc.vector.tensor_tensor(window[:].indirect(idx_list[:]), e_listed[t][:], tw_listed[:], MULT)
+            nc.vector.tensor_tensor(window[:].indirect(idx_list[:]), e_listed[t], tw_listed[:], MULT)
             nc.sync.dma_start(out_planes[t], window[:])
             if i < LANES - 2:
                 nc.scalar.copy(rounded[:, :, t], window[:])

@@ -22,15 +22,21 @@ X = 512
 SLOTS = 1024
 T = 2048
 PER_COL = 16
-CHUNKS = ((0, 512), (512, 1024), (1024, 1536), (1536, 1792), (1792, 2048))
-VECTOR_CHUNKS = 2
 ORDER = (0, 3, 1, 2)
 WINDOW = 1376
 TW_SPLIT = 1792
-LISTED_AT = (3 * SLOTS, 2 * SLOTS, SLOTS, 0)
+CALL = 256
+STORES = (0, 512, 1024, 1536, 1792, 2048)
+VECTOR_PIECES = (0, 512, 1024)
+SCALAR_PIECES = (1024, 1536, 1792, 2048)
+GPSIMD_SHARE = 256
 E_AT = (3 * X, 4 * X, 2 * X, X)
 
 FLOPS = 2 * M * D * X
+
+
+def pieces(edges):
+    return [slice(a, b) for a, b in zip(edges, edges[1:])]
 
 
 def tile_attend_gfm_mlp_pl_kernel(tc, vT, W, dz, tw, offs, boffs, soffs, out_0, out_1, out_2):
@@ -41,37 +47,37 @@ def tile_attend_gfm_mlp_pl_kernel(tc, vT, W, dz, tw, offs, boffs, soffs, out_0, 
         work = ctx.enter_context(tc.tile_pool(name="work", bufs=2))
         psum = ctx.enter_context(tc.psum_pool(name="psum", bufs=1))
 
-        vT_planes = vT.rearrange("(p t) c -> t p c", t=LANES)
-        out_planes = out_0.rearrange("(p t) c -> t p c", t=LANES)
+        vT_lanes = vT.rearrange("(p t) c -> t p c", t=LANES)
+        out_lanes = out_0.rearrange("(p t) c -> t p c", t=LANES)
         out_words = out_1.rearrange("a p c l -> p (a c l)").bitcast(I32)
         out_scales = out_2.rearrange("a (q r) (j c) -> (a q) j r c", r=4, j=4).bitcast(I32)
 
         idx_list = lists.tile([P, SLOTS // PER_COL], U16, name="idx_list")
         bag_list = lists.tile([P, SLOTS // PER_COL], U16, name="bag_list")
         slot_list = lists.tile([P, SLOTS // PER_COL], U16, name="slot_list")
-        table = {t: keep.tile([P, T], F32, name=f"table{t}") for t in ORDER}
+        table = [keep.tile([P, T], F32, name=f"table{i}") for i in range(LANES)]
         w_raw = keep.tile([P, LANES, D], F32, name="w_raw", tag="w_slot")
         dz_raw = keep.tile([P, LANES, X], F32, name="dz_raw", tag="dz_slot")
         tw_all = keep.tile([P, T], F32, name="tw_all")
 
-        nc.sync.dma_start(table[ORDER[0]][:], vT_planes[ORDER[0]])
+        nc.sync.dma_start(table[0][:], vT_lanes[ORDER[0]])
         nc.sync.dma_start(idx_list[:], offs)
-        nc.sync.dma_start(table[ORDER[1]][:], vT_planes[ORDER[1]])
+        nc.sync.dma_start(table[1][:], vT_lanes[ORDER[1]])
         nc.sync.dma_start(slot_list[:], soffs)
         nc.sync.dma_start(w_raw[:], W.rearrange("(p j) d -> p j d", j=LANES))
         nc.sync.dma_start(dz_raw[:], dz.rearrange("(p j) x -> p j x", j=LANES))
-        nc.sync.dma_start(table[ORDER[2]][:], vT_planes[ORDER[2]])
+        nc.sync.dma_start(table[2][:], vT_lanes[ORDER[2]])
         nc.sync.dma_start(tw_all[:, :TW_SPLIT], tw[:, :TW_SPLIT])
-        nc.sync.dma_start(table[ORDER[3]][:], vT_planes[ORDER[3]])
+        nc.sync.dma_start(table[3][:], vT_lanes[ORDER[3]])
         nc.sync.dma_start(tw_all[:, TW_SPLIT:], tw[:, TW_SPLIT:])
         nc.sync.dma_start(bag_list[:], boffs)
 
         windows = [keep.tile([P, T], F32, name=f"window{i}") for i in range(2)]
         identity = keep.tile([P, P], F32, name="identity")
-        make_identity(nc, identity[:])
-        nc.vector.memset(windows[0][:], 0.0)
         listed = keep.tile([P, 3 * SLOTS + WINDOW], F32, name="listed")
         e = keep.tile([P, 4 * X + WINDOW], F32, name="e")
+        make_identity(nc, identity[:])
+        nc.vector.memset(windows[0][:], 0.0)
         nc.gpsimd.memset(listed[:, LANES * SLOTS :], 0.0)
         nc.gpsimd.memset(e[:, 5 * X :], 0.0)
         nc.gpsimd.memset(windows[1][:], 0.0)
@@ -82,23 +88,29 @@ def tile_attend_gfm_mlp_pl_kernel(tc, vT, W, dz, tw, offs, boffs, soffs, out_0, 
         w_scales = keep.tile([P, D], U8, name="w_scales", align_bytes=64)
         dz_codes = keep.tile([P, X], U32, name="dz_codes", align_bytes=64)
         dz_scales = keep.tile([P, X], U8, name="dz_scales", align_bytes=64)
-        dh_sb = {t: keep.tile([P, X], F32, name=f"dh_sb{t}") for t in ORDER}
+        dh_sb = [keep.tile([P, X], F32, name=f"dh_sb{i}", tag=f"dh_slot{i}") for i in range(LANES)]
+        slope = [keep.tile([P, X], F32, name=f"slope{i}", tag=f"slope_slot{i}") for i in range(LANES)]
+        dv = {}
+        e_listed = [e[:, :SLOTS]] + [keep.tile([P, SLOTS], F32, name=f"e_listed{i}")[:] for i in range(1, LANES)]
+        tw_listed = keep.tile([P, SLOTS], F32, name="tw_listed")
 
-        def quantise_w():
+        def gather_table(i):
+            at = (LANES - 1 - i) * SLOTS
+            nc.vector.tensor_copy(listed[:, at : at + SLOTS], table[i][:].indirect(idx_list[:]))
+
+        def quantise_operands():
             nc.scalar.copy(
                 w_bf[:].rearrange("p (t q j) -> p q t j", t=LANES, j=LANES),
                 w_raw[:].rearrange("p j (q t) -> p q t j", t=LANES),
             )
             nc.vector.quantize_mx(w_codes[:].bitcast(E4M3X4), w_scales[:], w_bf[:])
-
-        def quantise_dz():
             nc.scalar.copy(dz_bf[:].rearrange("p (x j) -> p x j", j=LANES), dz_raw[:].rearrange("p j x -> p x j"))
             nc.vector.quantize_mx(dz_codes[:].bitcast(E5M2X4), dz_scales[:], dz_bf[:])
 
         def dense_backward():
             for i, t in enumerate(ORDER):
                 cols = slice(t * P, (t + 1) * P)
-                dh = psum.tile([P, X], F32, name=f"dh{t}", tag=("second_sum", "second_h")[i % 2])
+                dh = psum.tile([P, X], F32, name=f"dh{i}", tag=("second_sum", "second_h")[i % 2])
                 nc.tensor.matmul_mx(
                     dh[:],
                     lhsT=w_codes[:, cols].bitcast(E4M3X4),
@@ -108,23 +120,16 @@ def tile_attend_gfm_mlp_pl_kernel(tc, vT, W, dz, tw, offs, boffs, soffs, out_0, 
                     start=True,
                     stop=True,
                 )
-                nc.scalar.copy(dh_sb[t][:], dh[:])
+                nc.scalar.copy(dh_sb[i][:], dh[:])
 
-        slope = {}
-        e_listed = {}
-
-        def gather_table(t):
-            at = LISTED_AT[ORDER.index(t)]
-            nc.vector.tensor_copy(listed[:, at : at + SLOTS], table[t][:].indirect(idx_list[:]))
-
-        def pool_bags(t):
-            if t == ORDER[2]:
+        def pool_bags(i):
+            if i == 2:
                 pairs = keep.tile([P, SLOTS], F32, name="pairs_third", tag="dz_slot")
             else:
-                pairs = keep.tile([P, SLOTS], F32, name=f"pairs{t}")
-            at = LISTED_AT[ORDER.index(t)]
+                pairs = keep.tile([P, SLOTS], F32, name=f"pairs{i}")
+            at = (LANES - 1 - i) * SLOTS
             nc.vector.tensor_copy(pairs[:], listed[:, at : at + WINDOW].indirect(slot_list[:]))
-            s_turned = psum.tile([P, X], F32, name=f"s_turned{t}", tag="second_sum" if t == ORDER[1] else "sum")
+            s_turned = psum.tile([P, X], F32, name=f"s_turned{i}", tag="second_sum" if i == 1 else "sum")
             for blk in range(X // P):
                 for j in range(2):
                     nc.tensor.matmul(
@@ -135,89 +140,86 @@ def tile_attend_gfm_mlp_pl_kernel(tc, vT, W, dz, tw, offs, boffs, soffs, out_0, 
                         start=(j == 0),
                         stop=(j == 1),
                     )
-            if t == ORDER[0]:
+            if i == 0:
                 h_turned = keep.tile([P, X], F32, name="h_turned_held", tag="w_slot")
             else:
                 h_turned = work.tile([P, X], F32, name="h_turned")
             nc.scalar.activation(h_turned[:], s_turned[:], ACT.Tanh)
-            h = psum.tile([P, X], F32, name=f"h{t}", tag="second_h" if t == ORDER[1] else "h")
+            h = psum.tile([P, X], F32, name=f"h{i}", tag="second_h" if i == 1 else "h")
             for blk in range(X // P):
                 cols = slice(blk * P, (blk + 1) * P)
                 nc.tensor.transpose(h[:, cols], h_turned[:, cols], identity[:])
-            if t == ORDER[3]:
+            if i == LANES - 1:
                 h_squared = keep.tile([P, X], F32, name="h_squared_held", tag="rounded_slot", align_bytes=64)
             else:
                 h_squared = work.tile([P, X], F32, name="h_squared")
             nc.scalar.activation(h_squared[:], h[:], ACT.Square)
-            slope[t] = keep.tile([P, X], F32, name=f"slope{t}")
-            nc.scalar.activation(slope[t][:], h_squared[:], ACT.Copy, bias=1.0, scale=-1.0)
+            nc.scalar.activation(slope[i][:], h_squared[:], ACT.Copy, bias=1.0, scale=-1.0)
 
-        def form_e(t):
-            at = E_AT[ORDER.index(t)]
-            nc.gpsimd.tensor_tensor(e[:, at : at + X], dh_sb[t][:], slope[t][:], MULT)
+        def form_e(i):
+            at = E_AT[i]
+            nc.gpsimd.tensor_tensor(e[:, at : at + X], dh_sb[i][:], slope[i][:], MULT)
 
-        def gather_e(t):
-            if t == ORDER[0]:
-                e_listed[t] = e[:, :SLOTS]
-            else:
-                e_listed[t] = work.tile([P, SLOTS], F32, name="e_listed", bufs=3)[:]
-            at = E_AT[ORDER.index(t)]
-            nc.vector.tensor_copy(e_listed[t], e[:, at : at + WINDOW].indirect(bag_list[:]))
+        def gather_e(i):
+            at = E_AT[i]
+            nc.vector.tensor_copy(e_listed[i], e[:, at : at + WINDOW].indirect(bag_list[:]))
 
-        words = [keep.tile([P, b - a], U32, name=f"words{a}", align_bytes=64) for a, b in CHUNKS]
-        scales = keep.tile([P, T // 4], U8, name="scales", align_bytes=64)
-        tw_listed = keep.tile([P, SLOTS], F32, name="tw_listed")
+        def weigh(i):
+            dv[i] = keep.tile([P, SLOTS], F32, name=f"dv{i}", tag=("slope_slot2", "dh_slot2", "slope_slot3", "dh_slot3")[i])
+            nc.gpsimd.tensor_tensor(dv[i][:], e_listed[i], tw_listed[:], MULT)
 
         def scatter(i):
-            t = ORDER[i]
-            window = windows[i % 2]
-            nc.vector.tensor_tensor(window[:].indirect(idx_list[:]), e_listed[t], tw_listed[:], MULT)
-            nc.sync.dma_start(out_planes[t], window[:])
-            if i < LANES - 2:
-                nc.scalar.copy(rounded[:, :, t], window[:])
-            elif i == LANES - 2:
-                for cols in (slice(0, T // 2), slice(T // 2, T)):
-                    nc.scalar.copy(rounded[:, cols, t], window[:, cols])
-            else:
-                for c, (a, b) in enumerate(CHUNKS):
-                    cols = slice(a, b)
-                    if c < VECTOR_CHUNKS:
-                        nc.vector.tensor_copy(rounded[:, cols, t], window[:, cols])
-                    else:
-                        nc.scalar.copy(rounded[:, cols, t], window[:, cols])
+            nc.vector.tensor_copy(windows[i % 2][:].indirect(idx_list[:]), dv[i][:])
+            nc.sync.dma_start(out_lanes[ORDER[i]], windows[i % 2][:])
 
-        gather_table(ORDER[0])
-        gather_table(ORDER[1])
-        quantise_w()
-        quantise_dz()
-        pool_bags(ORDER[0])
-        pool_bags(ORDER[1])
+        gather_table(0)
+        gather_table(1)
+        quantise_operands()
+        pool_bags(0)
+        pool_bags(1)
         dense_backward()
-        gather_table(ORDER[2])
-        pool_bags(ORDER[2])
-        gather_table(ORDER[3])
+        gather_table(2)
+        pool_bags(2)
+        gather_table(3)
         nc.vector.tensor_copy(tw_listed[:], tw_all[:].indirect(idx_list[:]))
-        pool_bags(ORDER[3])
-        for t in ORDER[:3]:
-            form_e(t)
+        pool_bags(3)
+        for i in range(3):
+            form_e(i)
+        for i in range(3):
+            gather_e(i)
         rounded = keep.tile([P, T, LANES], BF16, name="rounded", tag="rounded_slot", align_bytes=64)
-        gather_e(ORDER[0])
-        for i in range(LANES):
-            if i + 1 < LANES:
-                gather_e(ORDER[i + 1])
-            scatter(i)
-            if i == 0:
-                form_e(ORDER[3])
 
-        for c, (a, b) in enumerate(CHUNKS):
-            cols = slice(a, b)
-            for first in range(a, b, 256):
+        def round_lane(copy, i, cols):
+            copy(rounded[:, cols, ORDER[i]], windows[i % 2][:, cols])
+
+        weigh(0)
+        weigh(1)
+        form_e(3)
+        weigh(2)
+        scatter(0)
+        round_lane(nc.scalar.copy, 0, slice(0, T))
+        gather_e(3)
+        weigh(3)
+        for i in (1, 2):
+            scatter(i)
+            round_lane(nc.scalar.copy, i, slice(0, T - GPSIMD_SHARE))
+            round_lane(nc.gpsimd.tensor_copy, i, slice(T - GPSIMD_SHARE, T))
+        scatter(3)
+        for cols in pieces(VECTOR_PIECES):
+            round_lane(nc.vector.tensor_copy, 3, cols)
+        for cols in pieces(SCALAR_PIECES):
+            round_lane(nc.scalar.copy, 3, cols)
+
+        scales = keep.tile([P, T // 4], U8, name="scales", align_bytes=64)
+        for cols in pieces(STORES):
+            words = keep.tile([P, cols.stop - cols.start], U32, name=f"words{cols.start}", align_bytes=64)
+            for first in range(cols.start, cols.stop, CALL):
                 nc.vector.quantize_mx(
-                    words[c][:, first - a : first - a + 256].bitcast(E4M3X4),
-                    scales[4 * (first // 512) : P, first % 512 : first % 512 + 256],
-                    rounded[:, first : first + 256, :].rearrange("p c l -> p (c l)"),
+                    words[:, first - cols.start : first - cols.start + CALL].bitcast(E4M3X4),
+                    scales[4 * (first // 512) : P, first % 512 : first % 512 + CALL],
+                    rounded[:, first : first + CALL, :].rearrange("p c l -> p (c l)"),
                 )
-            nc.sync.dma_start(out_words[:, cols], words[c][:].bitcast(I32))
+            nc.sync.dma_start(out_words[:, cols], words[:].bitcast(I32))
         for q in range(4):
             queue = nc.sync if q % 2 == 0 else nc.scalar
             queue.dma_start(out_scales[q], scales[32 * q : 32 * q + 16, :].bitcast(I32))

@@ -30,7 +30,7 @@ STORES = (0, 512, 1024, 1536, 1792, 2048)
 VECTOR_PIECES = (0, 512, 1024)
 SCALAR_PIECES = (1024, 1536, 1792, 2048)
 GPSIMD_SHARE = 256
-E_AT = (3 * X, 4 * X, 2 * X, X)
+E_AT = (4 * X, 3 * X, 2 * X, X)
 
 FLOPS = 2 * M * D * X
 

@@ -13,6 +13,7 @@ E4M3X4 = mybir.dt.float8_e4m3fn_x4
 E5M2X4 = mybir.dt.float8_e5m2_x4
 ACT = mybir.ActivationFunctionType
 MULT = mybir.AluOpType.mult
+ADD = mybir.AluOpType.add
 
 P = 128
 LANES = 4
@@ -22,15 +23,15 @@ X = 512
 SLOTS = 1024
 T = 2048
 PER_COL = 16
-ORDER = (0, 3, 1, 2)
-WINDOW = 1376
-TW_SPLIT = 1792
-CALL = 256
+MARGIN = 16
+HALVES = (0, 512, 1024)
+QUARTERS = (0, 256, 512, 768, 1024)
+SHARE = 640
+PIECE = 256
+PAIR = 512
+VECTOR_WEAVES = 2
 STORES = (0, 512, 1024, 1536, 1792, 2048)
-VECTOR_PIECES = (0, 512, 1024)
-SCALAR_PIECES = (1024, 1536, 1792, 2048)
-GPSIMD_SHARE = 256
-E_AT = (4 * X, 3 * X, 2 * X, X)
+KIB = 1024
 
 FLOPS = 2 * M * D * X
 
@@ -44,7 +45,8 @@ def tile_attend_gfm_mlp_pl_kernel(tc, vT, W, dz, tw, offs, boffs, soffs, out_0, 
     with ExitStack() as ctx:
         lists = ctx.enter_context(tc.tile_pool(name="lists", bufs=1))
         keep = ctx.enter_context(tc.tile_pool(name="keep", bufs=1))
-        work = ctx.enter_context(tc.tile_pool(name="work", bufs=2))
+        reused = ctx.enter_context(tc.tile_pool(name="reused", bufs=1))
+        late = ctx.enter_context(tc.tile_pool(name="late", bufs=1))
         psum = ctx.enter_context(tc.psum_pool(name="psum", bufs=1))
 
         vT_lanes = vT.rearrange("(p t) c -> t p c", t=LANES)
@@ -55,81 +57,62 @@ def tile_attend_gfm_mlp_pl_kernel(tc, vT, W, dz, tw, offs, boffs, soffs, out_0, 
         idx_list = lists.tile([P, SLOTS // PER_COL], U16, name="idx_list")
         bag_list = lists.tile([P, SLOTS // PER_COL], U16, name="bag_list")
         slot_list = lists.tile([P, SLOTS // PER_COL], U16, name="slot_list")
-        table = [keep.tile([P, T], F32, name=f"table{i}") for i in range(LANES)]
         w_raw = keep.tile([P, LANES, D], F32, name="w_raw", tag="w_slot")
-        dz_raw = keep.tile([P, LANES, X], F32, name="dz_raw", tag="dz_slot")
-        tw_all = keep.tile([P, T], F32, name="tw_all")
+        dz_raw = keep.tile([P, LANES, X], F32, name="dz_raw", tag="dz_slot", align_bytes=64)
+        identity = keep.tile([P, P], F32, name="identity")
+        table = {
+            0: reused.tile([P, T], F32, name="table0", offset=0),
+            1: reused.tile([P, T], F32, name="table1", offset=8 * KIB),
+            2: keep.tile([P, T], F32, name="table2", tag="third_table", align_bytes=64),
+        }
 
-        nc.sync.dma_start(table[0][:], vT_lanes[ORDER[0]])
+        def entries(a_list, part):
+            return a_list[:, part.start // PER_COL : part.stop // PER_COL]
+
+        def on_vector(out, in_):
+            nc.vector.tensor_copy(out, in_)
+
+        def on_scalar(out, in_):
+            nc.scalar.activation(out, in_, ACT.Copy)
+
+        shared = ((on_vector, slice(0, SHARE)), (on_scalar, slice(SHARE, SLOTS)))
+
+        def gather(out, window, a_list, shares):
+            for move, part in shares:
+                move(out[:, part], window[:].indirect(entries(a_list, part)))
+
+        nc.sync.dma_start(table[0][:], vT_lanes[0])
         nc.sync.dma_start(idx_list[:], offs)
-        nc.sync.dma_start(table[1][:], vT_lanes[ORDER[1]])
         nc.sync.dma_start(slot_list[:], soffs)
+        nc.sync.dma_start(table[1][:], vT_lanes[1])
+        nc.sync.dma_start(table[2][:], vT_lanes[2])
         nc.sync.dma_start(w_raw[:], W.rearrange("(p j) d -> p j d", j=LANES))
         nc.sync.dma_start(dz_raw[:], dz.rearrange("(p j) x -> p j x", j=LANES))
-        nc.sync.dma_start(table[2][:], vT_lanes[ORDER[2]])
-        nc.sync.dma_start(tw_all[:, :TW_SPLIT], tw[:, :TW_SPLIT])
-        nc.sync.dma_start(table[3][:], vT_lanes[ORDER[3]])
-        nc.sync.dma_start(tw_all[:, TW_SPLIT:], tw[:, TW_SPLIT:])
         nc.sync.dma_start(bag_list[:], boffs)
 
-        windows = [keep.tile([P, T], F32, name=f"window{i}") for i in range(2)]
-        identity = keep.tile([P, P], F32, name="identity")
-        listed = keep.tile([P, 3 * SLOTS + WINDOW], F32, name="listed")
-        e = keep.tile([P, 4 * X + WINDOW], F32, name="e")
         make_identity(nc, identity[:])
+        windows = {t: keep.tile([P, T], F32, name=f"window{t}") for t in range(LANES)}
+        e = [keep.tile([P, X + MARGIN], F32, name=f"e{t}") for t in range(LANES)]
         nc.vector.memset(windows[0][:], 0.0)
-        nc.gpsimd.memset(listed[:, LANES * SLOTS :], 0.0)
-        nc.gpsimd.memset(e[:, 5 * X :], 0.0)
-        nc.gpsimd.memset(windows[1][:], 0.0)
+        for t in range(LANES):
+            nc.gpsimd.memset(e[t][:, X:], 0.0)
+        for t in range(1, LANES):
+            nc.gpsimd.memset(windows[t][:], 0.0)
 
         w_bf = keep.tile([P, LANES * D], BF16, name="w_bf", align_bytes=64)
-        dz_bf = keep.tile([P, LANES * X], BF16, name="dz_bf", align_bytes=64)
-        w_codes = keep.tile([P, D], U32, name="w_codes", align_bytes=64)
         w_scales = keep.tile([P, D], U8, name="w_scales", align_bytes=64)
         dz_codes = keep.tile([P, X], U32, name="dz_codes", align_bytes=64)
         dz_scales = keep.tile([P, X], U8, name="dz_scales", align_bytes=64)
-        dh_sb = [keep.tile([P, X], F32, name=f"dh_sb{i}", tag=f"dh_slot{i}") for i in range(LANES)]
-        slope = [keep.tile([P, X], F32, name=f"slope{i}", tag=f"slope_slot{i}") for i in range(LANES)]
-        dv = {}
-        e_listed = [e[:, :SLOTS]] + [keep.tile([P, SLOTS], F32, name=f"e_listed{i}")[:] for i in range(1, LANES)]
-        tw_listed = keep.tile([P, SLOTS], F32, name="tw_listed")
+        listed, h_squared, slope, dh, dv = {}, {}, {}, {}, {}
 
-        def gather_table(i):
-            at = (LANES - 1 - i) * SLOTS
-            nc.vector.tensor_copy(listed[:, at : at + SLOTS], table[i][:].indirect(idx_list[:]))
+        def gather_table(t, shares):
+            listed[t] = keep.tile([P, SLOTS], F32, name=f"listed{t}", tag="pairs2" if t == 3 else f"listed{t}", align_bytes=64)
+            gather(listed[t], table[t], idx_list, shares)
 
-        def quantise_operands():
-            nc.scalar.copy(
-                w_bf[:].rearrange("p (t q j) -> p q t j", t=LANES, j=LANES),
-                w_raw[:].rearrange("p j (q t) -> p q t j", t=LANES),
-            )
-            nc.vector.quantize_mx(w_codes[:].bitcast(E4M3X4), w_scales[:], w_bf[:])
-            nc.scalar.copy(dz_bf[:].rearrange("p (x j) -> p x j", j=LANES), dz_raw[:].rearrange("p j x -> p x j"))
-            nc.vector.quantize_mx(dz_codes[:].bitcast(E5M2X4), dz_scales[:], dz_bf[:])
-
-        def dense_backward():
-            for i, t in enumerate(ORDER):
-                cols = slice(t * P, (t + 1) * P)
-                dh = psum.tile([P, X], F32, name=f"dh{i}", tag=("second_sum", "second_h")[i % 2])
-                nc.tensor.matmul_mx(
-                    dh[:],
-                    lhsT=w_codes[:, cols].bitcast(E4M3X4),
-                    lhsT_scale=w_scales[:, cols],
-                    rhs=dz_codes[:].bitcast(E5M2X4),
-                    rhs_scale=dz_scales[:],
-                    start=True,
-                    stop=True,
-                )
-                nc.scalar.copy(dh_sb[i][:], dh[:])
-
-        def pool_bags(i):
-            if i == 2:
-                pairs = keep.tile([P, SLOTS], F32, name="pairs_third", tag="dz_slot")
-            else:
-                pairs = keep.tile([P, SLOTS], F32, name=f"pairs{i}")
-            at = (LANES - 1 - i) * SLOTS
-            nc.vector.tensor_copy(pairs[:], listed[:, at : at + WINDOW].indirect(slot_list[:]))
-            s_turned = psum.tile([P, X], F32, name=f"s_turned{i}", tag="second_sum" if i == 1 else "sum")
+        def pool_bags(t, shares):
+            pairs = keep.tile([P, SLOTS], F32, name=f"pairs{t}", tag="third_table" if t == 1 else f"pairs{t}", align_bytes=64)
+            gather(pairs, listed[t], slot_list, shares)
+            s_turned = psum.tile([P, X], F32, name=f"s_turned{t}", tag=f"sum{t % 2}")
             for blk in range(X // P):
                 for j in range(2):
                     nc.tensor.matmul(
@@ -140,84 +123,146 @@ def tile_attend_gfm_mlp_pl_kernel(tc, vT, W, dz, tw, offs, boffs, soffs, out_0, 
                         start=(j == 0),
                         stop=(j == 1),
                     )
-            if i == 0:
-                h_turned = keep.tile([P, X], F32, name="h_turned_held", tag="w_slot")
-            else:
-                h_turned = work.tile([P, X], F32, name="h_turned")
+            h_turned = keep.tile([P, X], F32, name=f"h_turned{t}", tag=f"h_turned{t}")
             nc.scalar.activation(h_turned[:], s_turned[:], ACT.Tanh)
-            h = psum.tile([P, X], F32, name=f"h{i}", tag="second_h" if i == 1 else "h")
+            h = psum.tile([P, X], F32, name=f"h{t}", tag=f"h{t % 2}")
             for blk in range(X // P):
                 cols = slice(blk * P, (blk + 1) * P)
                 nc.tensor.transpose(h[:, cols], h_turned[:, cols], identity[:])
-            if i == LANES - 1:
-                h_squared = keep.tile([P, X], F32, name="h_squared_held", tag="rounded_slot", align_bytes=64)
+            if t == 2:
+                h_squared[t] = reused.tile([P, X], F32, name="h_squared2", offset=0)
+            elif t == 3:
+                h_squared[t] = late.tile([P, X], F32, name="h_squared3", offset=KIB)
             else:
-                h_squared = work.tile([P, X], F32, name="h_squared")
-            nc.scalar.activation(h_squared[:], h[:], ACT.Square)
-            nc.scalar.activation(slope[i][:], h_squared[:], ACT.Copy, bias=1.0, scale=-1.0)
+                h_squared[t] = keep.tile([P, X], F32, name=f"h_squared{t}", tag=f"h_squared{t}")
+            nc.scalar.activation(h_squared[t][:], h[:], ACT.Square)
 
-        def form_e(i):
-            at = E_AT[i]
-            nc.gpsimd.tensor_tensor(e[:, at : at + X], dh_sb[i][:], slope[i][:], MULT)
+        def form_slope(t):
+            slope[t] = keep.tile([P, X], F32, name=f"slope{t}", tag=("w_slot", "h_squared0", "slope2", "slope3")[t])
+            nc.gpsimd.tensor_scalar(slope[t][:], h_squared[t][:], -1.0, 1.0, MULT, ADD)
 
-        def gather_e(i):
-            at = E_AT[i]
-            nc.vector.tensor_copy(e_listed[i], e[:, at : at + WINDOW].indirect(bag_list[:]))
+        def dense_backward():
+            nc.gpsimd.tensor_scalar(
+                w_bf[:].rearrange("p (t q j) -> p q t j", t=LANES, j=LANES),
+                w_raw[:].rearrange("p j (q t) -> p q t j", t=LANES),
+                1.0,
+                -0.0,
+                MULT,
+                ADD,
+            )
+            dz_bf = keep.tile([P, LANES * X], BF16, name="dz_bf", tag="listed2", align_bytes=64)
+            nc.vector.tensor_copy(dz_bf[:].rearrange("p (x j) -> p x j", j=LANES), dz_raw[:].rearrange("p j x -> p x j"))
+            w_codes = keep.tile([P, D], U32, name="w_codes", tag="dz_slot", align_bytes=64)
+            nc.vector.quantize_mx(w_codes[:].bitcast(E4M3X4), w_scales[:], w_bf[:])
+            nc.vector.quantize_mx(dz_codes[:].bitcast(E5M2X4), dz_scales[:], dz_bf[:])
+            for t in range(LANES):
+                cols = slice(t * P, (t + 1) * P)
+                dh[t] = psum.tile([P, X], F32, name=f"dh{t}", tag=f"dh{t}")
+                nc.tensor.matmul_mx(
+                    dh[t][:],
+                    lhsT=w_codes[:, cols].bitcast(E4M3X4),
+                    lhsT_scale=w_scales[:, cols],
+                    rhs=dz_codes[:].bitcast(E5M2X4),
+                    rhs_scale=dz_scales[:],
+                    start=True,
+                    stop=True,
+                )
 
-        def weigh(i):
-            dv[i] = keep.tile([P, SLOTS], F32, name=f"dv{i}", tag=("slope_slot2", "dh_slot2", "slope_slot3", "dh_slot3")[i])
-            nc.gpsimd.tensor_tensor(dv[i][:], e_listed[i], tw_listed[:], MULT)
+        def form_e(t):
+            nc.vector.tensor_tensor(e[t][:, :X], dh[t][:], slope[t][:], MULT)
 
-        def scatter(i):
-            nc.vector.tensor_copy(windows[i % 2][:].indirect(idx_list[:]), dv[i][:])
-            nc.sync.dma_start(out_lanes[ORDER[i]], windows[i % 2][:])
+        def weigh(t, half):
+            part = pieces(HALVES)[half]
+            if (t, half) == (0, 1):
+                dv[t, half] = late.tile([P, X], F32, name="dv01", offset=0)
+            else:
+                dv[t, half] = keep.tile([P, X], F32, name=f"dv{t}{half}", tag="slope3" if (t, half) == (2, 0) else f"dv{t}{half}")
+            nc.gpsimd.tensor_tensor(dv[t, half][:], e_listed[t, half], tw_listed[:, part], MULT)
 
-        gather_table(0)
-        gather_table(1)
-        quantise_operands()
-        pool_bags(0)
-        pool_bags(1)
+        def scatter(t):
+            move, edges = (on_vector, HALVES) if t % 2 == 0 else (on_scalar, QUARTERS)
+            for part in pieces(edges):
+                half, at = divmod(part.start, X)
+                move(windows[t][:].indirect(entries(idx_list, part)), dv[t, half][:, at : at + part.stop - part.start])
+            nc.sync.dma_start(out_lanes[t], windows[t][:])
+
+        evenly = list(zip((on_vector, on_scalar), pieces(HALVES)))
+        scalar_whole = [(on_scalar, slice(0, SLOTS))]
+
+        gather_table(0, shared)
+        table[3] = reused.tile([P, T], F32, name="table3", offset=0)
+        nc.sync.dma_start(table[3][:], vT_lanes[3])
+        pool_bags(0, shared)
+        gather_table(1, shared)
+        tw_all = reused.tile([P, T], F32, name="tw_all", offset=8 * KIB)
+        nc.sync.dma_start(tw_all[:], tw)
+        gather_table(2, shared)
+        pool_bags(1, shared)
+        pool_bags(2, shared)
         dense_backward()
-        gather_table(2)
-        pool_bags(2)
-        gather_table(3)
-        nc.vector.tensor_copy(tw_listed[:], tw_all[:].indirect(idx_list[:]))
-        pool_bags(3)
-        for i in range(3):
-            form_e(i)
-        for i in range(3):
-            gather_e(i)
-        rounded = keep.tile([P, T, LANES], BF16, name="rounded", tag="rounded_slot", align_bytes=64)
+        for t in range(3):
+            form_slope(t)
+        gather_table(3, evenly)
+        form_e(0)
+        pool_bags(3, evenly)
+        form_slope(3)
+        form_e(1)
+        form_e(2)
+        tw_listed = reused.tile([P, SLOTS], F32, name="tw_listed", offset=4 * KIB)
+        gather(tw_listed, tw_all, idx_list, scalar_whole)
+        first_listed = reused.tile([P, SLOTS], F32, name="e_listed0", offset=0)
+        e_listed = {
+            (0, 0): first_listed[:, :X],
+            (0, 1): first_listed[:, X:],
+            (1, 0): keep.tile([P, X], F32, name="e_listed10", tag="pairs3", align_bytes=64)[:],
+            (1, 1): keep.tile([P, X], F32, name="e_listed11", tag="h_turned3")[:],
+            (2, 0): keep.tile([P, X], F32, name="e_listed20")[:],
+            (2, 1): late.tile([P, X], F32, name="e_listed21", offset=2 * KIB)[:],
+            (3, 0): keep.tile([P, X], F32, name="e_listed30")[:],
+            (3, 1): keep.tile([P, X], F32, name="e_listed31")[:],
+        }
 
-        def round_lane(copy, i, cols):
-            copy(rounded[:, cols, ORDER[i]], windows[i % 2][:, cols])
+        def gather_e(t):
+            move = on_vector if t % 2 == 0 else on_scalar
+            for half, part in enumerate(pieces(HALVES)):
+                move(e_listed[t, half], e[t][:].indirect(entries(bag_list, part)))
 
-        weigh(0)
-        weigh(1)
+        gather_e(0)
+        gather_e(1)
         form_e(3)
-        weigh(2)
-        scatter(0)
-        round_lane(nc.scalar.copy, 0, slice(0, T))
+        gather_e(2)
         gather_e(3)
-        weigh(3)
-        for i in (1, 2):
-            scatter(i)
-            round_lane(nc.scalar.copy, i, slice(0, T - GPSIMD_SHARE))
-            round_lane(nc.gpsimd.tensor_copy, i, slice(T - GPSIMD_SHARE, T))
-        scatter(3)
-        for cols in pieces(VECTOR_PIECES):
-            round_lane(nc.vector.tensor_copy, 3, cols)
-        for cols in pieces(SCALAR_PIECES):
-            round_lane(nc.scalar.copy, 3, cols)
+        for t, half in ((0, 0), (1, 0), (0, 1), (1, 1), (2, 0), (2, 1), (3, 0), (3, 1)):
+            weigh(t, half)
+        for t in range(LANES):
+            scatter(t)
 
+        pair_words = reused.tile([P, T * LANES], BF16, name="pair_words", offset=0)
+        by_piece = pair_words[:].rearrange("p (k u c l) -> p k u c l", u=2, c=PAIR, l=2)
+        for t in range(2):
+            nc.gpsimd.tensor_scalar(by_piece[:, :, 0, :, t], windows[t][:].rearrange("p (k c) -> p k c", c=PAIR), 1.0, -0.0, MULT, ADD)
+        nc.vector.tensor_copy(by_piece[:, :, 1, :, 0], windows[2][:].rearrange("p (k c) -> p k c", c=PAIR))
+        for k in range(T // PAIR):
+            nc.vector.tensor_copy(by_piece[:, k, 1, :, 1], windows[3][:, k * PAIR : (k + 1) * PAIR])
+        as_words = pair_words[:].bitcast(U32).rearrange("p (k u c) -> p k c u", u=2, c=PAIR)
+
+        signed_words = pair_words[:].bitcast(I32).rearrange("p (k u c) -> p k c u", u=2, c=PAIR)
+        rounded = keep.tile([P, T, 2], U32, name="rounded", align_bytes=64)
         scales = keep.tile([P, T // 4], U8, name="scales", align_bytes=64)
+        for first in range(0, T, PIECE):
+            k, at = divmod(first, PAIR)
+            source = as_words[:, k, at : at + PIECE, :]
+            if first < T - VECTOR_WEAVES * PIECE:
+                nc.scalar.copy(rounded[:, first : first + PIECE, :], source)
+            else:
+                nc.vector.tensor_copy(rounded[:, first : first + PIECE, :].bitcast(I32), signed_words[:, k, at : at + PIECE, :])
         for cols in pieces(STORES):
             words = keep.tile([P, cols.stop - cols.start], U32, name=f"words{cols.start}", align_bytes=64)
-            for first in range(cols.start, cols.stop, CALL):
+            for first in range(cols.start, cols.stop, PIECE):
                 nc.vector.quantize_mx(
-                    words[:, first - cols.start : first - cols.start + CALL].bitcast(E4M3X4),
-                    scales[4 * (first // 512) : P, first % 512 : first % 512 + CALL],
-                    rounded[:, first : first + CALL, :].rearrange("p c l -> p (c l)"),
+                    words[:, first - cols.start : first - cols.start + PIECE].bitcast(E4M3X4),
+                    scales[4 * (first // 512) : P, first % 512 : first % 512 + PIECE],
+                    rounded[:, first : first + PIECE, :].rearrange("p c u -> p (c u)").bitcast(BF16),
                 )
             nc.sync.dma_start(out_words[:, cols], words[:].bitcast(I32))
         for q in range(4):

@@ -1,7 +1,6 @@
 from contextlib import ExitStack
 
 import concourse.mybir as mybir
-from concourse.masks import make_identity
 
 F32 = mybir.dt.float32
 BF16 = mybir.dt.bfloat16
@@ -24,12 +23,15 @@ SLOTS = 1024
 T = 2048
 PER_COL = 16
 MARGIN = 16
+BLOCK = 32
 HALVES = (0, 512, 1024)
-QUARTERS = (0, 256, 512, 768, 1024)
-SHARE = 640
+PRODUCTS = ((0, SLOTS), (0, 384, SLOTS), (0, SLOTS), (0, SLOTS))
+SCATTERS = ((0, SLOTS), (0, 384, 768, SLOTS), (0, SLOTS), (0, 384, 768, SLOTS))
+SHARE = 576
+LAST_SHARE = 384
 PIECE = 256
 PAIR = 512
-VECTOR_WEAVES = 2
+VECTOR_WEAVES = 4
 STORES = (0, 512, 1024, 1536, 1792, 2048)
 KIB = 1024
 
@@ -46,7 +48,6 @@ def tile_attend_gfm_mlp_pl_kernel(tc, vT, W, dz, tw, offs, boffs, soffs, out_0, 
         lists = ctx.enter_context(tc.tile_pool(name="lists", bufs=1))
         keep = ctx.enter_context(tc.tile_pool(name="keep", bufs=1))
         reused = ctx.enter_context(tc.tile_pool(name="reused", bufs=1))
-        late = ctx.enter_context(tc.tile_pool(name="late", bufs=1))
         psum = ctx.enter_context(tc.psum_pool(name="psum", bufs=1))
 
         vT_lanes = vT.rearrange("(p t) c -> t p c", t=LANES)
@@ -54,17 +55,52 @@ def tile_attend_gfm_mlp_pl_kernel(tc, vT, W, dz, tw, offs, boffs, soffs, out_0, 
         out_words = out_1.rearrange("a p c l -> p (a c l)").bitcast(I32)
         out_scales = out_2.rearrange("a (q r) (j c) -> (a q) j r c", r=4, j=4).bitcast(I32)
 
+        places = {
+            "table3": 0,
+            "h_turned2": 0,
+            "h_squared1": 2,
+            "planes": 0,
+            "tw_listed": 8,
+            "table1": 16,
+            "tw_all": 16,
+            "table2": 24,
+            "pairs1": 24,
+            "h_turned0": 28,
+            "dv00": 30,
+            "h_squared3": 33,
+            "dv10": 34,
+            "dv11": 37,
+            "slope3": 37,
+            "w_raw1": 40,
+            "slope0": 40,
+            "pairs3": 48,
+            "e_listed1": 48,
+            "e3": 52,
+            "dv20": 52,
+            "ones": 56,
+            "window1": 56,
+            "column": 64,
+            "window2": 64,
+            "dz_bf": 72,
+            "window3": 72,
+        }
+
+        def tile(name, shape, dtype=F32):
+            if name in places:
+                return reused.tile(shape, dtype, name=name, offset=places[name] * KIB, align_bytes=64)
+            return keep.tile(shape, dtype, name=name, align_bytes=64)
+
         idx_list = lists.tile([P, SLOTS // PER_COL], U16, name="idx_list")
         bag_list = lists.tile([P, SLOTS // PER_COL], U16, name="bag_list")
         slot_list = lists.tile([P, SLOTS // PER_COL], U16, name="slot_list")
-        w_raw = keep.tile([P, LANES, D], F32, name="w_raw", tag="w_slot")
-        dz_raw = keep.tile([P, LANES, X], F32, name="dz_raw", tag="dz_slot", align_bytes=64)
-        identity = keep.tile([P, P], F32, name="identity")
-        table = {
-            0: reused.tile([P, T], F32, name="table0", offset=0),
-            1: reused.tile([P, T], F32, name="table1", offset=8 * KIB),
-            2: keep.tile([P, T], F32, name="table2", tag="third_table", align_bytes=64),
-        }
+        w_raw = [tile(f"w_raw{half}", [P, LANES, D // 2]) for half in range(2)]
+        dz_raw = tile("dz_raw", [P, LANES, X])
+        identity = tile("identity", [P, P])
+        table, listed, pairs, h_turned, h_squared, slope, dh, e_listed, dv = {}, {}, {}, {}, {}, {}, {}, {}, {}
+
+        def load_table(t):
+            table[t] = tile(f"table{t}", [P, T])
+            nc.sync.dma_start(table[t][:], vT_lanes[t])
 
         def entries(a_list, part):
             return a_list[:, part.start // PER_COL : part.stop // PER_COL]
@@ -75,84 +111,106 @@ def tile_attend_gfm_mlp_pl_kernel(tc, vT, W, dz, tw, offs, boffs, soffs, out_0, 
         def on_scalar(out, in_):
             nc.scalar.activation(out, in_, ACT.Copy)
 
-        shared = ((on_vector, slice(0, SHARE)), (on_scalar, slice(SHARE, SLOTS)))
+        def shared(vector_share):
+            return ((on_vector, slice(0, vector_share)), (on_scalar, slice(vector_share, SLOTS)))
 
         def gather(out, window, a_list, shares):
             for move, part in shares:
                 move(out[:, part], window[:].indirect(entries(a_list, part)))
 
-        nc.sync.dma_start(table[0][:], vT_lanes[0])
+        load_table(0)
         nc.sync.dma_start(idx_list[:], offs)
         nc.sync.dma_start(slot_list[:], soffs)
-        nc.sync.dma_start(table[1][:], vT_lanes[1])
-        nc.sync.dma_start(table[2][:], vT_lanes[2])
-        nc.sync.dma_start(w_raw[:], W.rearrange("(p j) d -> p j d", j=LANES))
+        load_table(1)
+        load_table(2)
+        for half in range(2):
+            nc.sync.dma_start(w_raw[half][:], W.rearrange("(p j) (h d) -> h p j d", j=LANES, h=2)[half])
         nc.sync.dma_start(dz_raw[:], dz.rearrange("(p j) x -> p j x", j=LANES))
+        load_table(3)
         nc.sync.dma_start(bag_list[:], boffs)
 
-        make_identity(nc, identity[:])
-        windows = {t: keep.tile([P, T], F32, name=f"window{t}") for t in range(LANES)}
-        e = [keep.tile([P, X + MARGIN], F32, name=f"e{t}") for t in range(LANES)]
+        warm = tile("warm", [P, 2])
+        nc.vector.memset(warm[:, 0:1], 0.0)
+        nc.scalar.activation(warm[:, 1:2], warm[:, 0:1], ACT.Tanh)
+        windows = {0: tile("window0", [P, T])}
         nc.vector.memset(windows[0][:], 0.0)
+        ones = tile("ones", [P, BLOCK])
+        column = tile("column", [P, BLOCK])
+        row = tile("row", [P, BLOCK])
+        nc.vector.memset(ones[:], 1.0)
+        nc.vector.memset(identity[:], 0.0)
+        nc.vector.tensor_tensor_scan(column[:], ones[:], ones[:], 0.0, MULT, ADD)
+        nc.vector.transpose(row[:], column[:])
+        for first in range(0, P, BLOCK):
+            block = slice(first, first + BLOCK)
+            nc.vector.tensor_tensor(identity[block, block], row[block, :], column[block, :], mybir.AluOpType.is_equal)
+        e = [tile(f"e{t}", [P, X + MARGIN]) for t in range(LANES)]
         for t in range(LANES):
             nc.gpsimd.memset(e[t][:, X:], 0.0)
-        for t in range(1, LANES):
+        for t in (1, 2):
+            windows[t] = tile(f"window{t}", [P, T])
             nc.gpsimd.memset(windows[t][:], 0.0)
 
-        w_bf = keep.tile([P, LANES * D], BF16, name="w_bf", align_bytes=64)
-        w_scales = keep.tile([P, D], U8, name="w_scales", align_bytes=64)
-        dz_codes = keep.tile([P, X], U32, name="dz_codes", align_bytes=64)
-        dz_scales = keep.tile([P, X], U8, name="dz_scales", align_bytes=64)
-        listed, h_squared, slope, dh, dv = {}, {}, {}, {}, {}
-
         def gather_table(t, shares):
-            listed[t] = keep.tile([P, SLOTS], F32, name=f"listed{t}", tag="pairs2" if t == 3 else f"listed{t}", align_bytes=64)
+            listed[t] = tile(f"listed{t}", [P, SLOTS])
             gather(listed[t], table[t], idx_list, shares)
 
-        def pool_bags(t, shares):
-            pairs = keep.tile([P, SLOTS], F32, name=f"pairs{t}", tag="third_table" if t == 1 else f"pairs{t}", align_bytes=64)
-            gather(pairs, listed[t], slot_list, shares)
+        def gather_pairs(t, shares):
+            pairs[t] = tile(f"pairs{t}", [P, SLOTS])
+            gather(pairs[t], listed[t], slot_list, shares)
+
+        def squash(t):
             s_turned = psum.tile([P, X], F32, name=f"s_turned{t}", tag=f"sum{t % 2}")
             for blk in range(X // P):
                 for j in range(2):
                     nc.tensor.matmul(
                         s_turned[:, blk * P : (blk + 1) * P],
-                        lhsT=pairs[:, 2 * P * blk + j : 2 * P * (blk + 1) : 2],
+                        lhsT=pairs[t][:, 2 * P * blk + j : 2 * P * (blk + 1) : 2],
                         rhs=identity[:],
                         is_transpose=True,
                         start=(j == 0),
                         stop=(j == 1),
                     )
-            h_turned = keep.tile([P, X], F32, name=f"h_turned{t}", tag=f"h_turned{t}")
-            nc.scalar.activation(h_turned[:], s_turned[:], ACT.Tanh)
+            h_turned[t] = tile(f"h_turned{t}", [P, X])
+            nc.scalar.activation(h_turned[t][:], s_turned[:], ACT.Tanh)
+
+        def square(t):
             h = psum.tile([P, X], F32, name=f"h{t}", tag=f"h{t % 2}")
             for blk in range(X // P):
                 cols = slice(blk * P, (blk + 1) * P)
-                nc.tensor.transpose(h[:, cols], h_turned[:, cols], identity[:])
-            if t == 2:
-                h_squared[t] = reused.tile([P, X], F32, name="h_squared2", offset=0)
-            elif t == 3:
-                h_squared[t] = late.tile([P, X], F32, name="h_squared3", offset=KIB)
-            else:
-                h_squared[t] = keep.tile([P, X], F32, name=f"h_squared{t}", tag=f"h_squared{t}")
+                nc.tensor.transpose(h[:, cols], h_turned[t][:, cols], identity[:])
+            h_squared[t] = tile(f"h_squared{t}", [P, X])
+            nc.scalar.activation(h_squared[t][:], h[:], ACT.Square)
+
+        def squash_and_square_last(t):
+            s = tile("s_last", [P, X])
+            nc.gpsimd.tensor_tensor(s[:], pairs[t][:, 0:SLOTS:2], pairs[t][:, 1:SLOTS:2], ADD)
+            h = tile("h_last", [P, X])
+            nc.scalar.activation(h[:], s[:], ACT.Tanh)
+            h_squared[t] = tile(f"h_squared{t}", [P, X])
             nc.scalar.activation(h_squared[t][:], h[:], ACT.Square)
 
         def form_slope(t):
-            slope[t] = keep.tile([P, X], F32, name=f"slope{t}", tag=("w_slot", "h_squared0", "slope2", "slope3")[t])
+            slope[t] = tile(f"slope{t}", [P, X])
             nc.gpsimd.tensor_scalar(slope[t][:], h_squared[t][:], -1.0, 1.0, MULT, ADD)
 
         def dense_backward():
-            nc.gpsimd.tensor_scalar(
-                w_bf[:].rearrange("p (t q j) -> p q t j", t=LANES, j=LANES),
-                w_raw[:].rearrange("p j (q t) -> p q t j", t=LANES),
-                1.0,
-                -0.0,
-                MULT,
-                ADD,
-            )
-            dz_bf = keep.tile([P, LANES * X], BF16, name="dz_bf", tag="listed2", align_bytes=64)
+            w_bf = tile("w_bf", [P, LANES * D], BF16)
+            dz_bf = tile("dz_bf", [P, LANES * X], BF16)
+            w_codes = tile("w_codes", [P, D], U32)
+            w_scales = tile("w_scales", [P, D], U8)
+            dz_codes = tile("dz_codes", [P, X], U32)
+            dz_scales = tile("dz_scales", [P, X], U8)
+            for half in range(2):
+                nc.gpsimd.tensor_scalar(
+                    w_bf[:].rearrange("p (t q j) -> p q t j", t=LANES, j=LANES)[:, half * P // 2 : (half + 1) * P // 2],
+                    w_raw[half][:].rearrange("p j (q t) -> p q t j", t=LANES),
+                    1.0,
+                    -0.0,
+                    MULT,
+                    ADD,
+                )
             nc.vector.tensor_copy(dz_bf[:].rearrange("p (x j) -> p x j", j=LANES), dz_raw[:].rearrange("p j x -> p x j"))
-            w_codes = keep.tile([P, D], U32, name="w_codes", tag="dz_slot", align_bytes=64)
             nc.vector.quantize_mx(w_codes[:].bitcast(E4M3X4), w_scales[:], w_bf[:])
             nc.vector.quantize_mx(dz_codes[:].bitcast(E5M2X4), dz_scales[:], dz_bf[:])
             for t in range(LANES):
@@ -171,98 +229,88 @@ def tile_attend_gfm_mlp_pl_kernel(tc, vT, W, dz, tw, offs, boffs, soffs, out_0, 
         def form_e(t):
             nc.vector.tensor_tensor(e[t][:, :X], dh[t][:], slope[t][:], MULT)
 
-        def weigh(t, half):
-            part = pieces(HALVES)[half]
-            if (t, half) == (0, 1):
-                dv[t, half] = late.tile([P, X], F32, name="dv01", offset=0)
-            else:
-                dv[t, half] = keep.tile([P, X], F32, name=f"dv{t}{half}", tag="slope3" if (t, half) == (2, 0) else f"dv{t}{half}")
-            nc.gpsimd.tensor_tensor(dv[t, half][:], e_listed[t, half], tw_listed[:, part], MULT)
+        def gather_e(t, moves):
+            e_listed[t] = tile(f"e_listed{t}", [P, SLOTS])
+            gather(e_listed[t], e[t], bag_list, list(zip(moves, pieces(HALVES))))
 
-        def scatter(t):
-            move, edges = (on_vector, HALVES) if t % 2 == 0 else (on_scalar, QUARTERS)
-            for part in pieces(edges):
-                half, at = divmod(part.start, X)
-                move(windows[t][:].indirect(entries(idx_list, part)), dv[t, half][:, at : at + part.stop - part.start])
-            nc.sync.dma_start(out_lanes[t], windows[t][:])
+        def weigh(t, piece):
+            part = pieces(PRODUCTS[t])[piece]
+            dv[t, piece] = tile(f"dv{t}{piece}", [P, part.stop - part.start])
+            nc.gpsimd.tensor_tensor(dv[t, piece][:], e_listed[t][:, part], tw_listed[:, part], MULT)
 
-        evenly = list(zip((on_vector, on_scalar), pieces(HALVES)))
-        scalar_whole = [(on_scalar, slice(0, SLOTS))]
+        def scatter(move, t, parts):
+            for part in parts:
+                piece = int(part.start >= PRODUCTS[t][1])
+                at = part.start - PRODUCTS[t][piece]
+                move(windows[t][:].indirect(entries(idx_list, part)), dv[t, piece][:, at : at + part.stop - part.start])
+            if parts[-1].stop == SLOTS:
+                nc.sync.dma_start(out_lanes[t], windows[t][:])
 
-        gather_table(0, shared)
-        table[3] = reused.tile([P, T], F32, name="table3", offset=0)
-        nc.sync.dma_start(table[3][:], vT_lanes[3])
-        pool_bags(0, shared)
-        gather_table(1, shared)
-        tw_all = reused.tile([P, T], F32, name="tw_all", offset=8 * KIB)
+        gather_table(0, shared(SLOTS // 2))
+        gather_pairs(0, shared(SLOTS // 2))
+        gather_table(1, shared(SHARE))
+        tw_all = tile("tw_all", [P, T])
         nc.sync.dma_start(tw_all[:], tw)
-        gather_table(2, shared)
-        pool_bags(1, shared)
-        pool_bags(2, shared)
+        gather_table(2, shared(SHARE))
+        squash(0)
+        gather_pairs(1, shared(SHARE))
+        gather_pairs(2, shared(SHARE))
+        square(0)
+        squash(1)
         dense_backward()
-        for t in range(3):
-            form_slope(t)
-        gather_table(3, evenly)
+        form_slope(0)
+        windows[3] = tile("window3", [P, T])
+        nc.gpsimd.memset(windows[3][:], 0.0)
+        gather_table(3, shared(LAST_SHARE))
         form_e(0)
-        pool_bags(3, evenly)
+        gather_pairs(3, shared(SLOTS // 2))
+        square(1)
+        form_slope(1)
+        squash(2)
+        tw_listed = tile("tw_listed", [P, SLOTS])
+        gather(tw_listed, tw_all, idx_list, shared(SLOTS // 2))
+        squash_and_square_last(3)
+        square(2)
+        form_slope(2)
         form_slope(3)
         form_e(1)
         form_e(2)
-        tw_listed = reused.tile([P, SLOTS], F32, name="tw_listed", offset=4 * KIB)
-        gather(tw_listed, tw_all, idx_list, scalar_whole)
-        first_listed = reused.tile([P, SLOTS], F32, name="e_listed0", offset=0)
-        e_listed = {
-            (0, 0): first_listed[:, :X],
-            (0, 1): first_listed[:, X:],
-            (1, 0): keep.tile([P, X], F32, name="e_listed10", tag="pairs3", align_bytes=64)[:],
-            (1, 1): keep.tile([P, X], F32, name="e_listed11", tag="h_turned3")[:],
-            (2, 0): keep.tile([P, X], F32, name="e_listed20")[:],
-            (2, 1): late.tile([P, X], F32, name="e_listed21", offset=2 * KIB)[:],
-            (3, 0): keep.tile([P, X], F32, name="e_listed30")[:],
-            (3, 1): keep.tile([P, X], F32, name="e_listed31")[:],
-        }
-
-        def gather_e(t):
-            move = on_vector if t % 2 == 0 else on_scalar
-            for half, part in enumerate(pieces(HALVES)):
-                move(e_listed[t, half], e[t][:].indirect(entries(bag_list, part)))
-
-        gather_e(0)
-        gather_e(1)
         form_e(3)
-        gather_e(2)
-        gather_e(3)
-        for t, half in ((0, 0), (1, 0), (0, 1), (1, 1), (2, 0), (2, 1), (3, 0), (3, 1)):
-            weigh(t, half)
+        gather_e(0, (on_vector, on_vector))
+        gather_e(1, (on_scalar, on_scalar))
+        gather_e(2, (on_vector, on_scalar))
+        gather_e(3, (on_vector, on_scalar))
+        for t, piece in ((0, 0), (1, 0), (1, 1), (2, 0), (3, 0)):
+            weigh(t, piece)
         for t in range(LANES):
-            scatter(t)
+            scatter(on_vector if t % 2 == 0 else on_scalar, t, pieces(SCATTERS[t]))
 
-        pair_words = reused.tile([P, T * LANES], BF16, name="pair_words", offset=0)
-        by_piece = pair_words[:].rearrange("p (k u c l) -> p k u c l", u=2, c=PAIR, l=2)
+        planes = tile("planes", [P, T * LANES], BF16)
+        by_piece = planes[:].rearrange("p (k t c) -> p k t c", t=LANES, c=PAIR)
+        cut = [windows[t][:].rearrange("p (k c) -> p k c", c=PAIR) for t in range(LANES)]
         for t in range(2):
-            nc.gpsimd.tensor_scalar(by_piece[:, :, 0, :, t], windows[t][:].rearrange("p (k c) -> p k c", c=PAIR), 1.0, -0.0, MULT, ADD)
-        nc.vector.tensor_copy(by_piece[:, :, 1, :, 0], windows[2][:].rearrange("p (k c) -> p k c", c=PAIR))
-        for k in range(T // PAIR):
-            nc.vector.tensor_copy(by_piece[:, k, 1, :, 1], windows[3][:, k * PAIR : (k + 1) * PAIR])
-        as_words = pair_words[:].bitcast(U32).rearrange("p (k u c) -> p k c u", u=2, c=PAIR)
-
-        signed_words = pair_words[:].bitcast(I32).rearrange("p (k u c) -> p k c u", u=2, c=PAIR)
-        rounded = keep.tile([P, T, 2], U32, name="rounded", align_bytes=64)
+            nc.gpsimd.tensor_scalar(by_piece[:, :, t, :], cut[t], 1.0, -0.0, MULT, ADD)
+        nc.vector.tensor_copy(by_piece[:, :, 2, :], cut[2])
+        nc.scalar.copy(by_piece[:, 0, 3, :], cut[3][:, 0])
+        for k in reversed(range(1, T // PAIR)):
+            nc.vector.tensor_copy(by_piece[:, k, 3, :], cut[3][:, k])
+        rounded = tile("rounded", [P, T * LANES], BF16)
         scales = keep.tile([P, T // 4], U8, name="scales", align_bytes=64)
         for first in range(0, T, PIECE):
             k, at = divmod(first, PAIR)
-            source = as_words[:, k, at : at + PIECE, :]
+            source = by_piece[:, k, :, at : at + PIECE].rearrange("p t (c i) -> p c t i", i=4)
+            out = rounded[:, LANES * first : LANES * (first + PIECE)].rearrange("p (c i t) -> p c t i", i=4, t=LANES)
             if first < T - VECTOR_WEAVES * PIECE:
-                nc.scalar.copy(rounded[:, first : first + PIECE, :], source)
+                nc.scalar.copy(out, source)
             else:
-                nc.vector.tensor_copy(rounded[:, first : first + PIECE, :].bitcast(I32), signed_words[:, k, at : at + PIECE, :])
+                nc.vector.tensor_copy(out, source)
         for cols in pieces(STORES):
             words = keep.tile([P, cols.stop - cols.start], U32, name=f"words{cols.start}", align_bytes=64)
             for first in range(cols.start, cols.stop, PIECE):
                 nc.vector.quantize_mx(
                     words[:, first - cols.start : first - cols.start + PIECE].bitcast(E4M3X4),
                     scales[4 * (first // 512) : P, first % 512 : first % 512 + PIECE],
-                    rounded[:, first : first + PIECE, :].rearrange("p c u -> p (c u)").bitcast(BF16),
+                    rounded[:, LANES * first : LANES * (first + PIECE)],
                 )
             nc.sync.dma_start(out_words[:, cols], words[:].bitcast(I32))
         for q in range(4):

@@ -25,8 +25,9 @@ PER_COL = 16
 MARGIN = 16
 BLOCK = 32
 HALVES = (0, 512, 1024)
-PRODUCTS = ((0, SLOTS), (0, 384, SLOTS), (0, SLOTS), (0, SLOTS))
-SCATTERS = ((0, SLOTS), (0, 384, 768, SLOTS), (0, SLOTS), (0, 384, 768, SLOTS))
+THIRDS = (0, 384, 768, SLOTS)
+PRODUCTS = ((0, SLOTS), THIRDS, (0, SLOTS), (0, 384, SLOTS))
+TW_SHARE = 704
 SHARE = 576
 LAST_SHARE = 384
 PIECE = 256
@@ -71,7 +72,9 @@ def tile_attend_gfm_mlp_pl_kernel(tc, vT, W, dz, tw, offs, boffs, soffs, out_0, 
             "dv10": 34,
             "dv11": 37,
             "slope3": 37,
-            "w_raw1": 40,
+            "e2": 44,
+            "dv12": 44,
+            "dz_raw1": 40,
             "slope0": 40,
             "pairs3": 48,
             "e_listed1": 48,
@@ -81,7 +84,7 @@ def tile_attend_gfm_mlp_pl_kernel(tc, vT, W, dz, tw, offs, boffs, soffs, out_0, 
             "window1": 56,
             "column": 64,
             "window2": 64,
-            "dz_bf": 72,
+            "w_bf": 72,
             "window3": 72,
         }
 
@@ -93,8 +96,8 @@ def tile_attend_gfm_mlp_pl_kernel(tc, vT, W, dz, tw, offs, boffs, soffs, out_0, 
         idx_list = lists.tile([P, SLOTS // PER_COL], U16, name="idx_list")
         bag_list = lists.tile([P, SLOTS // PER_COL], U16, name="bag_list")
         slot_list = lists.tile([P, SLOTS // PER_COL], U16, name="slot_list")
-        w_raw = [tile(f"w_raw{half}", [P, LANES, D // 2]) for half in range(2)]
-        dz_raw = tile("dz_raw", [P, LANES, X])
+        dz_raw = [tile(f"dz_raw{half}", [P, LANES, X // 2]) for half in range(2)]
+        w_raw = tile("w_raw", [P, LANES, D])
         identity = tile("identity", [P, P])
         table, listed, pairs, h_turned, h_squared, slope, dh, e_listed, dv = {}, {}, {}, {}, {}, {}, {}, {}, {}
 
@@ -124,8 +127,8 @@ def tile_attend_gfm_mlp_pl_kernel(tc, vT, W, dz, tw, offs, boffs, soffs, out_0, 
         load_table(1)
         load_table(2)
         for half in range(2):
-            nc.sync.dma_start(w_raw[half][:], W.rearrange("(p j) (h d) -> h p j d", j=LANES, h=2)[half])
-        nc.sync.dma_start(dz_raw[:], dz.rearrange("(p j) x -> p j x", j=LANES))
+            nc.sync.dma_start(dz_raw[half][:], dz.rearrange("(p j) (h x) -> h p j x", j=LANES, h=2)[half])
+        nc.sync.dma_start(w_raw[:], W.rearrange("(p j) d -> p j d", j=LANES))
         load_table(3)
         nc.sync.dma_start(bag_list[:], boffs)
 
@@ -203,16 +206,19 @@ def tile_attend_gfm_mlp_pl_kernel(tc, vT, W, dz, tw, offs, boffs, soffs, out_0, 
             dz_scales = tile("dz_scales", [P, X], U8)
             for half in range(2):
                 nc.gpsimd.tensor_scalar(
-                    w_bf[:].rearrange("p (t q j) -> p q t j", t=LANES, j=LANES)[:, half * P // 2 : (half + 1) * P // 2],
-                    w_raw[half][:].rearrange("p j (q t) -> p q t j", t=LANES),
+                    dz_bf[:].rearrange("p (x j) -> p x j", j=LANES)[:, half * X // 2 : (half + 1) * X // 2],
+                    dz_raw[half][:].rearrange("p j x -> p x j"),
                     1.0,
                     -0.0,
                     MULT,
                     ADD,
                 )
-            nc.vector.tensor_copy(dz_bf[:].rearrange("p (x j) -> p x j", j=LANES), dz_raw[:].rearrange("p j x -> p x j"))
-            nc.vector.quantize_mx(w_codes[:].bitcast(E4M3X4), w_scales[:], w_bf[:])
+            nc.vector.tensor_copy(
+                w_bf[:].rearrange("p (t q j) -> p q t j", t=LANES, j=LANES),
+                w_raw[:].rearrange("p j (q t) -> p q t j", t=LANES),
+            )
             nc.vector.quantize_mx(dz_codes[:].bitcast(E5M2X4), dz_scales[:], dz_bf[:])
+            nc.vector.quantize_mx(w_codes[:].bitcast(E4M3X4), w_scales[:], w_bf[:])
             for t in range(LANES):
                 cols = slice(t * P, (t + 1) * P)
                 dh[t] = psum.tile([P, X], F32, name=f"dh{t}", tag=f"dh{t}")
@@ -238,12 +244,11 @@ def tile_attend_gfm_mlp_pl_kernel(tc, vT, W, dz, tw, offs, boffs, soffs, out_0, 
             dv[t, piece] = tile(f"dv{t}{piece}", [P, part.stop - part.start])
             nc.gpsimd.tensor_tensor(dv[t, piece][:], e_listed[t][:, part], tw_listed[:, part], MULT)
 
-        def scatter(move, t, parts):
-            for part in parts:
-                piece = int(part.start >= PRODUCTS[t][1])
-                at = part.start - PRODUCTS[t][piece]
-                move(windows[t][:].indirect(entries(idx_list, part)), dv[t, piece][:, at : at + part.stop - part.start])
-            if parts[-1].stop == SLOTS:
+        def scatter(move, t, part):
+            piece = sum(edge <= part.start for edge in PRODUCTS[t][1:])
+            at = part.start - PRODUCTS[t][piece]
+            move(windows[t][:].indirect(entries(idx_list, part)), dv[t, piece][:, at : at + part.stop - part.start])
+            if part.stop == SLOTS:
                 nc.sync.dma_start(out_lanes[t], windows[t][:])
 
         gather_table(0, shared(SLOTS // 2))
@@ -268,7 +273,7 @@ def tile_attend_gfm_mlp_pl_kernel(tc, vT, W, dz, tw, offs, boffs, soffs, out_0, 
         form_slope(1)
         squash(2)
         tw_listed = tile("tw_listed", [P, SLOTS])
-        gather(tw_listed, tw_all, idx_list, shared(SLOTS // 2))
+        gather(tw_listed, tw_all, idx_list, shared(TW_SHARE))
         squash_and_square_last(3)
         square(2)
         form_slope(2)
@@ -280,20 +285,23 @@ def tile_attend_gfm_mlp_pl_kernel(tc, vT, W, dz, tw, offs, boffs, soffs, out_0, 
         gather_e(1, (on_scalar, on_scalar))
         gather_e(2, (on_vector, on_scalar))
         gather_e(3, (on_vector, on_scalar))
-        for t, piece in ((0, 0), (1, 0), (1, 1), (2, 0), (3, 0)):
+        for t, piece in ((0, 0), (1, 0), (1, 1), (3, 0), (1, 2), (2, 0), (3, 1)):
             weigh(t, piece)
-        for t in range(LANES):
-            scatter(on_vector if t % 2 == 0 else on_scalar, t, pieces(SCATTERS[t]))
+        for t in (0, 2):
+            scatter(on_vector, t, slice(0, SLOTS))
+        for t, third in ((1, 0), (1, 1), (3, 0), (1, 2), (3, 1), (3, 2)):
+            scatter(on_scalar, t, pieces(THIRDS)[third])
 
         planes = tile("planes", [P, T * LANES], BF16)
         by_piece = planes[:].rearrange("p (k t c) -> p k t c", t=LANES, c=PAIR)
         cut = [windows[t][:].rearrange("p (k c) -> p k c", c=PAIR) for t in range(LANES)]
         for t in range(2):
             nc.gpsimd.tensor_scalar(by_piece[:, :, t, :], cut[t], 1.0, -0.0, MULT, ADD)
-        nc.vector.tensor_copy(by_piece[:, :, 2, :], cut[2])
-        nc.scalar.copy(by_piece[:, 0, 3, :], cut[3][:, 0])
-        for k in reversed(range(1, T // PAIR)):
-            nc.vector.tensor_copy(by_piece[:, k, 3, :], cut[3][:, k])
+        for half in (slice(0, 2), slice(2, 4)):
+            nc.vector.tensor_copy(by_piece[:, half, 2, :], cut[2][:, half])
+        for k in range(2):
+            nc.scalar.copy(by_piece[:, k, 3, :], cut[3][:, k])
+        nc.vector.tensor_copy(by_piece[:, 2:, 3, :], cut[3][:, 2:])
         rounded = tile("rounded", [P, T * LANES], BF16)
         scales = keep.tile([P, T // 4], U8, name="scales", align_bytes=64)
         for first in range(0, T, PIECE):

@@ -31,8 +31,8 @@ TW_SHARE = 704
 SHARE = 576
 LAST_SHARE = 384
 PIECE = 256
-PAIR = 512
-VECTOR_WEAVES = 4
+VECTOR_WEAVES = (0, 256, 512, 768, 1152)
+SCALAR_WEAVES = (1152, 1280, 1536, 1792, 2048)
 STORES = (0, 512, 1024, 1536, 1792, 2048)
 KIB = 1024
 
@@ -284,7 +284,8 @@ def tile_attend_gfm_mlp_pl_kernel(tc, vT, W, dz, tw, offs, boffs, soffs, out_0, 
         gather_e(0, (on_vector, on_vector))
         gather_e(1, (on_scalar, on_scalar))
         gather_e(2, (on_vector, on_scalar))
-        gather_e(3, (on_vector, on_scalar))
+        e_listed[3] = tile("e_listed3", [P, SLOTS])
+        gather(e_listed[3], e[3], bag_list, [(on_vector, slice(0, 192)), (on_scalar, slice(192, 608)), (on_scalar, slice(608, SLOTS))])
         for t, piece in ((0, 0), (1, 0), (1, 1), (3, 0), (1, 2), (2, 0), (3, 1)):
             weigh(t, piece)
         for t in (0, 2):
@@ -292,26 +293,19 @@ def tile_attend_gfm_mlp_pl_kernel(tc, vT, W, dz, tw, offs, boffs, soffs, out_0, 
         for t, third in ((1, 0), (1, 1), (3, 0), (1, 2), (3, 1), (3, 2)):
             scatter(on_scalar, t, pieces(THIRDS)[third])
 
-        planes = tile("planes", [P, T * LANES], BF16)
-        by_piece = planes[:].rearrange("p (k t c) -> p k t c", t=LANES, c=PAIR)
-        cut = [windows[t][:].rearrange("p (k c) -> p k c", c=PAIR) for t in range(LANES)]
+        planes = tile("planes", [P, LANES, T], BF16)
         for t in range(2):
-            nc.gpsimd.tensor_scalar(by_piece[:, :, t, :], cut[t], 1.0, -0.0, MULT, ADD)
-        for half in (slice(0, 2), slice(2, 4)):
-            nc.vector.tensor_copy(by_piece[:, half, 2, :], cut[2][:, half])
-        for k in range(2):
-            nc.scalar.copy(by_piece[:, k, 3, :], cut[3][:, k])
-        nc.vector.tensor_copy(by_piece[:, 2:, 3, :], cut[3][:, 2:])
+            nc.gpsimd.tensor_scalar(planes[:, t, :], windows[t][:], 1.0, -0.0, MULT, ADD)
+        nc.vector.tensor_copy(planes[:, 2, :], windows[2][:])
+        nc.vector.tensor_copy(planes[:, 3, : SCALAR_WEAVES[0]], windows[3][:, : SCALAR_WEAVES[0]])
+        for cols in pieces(SCALAR_WEAVES[::2]):
+            nc.scalar.copy(planes[:, 3, cols], windows[3][:, cols])
         rounded = tile("rounded", [P, T * LANES], BF16)
-        scales = keep.tile([P, T // 4], U8, name="scales", align_bytes=64)
-        for first in range(0, T, PIECE):
-            k, at = divmod(first, PAIR)
-            source = by_piece[:, k, :, at : at + PIECE].rearrange("p t (c i) -> p c t i", i=4)
-            out = rounded[:, LANES * first : LANES * (first + PIECE)].rearrange("p (c i t) -> p c t i", i=4, t=LANES)
-            if first < T - VECTOR_WEAVES * PIECE:
-                nc.scalar.copy(out, source)
-            else:
-                nc.vector.tensor_copy(out, source)
+        scales = tile("scales", [P, T // 4], U8)
+        for copy, edges in ((nc.vector.tensor_copy, VECTOR_WEAVES), (nc.scalar.copy, SCALAR_WEAVES)):
+            for cols in pieces(edges):
+                out = rounded[:, LANES * cols.start : LANES * cols.stop].rearrange("p (c i t) -> p c t i", i=4, t=LANES)
+                copy(out, planes[:, :, cols].rearrange("p t (c i) -> p c t i", i=4))
         for cols in pieces(STORES):
             words = keep.tile([P, cols.stop - cols.start], U32, name=f"words{cols.start}", align_bytes=64)
             for first in range(cols.start, cols.stop, PIECE):

@@ -26,14 +26,15 @@ MARGIN = 16
 BLOCK = 32
 HALVES = (0, 512, 1024)
 THIRDS = (0, 384, 768, SLOTS)
-PRODUCTS = ((0, SLOTS), THIRDS, (0, SLOTS), (0, 384, SLOTS))
+LAST_THIRDS = (0, 256, 640, SLOTS)
+PRODUCTS = ((0, SLOTS), THIRDS, (0, SLOTS), (0, 256, SLOTS))
 TW_SHARE = 704
 SHARE = 576
 LAST_SHARE = 384
 PIECE = 256
-VECTOR_WEAVES = (0, 256, 512, 768, 1152)
-SCALAR_WEAVES = (1152, 1280, 1536, 1792, 2048)
-STORES = (0, 512, 1024, 1536, 1792, 2048)
+VECTOR_PIECES = 2
+GPSIMD_PIECES = 7
+STORES = (0, 512, 1024, 1536, 2048)
 KIB = 1024
 
 FLOPS = 2 * M * D * X
@@ -60,7 +61,8 @@ def tile_attend_gfm_mlp_pl_kernel(tc, vT, W, dz, tw, offs, boffs, soffs, out_0, 
             "table3": 0,
             "h_turned2": 0,
             "h_squared1": 2,
-            "planes": 0,
+            "early_words": 0,
+            "late_words": 52,
             "tw_listed": 8,
             "table1": 16,
             "tw_all": 16,
@@ -248,8 +250,6 @@ def tile_attend_gfm_mlp_pl_kernel(tc, vT, W, dz, tw, offs, boffs, soffs, out_0, 
             piece = sum(edge <= part.start for edge in PRODUCTS[t][1:])
             at = part.start - PRODUCTS[t][piece]
             move(windows[t][:].indirect(entries(idx_list, part)), dv[t, piece][:, at : at + part.stop - part.start])
-            if part.stop == SLOTS:
-                nc.sync.dma_start(out_lanes[t], windows[t][:])
 
         gather_table(0, shared(SLOTS // 2))
         gather_pairs(0, shared(SLOTS // 2))
@@ -291,22 +291,42 @@ def tile_attend_gfm_mlp_pl_kernel(tc, vT, W, dz, tw, offs, boffs, soffs, out_0, 
         for t in (0, 2):
             scatter(on_vector, t, slice(0, SLOTS))
         for t, third in ((1, 0), (1, 1), (3, 0), (1, 2), (3, 1), (3, 2)):
-            scatter(on_scalar, t, pieces(THIRDS)[third])
+            scatter(on_scalar, t, pieces(THIRDS if t == 1 else LAST_THIRDS)[third])
+        for t in range(LANES):
+            nc.sync.dma_start(out_lanes[t], windows[t][:])
 
-        planes = tile("planes", [P, LANES, T], BF16)
+        early_words = tile("early_words", [P, GPSIMD_PIECES * PIECE * LANES], BF16)
+        late_words = tile("late_words", [P, PIECE * LANES], BF16)
+
+        def pair_words(run):
+            if run.start == VECTOR_PIECES:
+                return late_words[:]
+            skipped = int(run.start > VECTOR_PIECES)
+            return early_words[:, (run.start - skipped) * PIECE * LANES : (run.stop - skipped) * PIECE * LANES]
+
+        def round_lane(copy, t, run):
+            halves = pair_words(run).rearrange("p (k u c l) -> p k u c l", u=2, c=PIECE, l=2)
+            copy(halves[:, :, t // 2, :, t % 2], windows[t][:].rearrange("p (k c) -> p k c", c=PIECE)[:, run, :])
+
+        def on_gpsimd(out, in_):
+            nc.gpsimd.tensor_scalar(out, in_, 1.0, -0.0, MULT, ADD)
+
+        first_run, late, last_run = pieces((0, VECTOR_PIECES, VECTOR_PIECES + 1, T // PIECE))
         for t in range(2):
-            nc.gpsimd.tensor_scalar(planes[:, t, :], windows[t][:], 1.0, -0.0, MULT, ADD)
-        nc.vector.tensor_copy(planes[:, 2, :], windows[2][:])
-        nc.vector.tensor_copy(planes[:, 3, : SCALAR_WEAVES[0]], windows[3][:, : SCALAR_WEAVES[0]])
-        for cols in pieces(SCALAR_WEAVES[::2]):
-            nc.scalar.copy(planes[:, 3, cols], windows[3][:, cols])
+            round_lane(on_gpsimd, t, first_run)
+            round_lane(on_gpsimd, t, last_run)
+        for run in (first_run, slice(3, 7), slice(7, 8)):
+            round_lane(on_vector, 2, run)
+        for t in range(3):
+            round_lane(on_vector, t, late)
         rounded = tile("rounded", [P, T * LANES], BF16)
         scales = tile("scales", [P, T // 4], U8)
-        for copy, edges in ((nc.vector.tensor_copy, VECTOR_WEAVES), (nc.scalar.copy, SCALAR_WEAVES)):
-            for cols in pieces(edges):
-                out = rounded[:, LANES * cols.start : LANES * cols.stop].rearrange("p (c i t) -> p c t i", i=4, t=LANES)
-                copy(out, planes[:, :, cols].rearrange("p t (c i) -> p c t i", i=4))
-        for cols in pieces(STORES):
+
+        def weave(copy, dtype, run):
+            out = rounded[:].bitcast(dtype).rearrange("p (k c u) -> p k c u", c=PIECE, u=2)
+            copy(out[:, run], pair_words(run).bitcast(dtype).rearrange("p (k u c) -> p k c u", u=2, c=PIECE))
+
+        def quantize_and_store(cols):
             words = keep.tile([P, cols.stop - cols.start], U32, name=f"words{cols.start}", align_bytes=64)
             for first in range(cols.start, cols.stop, PIECE):
                 nc.vector.quantize_mx(
@@ -315,6 +335,17 @@ def tile_attend_gfm_mlp_pl_kernel(tc, vT, W, dz, tw, offs, boffs, soffs, out_0, 
                     rounded[:, LANES * first : LANES * (first + PIECE)],
                 )
             nc.sync.dma_start(out_words[:, cols], words[:].bitcast(I32))
+
+        for run in (late, first_run, slice(3, 5)):
+            round_lane(on_vector, 3, run)
+        weave(nc.vector.tensor_copy, I32, first_run)
+        round_lane(on_vector, 3, slice(5, 7))
+        quantize_and_store(pieces(STORES)[0])
+        round_lane(on_vector, 3, slice(7, 8))
+        for k in range(VECTOR_PIECES, T // PIECE):
+            weave(nc.scalar.copy, U32, slice(k, k + 1))
+        for cols in pieces(STORES)[1:]:
+            quantize_and_store(cols)
         for q in range(4):
             queue = nc.sync if q % 2 == 0 else nc.scalar
             queue.dma_start(out_scales[q], scales[32 * q : 32 * q + 16, :].bitcast(I32))

@@ -27,13 +27,13 @@ BLOCK = 32
 HALVES = (0, 512, 1024)
 THIRDS = (0, 384, 768, SLOTS)
 LAST_THIRDS = (0, 256, 640, SLOTS)
-PRODUCTS = ((0, SLOTS), THIRDS, (0, SLOTS), (0, 256, SLOTS))
+PRODUCTS = ((0, 384, SLOTS), THIRDS, (0, SLOTS), (0, 256, SLOTS))
 TW_SHARE = 704
 SHARE = 576
 LAST_SHARE = 384
 PIECE = 256
 VECTOR_PIECES = 2
-GPSIMD_PIECES = 7
+GPSIMD_PIECES = 6
 STORES = (0, 512, 1024, 1536, 2048)
 KIB = 1024
 
@@ -69,7 +69,8 @@ def tile_attend_gfm_mlp_pl_kernel(tc, vT, W, dz, tw, offs, boffs, soffs, out_0, 
             "table2": 24,
             "pairs1": 24,
             "h_turned0": 28,
-            "dv00": 30,
+            "dv00": 32,
+            "dv01": 38.5,
             "h_squared3": 33,
             "dv10": 34,
             "dv11": 37,
@@ -92,7 +93,7 @@ def tile_attend_gfm_mlp_pl_kernel(tc, vT, W, dz, tw, offs, boffs, soffs, out_0, 
 
         def tile(name, shape, dtype=F32):
             if name in places:
-                return reused.tile(shape, dtype, name=name, offset=places[name] * KIB, align_bytes=64)
+                return reused.tile(shape, dtype, name=name, offset=int(places[name] * KIB), align_bytes=64)
             return keep.tile(shape, dtype, name=name, align_bytes=64)
 
         idx_list = lists.tile([P, SLOTS // PER_COL], U16, name="idx_list")
@@ -284,25 +285,28 @@ def tile_attend_gfm_mlp_pl_kernel(tc, vT, W, dz, tw, offs, boffs, soffs, out_0, 
         gather_e(0, (on_vector, on_vector))
         gather_e(1, (on_scalar, on_scalar))
         gather_e(2, (on_vector, on_scalar))
-        e_listed[3] = tile("e_listed3", [P, SLOTS])
-        gather(e_listed[3], e[3], bag_list, [(on_vector, slice(0, 192)), (on_scalar, slice(192, 608)), (on_scalar, slice(608, SLOTS))])
-        for t, piece in ((0, 0), (1, 0), (1, 1), (3, 0), (1, 2), (2, 0), (3, 1)):
+        gather_e(3, (on_vector, on_scalar))
+        for t, piece in ((0, 0), (1, 0), (0, 1), (1, 1), (3, 0), (1, 2), (2, 0), (3, 1)):
             weigh(t, piece)
         for t in (0, 2):
-            scatter(on_vector, t, slice(0, SLOTS))
+            for part in pieces(PRODUCTS[t]):
+                scatter(on_vector, t, part)
         for t, third in ((1, 0), (1, 1), (3, 0), (1, 2), (3, 1), (3, 2)):
             scatter(on_scalar, t, pieces(THIRDS if t == 1 else LAST_THIRDS)[third])
         for t in range(LANES):
             nc.sync.dma_start(out_lanes[t], windows[t][:])
 
         early_words = tile("early_words", [P, GPSIMD_PIECES * PIECE * LANES], BF16)
-        late_words = tile("late_words", [P, PIECE * LANES], BF16)
+        late_words = tile("late_words", [P, (T // PIECE - GPSIMD_PIECES) * PIECE * LANES], BF16)
 
         def pair_words(run):
-            if run.start == VECTOR_PIECES:
-                return late_words[:]
-            skipped = int(run.start > VECTOR_PIECES)
-            return early_words[:, (run.start - skipped) * PIECE * LANES : (run.stop - skipped) * PIECE * LANES]
+            if run.start < late.start:
+                words, first = early_words, 0
+            elif run.start < late.stop:
+                words, first = late_words, late.start
+            else:
+                words, first = early_words, late.stop - late.start
+            return words[:, (run.start - first) * PIECE * LANES : (run.stop - first) * PIECE * LANES]
 
         def round_lane(copy, t, run):
             halves = pair_words(run).rearrange("p (k u c l) -> p k u c l", u=2, c=PIECE, l=2)
@@ -311,11 +315,11 @@ def tile_attend_gfm_mlp_pl_kernel(tc, vT, W, dz, tw, offs, boffs, soffs, out_0, 
         def on_gpsimd(out, in_):
             nc.gpsimd.tensor_scalar(out, in_, 1.0, -0.0, MULT, ADD)
 
-        first_run, late, last_run = pieces((0, VECTOR_PIECES, VECTOR_PIECES + 1, T // PIECE))
+        first_run, late, last_run = pieces((0, VECTOR_PIECES, VECTOR_PIECES + T // PIECE - GPSIMD_PIECES, T // PIECE))
         for t in range(2):
             round_lane(on_gpsimd, t, first_run)
             round_lane(on_gpsimd, t, last_run)
-        for run in (first_run, slice(3, 7), slice(7, 8)):
+        for run in (first_run, last_run):
             round_lane(on_vector, 2, run)
         for t in range(3):
             round_lane(on_vector, t, late)
@@ -336,12 +340,11 @@ def tile_attend_gfm_mlp_pl_kernel(tc, vT, W, dz, tw, offs, boffs, soffs, out_0, 
                 )
             nc.sync.dma_start(out_words[:, cols], words[:].bitcast(I32))
 
-        for run in (late, first_run, slice(3, 5)):
+        for run in (late, first_run, slice(4, 6)):
             round_lane(on_vector, 3, run)
         weave(nc.vector.tensor_copy, I32, first_run)
-        round_lane(on_vector, 3, slice(5, 7))
+        round_lane(on_vector, 3, slice(6, 8))
         quantize_and_store(pieces(STORES)[0])
-        round_lane(on_vector, 3, slice(7, 8))
         for k in range(VECTOR_PIECES, T // PIECE):
             weave(nc.scalar.copy, U32, slice(k, k + 1))
         for cols in pieces(STORES)[1:]:

@@ -31,6 +31,8 @@ PRODUCTS = ((0, 384, SLOTS), THIRDS, (0, SLOTS), (0, 256, SLOTS))
 TW_SHARE = 704
 SHARE = 576
 LAST_SHARE = 384
+LAST_E_SHARE = 384
+DZ_SHARE = 384
 PIECE = 256
 VECTOR_PIECES = 2
 GPSIMD_PIECES = 6
@@ -77,8 +79,8 @@ def tile_attend_gfm_mlp_pl_kernel(tc, vT, W, dz, tw, offs, boffs, soffs, out_0, 
             "slope3": 37,
             "e2": 44,
             "dv12": 44,
-            "dz_raw1": 40,
-            "slope0": 40,
+            "dz_raw": 84,
+            "slope0": 84,
             "pairs3": 48,
             "e_listed1": 48,
             "e3": 52,
@@ -99,7 +101,7 @@ def tile_attend_gfm_mlp_pl_kernel(tc, vT, W, dz, tw, offs, boffs, soffs, out_0, 
         idx_list = lists.tile([P, SLOTS // PER_COL], U16, name="idx_list")
         bag_list = lists.tile([P, SLOTS // PER_COL], U16, name="bag_list")
         slot_list = lists.tile([P, SLOTS // PER_COL], U16, name="slot_list")
-        dz_raw = [tile(f"dz_raw{half}", [P, LANES, X // 2]) for half in range(2)]
+        dz_raw = tile("dz_raw", [P, LANES, X])
         w_raw = tile("w_raw", [P, LANES, D])
         identity = tile("identity", [P, P])
         table, listed, pairs, h_turned, h_squared, slope, dh, e_listed, dv = {}, {}, {}, {}, {}, {}, {}, {}, {}
@@ -129,8 +131,7 @@ def tile_attend_gfm_mlp_pl_kernel(tc, vT, W, dz, tw, offs, boffs, soffs, out_0, 
         nc.sync.dma_start(slot_list[:], soffs)
         load_table(1)
         load_table(2)
-        for half in range(2):
-            nc.sync.dma_start(dz_raw[half][:], dz.rearrange("(p j) (h x) -> h p j x", j=LANES, h=2)[half])
+        nc.sync.dma_start(dz_raw[:], dz.rearrange("(p j) x -> p j x", j=LANES))
         nc.sync.dma_start(w_raw[:], W.rearrange("(p j) d -> p j d", j=LANES))
         load_table(3)
         nc.sync.dma_start(bag_list[:], boffs)
@@ -150,7 +151,7 @@ def tile_attend_gfm_mlp_pl_kernel(tc, vT, W, dz, tw, offs, boffs, soffs, out_0, 
         for first in range(0, P, BLOCK):
             block = slice(first, first + BLOCK)
             nc.vector.tensor_tensor(identity[block, block], row[block, :], column[block, :], mybir.AluOpType.is_equal)
-        e = [tile(f"e{t}", [P, X + MARGIN]) for t in range(LANES)]
+        e = [tile(f"e{t}", [P, (SLOTS - LAST_E_SHARE if t == LANES - 1 else X) + MARGIN]) for t in range(LANES)]
         for t in range(LANES):
             nc.gpsimd.memset(e[t][:, X:], 0.0)
         for t in (1, 2):
@@ -207,15 +208,10 @@ def tile_attend_gfm_mlp_pl_kernel(tc, vT, W, dz, tw, offs, boffs, soffs, out_0, 
             w_scales = tile("w_scales", [P, D], U8)
             dz_codes = tile("dz_codes", [P, X], U32)
             dz_scales = tile("dz_scales", [P, X], U8)
-            for half in range(2):
-                nc.gpsimd.tensor_scalar(
-                    dz_bf[:].rearrange("p (x j) -> p x j", j=LANES)[:, half * X // 2 : (half + 1) * X // 2],
-                    dz_raw[half][:].rearrange("p j x -> p x j"),
-                    1.0,
-                    -0.0,
-                    MULT,
-                    ADD,
-                )
+            dz_out = dz_bf[:].rearrange("p (x j) -> p x j", j=LANES)
+            dz_in = dz_raw[:].rearrange("p j x -> p x j")
+            nc.gpsimd.tensor_scalar(dz_out[:, :DZ_SHARE], dz_in[:, :DZ_SHARE], 1.0, -0.0, MULT, ADD)
+            nc.vector.tensor_copy(dz_out[:, DZ_SHARE:], dz_in[:, DZ_SHARE:])
             nc.vector.tensor_copy(
                 w_bf[:].rearrange("p (t q j) -> p q t j", t=LANES, j=LANES),
                 w_raw[:].rearrange("p j (q t) -> p q t j", t=LANES),
@@ -260,7 +256,7 @@ def tile_attend_gfm_mlp_pl_kernel(tc, vT, W, dz, tw, offs, boffs, soffs, out_0, 
         gather_table(2, shared(SHARE))
         squash(0)
         gather_pairs(1, shared(SHARE))
-        gather_pairs(2, shared(SHARE))
+        gather_pairs(2, shared(LAST_SHARE))
         square(0)
         squash(1)
         dense_backward()
@@ -285,7 +281,8 @@ def tile_attend_gfm_mlp_pl_kernel(tc, vT, W, dz, tw, offs, boffs, soffs, out_0, 
         gather_e(0, (on_vector, on_vector))
         gather_e(1, (on_scalar, on_scalar))
         gather_e(2, (on_vector, on_scalar))
-        gather_e(3, (on_vector, on_scalar))
+        e_listed[3] = tile("e_listed3", [P, SLOTS])
+        gather(e_listed[3], e[3], bag_list, shared(LAST_E_SHARE))
         for t, piece in ((0, 0), (1, 0), (0, 1), (1, 1), (3, 0), (1, 2), (2, 0), (3, 1)):
             weigh(t, piece)
         for t in (0, 2):

@@ -27,12 +27,13 @@ BLOCK = 32
 HALVES = (0, 512, 1024)
 THIRDS = (0, 384, 768, SLOTS)
 LAST_THIRDS = (0, 256, 640, SLOTS)
-PRODUCTS = ((0, 384, SLOTS), THIRDS, (0, SLOTS), (0, 256, SLOTS))
-TW_SHARE = 704
+PRODUCTS = ((0, 256, SLOTS), THIRDS, (0, SLOTS), (0, 256, SLOTS))
+TW_SHARE = 384
+RUN = T // P
 SHARE = 576
 LAST_SHARE = 384
-LAST_E_SHARE = 384
-DZ_SHARE = 384
+E_SHARES = (512, 448)
+E_WINDOW = 640 + MARGIN
 PIECE = 256
 VECTOR_PIECES = 2
 GPSIMD_PIECES = 6
@@ -66,25 +67,23 @@ def tile_attend_gfm_mlp_pl_kernel(tc, vT, W, dz, tw, offs, boffs, soffs, out_0, 
             "early_words": 0,
             "late_words": 52,
             "tw_listed": 8,
-            "table1": 16,
-            "tw_all": 16,
             "table2": 24,
             "pairs1": 24,
             "h_turned0": 28,
-            "dv00": 32,
-            "dv01": 38.5,
-            "h_squared3": 33,
-            "dv10": 34,
+            "dv12": 38.5,
             "dv11": 37,
             "slope3": 37,
-            "e2": 44,
-            "dv12": 44,
-            "dz_raw": 84,
-            "slope0": 84,
-            "pairs3": 48,
-            "e_listed1": 48,
-            "e3": 52,
+            "h_squared3": 44,
+            "dv01": 45,
+            "dz_raw1": 40,
+            "slope0": 40,
+            "pairs3": 84,
+            "dv00": 84,
+            "dv10": 85,
+            "e_listed1_384": 86.5,
             "dv20": 52,
+            "row": 16,
+            "window0": 16,
             "ones": 56,
             "window1": 56,
             "column": 64,
@@ -101,7 +100,7 @@ def tile_attend_gfm_mlp_pl_kernel(tc, vT, W, dz, tw, offs, boffs, soffs, out_0, 
         idx_list = lists.tile([P, SLOTS // PER_COL], U16, name="idx_list")
         bag_list = lists.tile([P, SLOTS // PER_COL], U16, name="bag_list")
         slot_list = lists.tile([P, SLOTS // PER_COL], U16, name="slot_list")
-        dz_raw = tile("dz_raw", [P, LANES, X])
+        dz_raw = [tile(f"dz_raw{half}", [P, LANES, X // 2]) for half in range(2)]
         w_raw = tile("w_raw", [P, LANES, D])
         identity = tile("identity", [P, P])
         table, listed, pairs, h_turned, h_squared, slope, dh, e_listed, dv = {}, {}, {}, {}, {}, {}, {}, {}, {}
@@ -126,12 +125,15 @@ def tile_attend_gfm_mlp_pl_kernel(tc, vT, W, dz, tw, offs, boffs, soffs, out_0, 
             for move, part in shares:
                 move(out[:, part], window[:].indirect(entries(a_list, part)))
 
+        tw_runs = tile("tw_runs", [P, RUN])
+        nc.sync.dma_start(tw_runs[:], tw[0].rearrange("(n m) -> n m", m=RUN))
         load_table(0)
         nc.sync.dma_start(idx_list[:], offs)
         nc.sync.dma_start(slot_list[:], soffs)
         load_table(1)
         load_table(2)
-        nc.sync.dma_start(dz_raw[:], dz.rearrange("(p j) x -> p j x", j=LANES))
+        for half in range(2):
+            nc.sync.dma_start(dz_raw[half][:], dz.rearrange("(p j) (h x) -> h p j x", j=LANES, h=2)[half])
         nc.sync.dma_start(w_raw[:], W.rearrange("(p j) d -> p j d", j=LANES))
         load_table(3)
         nc.sync.dma_start(bag_list[:], boffs)
@@ -139,8 +141,6 @@ def tile_attend_gfm_mlp_pl_kernel(tc, vT, W, dz, tw, offs, boffs, soffs, out_0, 
         warm = tile("warm", [P, 2])
         nc.vector.memset(warm[:, 0:1], 0.0)
         nc.scalar.activation(warm[:, 1:2], warm[:, 0:1], ACT.Tanh)
-        windows = {0: tile("window0", [P, T])}
-        nc.vector.memset(windows[0][:], 0.0)
         ones = tile("ones", [P, BLOCK])
         column = tile("column", [P, BLOCK])
         row = tile("row", [P, BLOCK])
@@ -151,10 +151,22 @@ def tile_attend_gfm_mlp_pl_kernel(tc, vT, W, dz, tw, offs, boffs, soffs, out_0, 
         for first in range(0, P, BLOCK):
             block = slice(first, first + BLOCK)
             nc.vector.tensor_tensor(identity[block, block], row[block, :], column[block, :], mybir.AluOpType.is_equal)
-        e = [tile(f"e{t}", [P, (SLOTS - LAST_E_SHARE if t == LANES - 1 else X) + MARGIN]) for t in range(LANES)]
+        windows = {}
+        tw_all = tile("tw_all", [P, T])
+        for bank in range(LANES):
+            spread = psum.tile([P, X], F32, name=f"spread{bank}", tag=f"dh{bank}")
+            for i in range(LANES):
+                m = LANES * bank + i
+                nc.tensor.transpose(spread[:, i * P : (i + 1) * P], tw_runs[:, m : m + 1].to_broadcast([P, P]), identity[:])
+            move = on_vector if bank % 2 == 0 else on_scalar
+            move(
+                tw_all[:].rearrange("p (n b i) -> p n b i", b=LANES, i=LANES)[:, :, bank, :],
+                spread[:].rearrange("p (i n) -> p n i", i=LANES),
+            )
+        e = [tile(f"e{t}", [P, E_WINDOW]) for t in range(LANES)]
         for t in range(LANES):
             nc.gpsimd.memset(e[t][:, X:], 0.0)
-        for t in (1, 2):
+        for t in range(LANES - 1):
             windows[t] = tile(f"window{t}", [P, T])
             nc.gpsimd.memset(windows[t][:], 0.0)
 
@@ -208,10 +220,15 @@ def tile_attend_gfm_mlp_pl_kernel(tc, vT, W, dz, tw, offs, boffs, soffs, out_0, 
             w_scales = tile("w_scales", [P, D], U8)
             dz_codes = tile("dz_codes", [P, X], U32)
             dz_scales = tile("dz_scales", [P, X], U8)
-            dz_out = dz_bf[:].rearrange("p (x j) -> p x j", j=LANES)
-            dz_in = dz_raw[:].rearrange("p j x -> p x j")
-            nc.gpsimd.tensor_scalar(dz_out[:, :DZ_SHARE], dz_in[:, :DZ_SHARE], 1.0, -0.0, MULT, ADD)
-            nc.vector.tensor_copy(dz_out[:, DZ_SHARE:], dz_in[:, DZ_SHARE:])
+            for half in range(2):
+                nc.gpsimd.tensor_scalar(
+                    dz_bf[:].rearrange("p (x j) -> p x j", j=LANES)[:, half * X // 2 : (half + 1) * X // 2],
+                    dz_raw[half][:].rearrange("p j x -> p x j"),
+                    1.0,
+                    -0.0,
+                    MULT,
+                    ADD,
+                )
             nc.vector.tensor_copy(
                 w_bf[:].rearrange("p (t q j) -> p q t j", t=LANES, j=LANES),
                 w_raw[:].rearrange("p j (q t) -> p q t j", t=LANES),
@@ -234,14 +251,18 @@ def tile_attend_gfm_mlp_pl_kernel(tc, vT, W, dz, tw, offs, boffs, soffs, out_0, 
         def form_e(t):
             nc.vector.tensor_tensor(e[t][:, :X], dh[t][:], slope[t][:], MULT)
 
-        def gather_e(t, moves):
-            e_listed[t] = tile(f"e_listed{t}", [P, SLOTS])
-            gather(e_listed[t], e[t], bag_list, list(zip(moves, pieces(HALVES))))
+        def gather_e(t, span, shares):
+            listed_e = tile(f"e_listed{t}_{span.start}", [P, span.stop - span.start])
+            e_listed[t, span.start] = listed_e
+            for move, part in shares:
+                move(listed_e[:, part.start - span.start : part.stop - span.start], e[t][:].indirect(entries(bag_list, part)))
 
         def weigh(t, piece):
             part = pieces(PRODUCTS[t])[piece]
             dv[t, piece] = tile(f"dv{t}{piece}", [P, part.stop - part.start])
-            nc.gpsimd.tensor_tensor(dv[t, piece][:], e_listed[t][:, part], tw_listed[:, part], MULT)
+            first = max(start for lane, start in e_listed if lane == t and start <= part.start)
+            listed_e = e_listed[t, first][:, part.start - first : part.stop - first]
+            nc.gpsimd.tensor_tensor(dv[t, piece][:], listed_e, tw_listed[:, part], MULT)
 
         def scatter(move, t, part):
             piece = sum(edge <= part.start for edge in PRODUCTS[t][1:])
@@ -250,9 +271,9 @@ def tile_attend_gfm_mlp_pl_kernel(tc, vT, W, dz, tw, offs, boffs, soffs, out_0, 
 
         gather_table(0, shared(SLOTS // 2))
         gather_pairs(0, shared(SLOTS // 2))
+        tw_listed = tile("tw_listed", [P, SLOTS])
+        gather(tw_listed, tw_all, idx_list, shared(TW_SHARE))
         gather_table(1, shared(SHARE))
-        tw_all = tile("tw_all", [P, T])
-        nc.sync.dma_start(tw_all[:], tw)
         gather_table(2, shared(SHARE))
         squash(0)
         gather_pairs(1, shared(SHARE))
@@ -269,26 +290,29 @@ def tile_attend_gfm_mlp_pl_kernel(tc, vT, W, dz, tw, offs, boffs, soffs, out_0, 
         square(1)
         form_slope(1)
         squash(2)
-        tw_listed = tile("tw_listed", [P, SLOTS])
-        gather(tw_listed, tw_all, idx_list, shared(TW_SHARE))
+        whole = slice(0, SLOTS)
+        first_third, other_thirds = pieces((0, THIRDS[1], SLOTS))
+        form_e(1)
+        gather_e(0, whole, [(on_vector, half) for half in pieces(HALVES)])
+        gather_e(1, first_third, [(on_scalar, first_third)])
         squash_and_square_last(3)
         square(2)
         form_slope(2)
         form_slope(3)
-        form_e(1)
+        weigh(0, 0)
+        weigh(1, 0)
+        gather_e(1, other_thirds, [(on_scalar, other_thirds)])
+        scatter(on_vector, 0, pieces(PRODUCTS[0])[0])
+        scatter(on_scalar, 1, first_third)
         form_e(2)
         form_e(3)
-        gather_e(0, (on_vector, on_vector))
-        gather_e(1, (on_scalar, on_scalar))
-        gather_e(2, (on_vector, on_scalar))
-        e_listed[3] = tile("e_listed3", [P, SLOTS])
-        gather(e_listed[3], e[3], bag_list, shared(LAST_E_SHARE))
-        for t, piece in ((0, 0), (1, 0), (0, 1), (1, 1), (3, 0), (1, 2), (2, 0), (3, 1)):
+        gather_e(2, whole, shared(E_SHARES[0]))
+        gather_e(3, whole, shared(E_SHARES[1]))
+        for t, piece in ((0, 1), (1, 1), (3, 0), (1, 2), (2, 0), (3, 1)):
             weigh(t, piece)
-        for t in (0, 2):
-            for part in pieces(PRODUCTS[t]):
-                scatter(on_vector, t, part)
-        for t, third in ((1, 0), (1, 1), (3, 0), (1, 2), (3, 1), (3, 2)):
+        scatter(on_vector, 0, pieces(PRODUCTS[0])[1])
+        scatter(on_vector, 2, whole)
+        for t, third in ((1, 1), (3, 0), (1, 2), (3, 1), (3, 2)):
             scatter(on_scalar, t, pieces(THIRDS if t == 1 else LAST_THIRDS)[third])
         for t in range(LANES):
             nc.sync.dma_start(out_lanes[t], windows[t][:])

@@ -13,6 +13,7 @@ E5M2X4 = mybir.dt.float8_e5m2_x4
 ACT = mybir.ActivationFunctionType
 MULT = mybir.AluOpType.mult
 ADD = mybir.AluOpType.add
+SUBTRACT = mybir.AluOpType.subtract
 
 P = 128
 LANES = 4
@@ -24,21 +25,19 @@ T = 2048
 PER_COL = 16
 MARGIN = 16
 BLOCK = 32
-HALVES = (0, 512, 1024)
+TW_SHARE = 512
+TABLE_SHARES = (512, 512, 512, 576)
+PAIR_SHARES = (512, 544, 512, 512)
+E_CUTS = (832, 704, 192, SLOTS)
+E_LONGEST = (832, 704, 832, SLOTS)
 THIRDS = (0, 384, 768, SLOTS)
 LAST_THIRDS = (0, 256, 640, SLOTS)
-PRODUCTS = ((0, 256, SLOTS), THIRDS, (0, SLOTS), (0, 256, SLOTS))
-TW_SHARE = 384
-RUN = T // P
-SHARE = 576
-LAST_SHARE = 384
-E_SHARES = (512, 448)
-E_WINDOW = 640 + MARGIN
-PIECE = 256
-VECTOR_PIECES = 2
-GPSIMD_PIECES = 6
+PRODUCTS = (THIRDS, (0, 704, SLOTS), (0, SLOTS), (0, 256, SLOTS))
+PIECE = 128
+CALL = 256
+LATE_PIECES = 4
 STORES = (0, 512, 1024, 1536, 2048)
-KIB = 1024
+LINE = 64
 
 FLOPS = 2 * M * D * X
 
@@ -61,53 +60,48 @@ def tile_attend_gfm_mlp_pl_kernel(tc, vT, W, dz, tw, offs, boffs, soffs, out_0, 
         out_scales = out_2.rearrange("a (q r) (j c) -> (a q) j r c", r=4, j=4).bitcast(I32)
 
         places = {
-            "table3": 0,
-            "h_turned2": 0,
-            "h_squared1": 2,
-            "early_words": 0,
-            "late_words": 52,
-            "tw_listed": 8,
-            "table2": 24,
-            "pairs1": 24,
-            "h_turned0": 28,
-            "dv12": 38.5,
-            "dv11": 37,
-            "slope3": 37,
-            "h_squared3": 44,
-            "dv01": 45,
-            "dz_raw1": 40,
-            "slope0": 40,
-            "pairs3": 84,
-            "dv00": 84,
-            "dv10": 85,
-            "e_listed1_384": 86.5,
-            "dv20": 52,
-            "row": 16,
-            "window0": 16,
-            "ones": 56,
-            "window1": 56,
-            "column": 64,
-            "window2": 64,
-            "w_bf": 72,
-            "window3": 72,
+            "table1": 32768,
+            "table2": 40960,
+            "ones": 40960 - LINE,
+            "listed3": 61440 - LINE,
+            "w_bf": 49152 - LINE,
+            "dz_codes": 43072,
+            "h_turned0": 40960 + LINE,
+            "dz_raw1": 49152,
+            "dz_raw0": 53248,
+            "table0": 49152 + LINE,
+            "w_raw": 61440,
+            "table3": 69632,
+            "tw_window": 61440 + LINE,
+            "h_squared2": 65536,
+            "e2": 45760,
+            "e3": 49152,
+            "h_turned1": 45120,
+            "pairs2": 57344,
+            "w_codes0": 114176,
+            "pairs3": 114176,
+                                    "dv10": 82240,
+            "h_squared1": 85056 - LINE,
+            "h_last": 85056 - LINE,
+            "dv11": 85056,
+            "e_rest1": 114176,
+            "s_last": 123648 - LINE,
+            "dv00": 123648,
+            "e_listed2": 125184,
+            "e_listed1": 91712,
+            "dv02": 91712,
+            "dv20": 118272,
+            "late_words": 118272,
+            "tw_listed": 99840,
+            "early_words": 99840,
+            "pairs0": 103936,
+            "pairs1": 108032,
         }
 
         def tile(name, shape, dtype=F32):
             if name in places:
-                return reused.tile(shape, dtype, name=name, offset=int(places[name] * KIB), align_bytes=64)
+                return reused.tile(shape, dtype, name=name, offset=places[name], align_bytes=64)
             return keep.tile(shape, dtype, name=name, align_bytes=64)
-
-        idx_list = lists.tile([P, SLOTS // PER_COL], U16, name="idx_list")
-        bag_list = lists.tile([P, SLOTS // PER_COL], U16, name="bag_list")
-        slot_list = lists.tile([P, SLOTS // PER_COL], U16, name="slot_list")
-        dz_raw = [tile(f"dz_raw{half}", [P, LANES, X // 2]) for half in range(2)]
-        w_raw = tile("w_raw", [P, LANES, D])
-        identity = tile("identity", [P, P])
-        table, listed, pairs, h_turned, h_squared, slope, dh, e_listed, dv = {}, {}, {}, {}, {}, {}, {}, {}, {}
-
-        def load_table(t):
-            table[t] = tile(f"table{t}", [P, T])
-            nc.sync.dma_start(table[t][:], vT_lanes[t])
 
         def entries(a_list, part):
             return a_list[:, part.start // PER_COL : part.stop // PER_COL]
@@ -118,74 +112,79 @@ def tile_attend_gfm_mlp_pl_kernel(tc, vT, W, dz, tw, offs, boffs, soffs, out_0, 
         def on_scalar(out, in_):
             nc.scalar.activation(out, in_, ACT.Copy)
 
-        def shared(vector_share):
-            return ((on_vector, slice(0, vector_share)), (on_scalar, slice(vector_share, SLOTS)))
+        def gather(move, out, window, a_list, part):
+            move(out[:, part], window[:].indirect(entries(a_list, part)))
 
-        def gather(out, window, a_list, shares):
-            for move, part in shares:
-                move(out[:, part], window[:].indirect(entries(a_list, part)))
+        def gather_shared(out, window, a_list, vector_share):
+            gather(on_vector, out, window, a_list, slice(0, vector_share))
+            gather(on_scalar, out, window, a_list, slice(vector_share, SLOTS))
 
-        tw_runs = tile("tw_runs", [P, RUN])
-        nc.sync.dma_start(tw_runs[:], tw[0].rearrange("(n m) -> n m", m=RUN))
-        load_table(0)
-        nc.sync.dma_start(idx_list[:], offs)
-        nc.sync.dma_start(slot_list[:], soffs)
-        load_table(1)
-        load_table(2)
-        for half in range(2):
-            nc.sync.dma_start(dz_raw[half][:], dz.rearrange("(p j) (h x) -> h p j x", j=LANES, h=2)[half])
-        nc.sync.dma_start(w_raw[:], W.rearrange("(p j) d -> p j d", j=LANES))
-        load_table(3)
-        nc.sync.dma_start(bag_list[:], boffs)
+        idx_list = lists.tile([P, SLOTS // PER_COL], U16, name="idx_list")
+        bag_list = lists.tile([P, SLOTS // PER_COL], U16, name="bag_list")
+        slot_list = lists.tile([P, SLOTS // PER_COL], U16, name="slot_list")
+        table, listed, pairs, h_turned, h_squared, dh, e, e_listed, dv, windows = {}, {}, {}, {}, {}, {}, {}, {}, {}, {}
 
-        warm = tile("warm", [P, 2])
-        nc.vector.memset(warm[:, 0:1], 0.0)
-        nc.scalar.activation(warm[:, 1:2], warm[:, 0:1], ACT.Tanh)
-        ones = tile("ones", [P, BLOCK])
-        column = tile("column", [P, BLOCK])
-        row = tile("row", [P, BLOCK])
-        nc.vector.memset(ones[:], 1.0)
-        nc.vector.memset(identity[:], 0.0)
-        nc.vector.tensor_tensor_scan(column[:], ones[:], ones[:], 0.0, MULT, ADD)
-        nc.vector.transpose(row[:], column[:])
-        for first in range(0, P, BLOCK):
-            block = slice(first, first + BLOCK)
-            nc.vector.tensor_tensor(identity[block, block], row[block, :], column[block, :], mybir.AluOpType.is_equal)
-        windows = {}
-        tw_all = tile("tw_all", [P, T])
-        for bank in range(LANES):
-            spread = psum.tile([P, X], F32, name=f"spread{bank}", tag=f"dh{bank}")
-            for i in range(LANES):
-                m = LANES * bank + i
-                nc.tensor.transpose(spread[:, i * P : (i + 1) * P], tw_runs[:, m : m + 1].to_broadcast([P, P]), identity[:])
-            move = on_vector if bank % 2 == 0 else on_scalar
-            move(
-                tw_all[:].rearrange("p (n b i) -> p n b i", b=LANES, i=LANES)[:, :, bank, :],
-                spread[:].rearrange("p (i n) -> p n i", i=LANES),
-            )
-        e = [tile(f"e{t}", [P, E_WINDOW]) for t in range(LANES)]
-        for t in range(LANES):
-            nc.gpsimd.memset(e[t][:, X:], 0.0)
-        for t in range(LANES - 1):
+        def load_table(t):
+            table[t] = tile(f"table{t}", [P, T])
+            nc.sync.dma_start(table[t][:], vT_lanes[t])
+
+        def zero_window(t):
             windows[t] = tile(f"window{t}", [P, T])
             nc.gpsimd.memset(windows[t][:], 0.0)
 
-        def gather_table(t, shares):
+        def open_e(t):
+            e[t] = tile(f"e{t}", [P, max(E_LONGEST[t], X) + MARGIN])
+            nc.gpsimd.memset(e[t][:, X:], 0.0)
+
+        nc.sync.dma_start(idx_list[:], offs)
+        load_table(0)
+        nc.sync.dma_start(slot_list[:], soffs)
+        nc.sync.dma_start(bag_list[:], boffs)
+
+        tw_window = tile("tw_window", [P, T])
+        nc.gpsimd.memset(tw_window[:, : T // 2], 0.0)
+        for part in pieces((T // 2, 3 * T // 4 - 1, T)):
+            nc.vector.memset(tw_window[:, part], 0.0)
+        nc.scalar.dma_start(tw_window[0:1, :], tw[0:1, :])
+        warm = tile("warm", [P, 2])
+        nc.vector.memset(warm[:, 0:1], 0.0)
+        nc.scalar.activation(warm[:, 1:2], warm[:, 0:1], ACT.Tanh)
+
+        identity_wide = tile("identity", [P, P + 1])
+        identity = identity_wide[:, :P]
+        ones = tile("ones", [P, BLOCK + 1])
+        column = tile("column", [P, BLOCK])
+        row = tile("row", [P, BLOCK])
+        nc.vector.memset(ones[:], 1.0)
+        nc.vector.memset(identity_wide[:], 0.0)
+        nc.vector.tensor_tensor_scan(column[:], ones[:, :BLOCK], ones[:, :BLOCK], 0.0, MULT, ADD)
+        nc.vector.transpose(row[:], column[:])
+        for first in range(0, P, BLOCK):
+            block = slice(first, first + BLOCK)
+            nc.vector.tensor_tensor(identity_wide[block, block], row[block, :], column[block, :], mybir.AluOpType.is_equal)
+        load_table(1)
+        load_table(2)
+        for t in range(LANES):
+            zero_window(t)
+        for t in range(2):
+            open_e(t)
+
+        def gather_table(t):
             listed[t] = tile(f"listed{t}", [P, SLOTS])
-            gather(listed[t], table[t], idx_list, shares)
+            gather_shared(listed[t], table[t], idx_list, TABLE_SHARES[t])
 
-        def gather_pairs(t, shares):
+        def gather_pairs(t):
             pairs[t] = tile(f"pairs{t}", [P, SLOTS])
-            gather(pairs[t], listed[t], slot_list, shares)
+            gather_shared(pairs[t], listed[t], slot_list, PAIR_SHARES[t])
 
-        def squash(t):
+        def pool(t):
             s_turned = psum.tile([P, X], F32, name=f"s_turned{t}", tag=f"sum{t % 2}")
             for blk in range(X // P):
                 for j in range(2):
                     nc.tensor.matmul(
                         s_turned[:, blk * P : (blk + 1) * P],
                         lhsT=pairs[t][:, 2 * P * blk + j : 2 * P * (blk + 1) : 2],
-                        rhs=identity[:],
+                        rhs=identity,
                         is_transpose=True,
                         start=(j == 0),
                         stop=(j == 1),
@@ -197,71 +196,84 @@ def tile_attend_gfm_mlp_pl_kernel(tc, vT, W, dz, tw, offs, boffs, soffs, out_0, 
             h = psum.tile([P, X], F32, name=f"h{t}", tag=f"h{t % 2}")
             for blk in range(X // P):
                 cols = slice(blk * P, (blk + 1) * P)
-                nc.tensor.transpose(h[:, cols], h_turned[t][:, cols], identity[:])
+                nc.tensor.transpose(h[:, cols], h_turned[t][:, cols], identity)
             h_squared[t] = tile(f"h_squared{t}", [P, X])
             nc.scalar.activation(h_squared[t][:], h[:], ACT.Square)
 
-        def squash_and_square_last(t):
-            s = tile("s_last", [P, X])
-            nc.gpsimd.tensor_tensor(s[:], pairs[t][:, 0:SLOTS:2], pairs[t][:, 1:SLOTS:2], ADD)
-            h = tile("h_last", [P, X])
-            nc.scalar.activation(h[:], s[:], ACT.Tanh)
-            h_squared[t] = tile(f"h_squared{t}", [P, X])
-            nc.scalar.activation(h_squared[t][:], h[:], ACT.Square)
+        gather_table(0)
+        dz_raw = [tile(f"dz_raw{half}", [P, LANES, X // 2]) for half in range(2)]
+        for half in range(2):
+            nc.sync.dma_start(dz_raw[half][:], dz.rearrange("(p j) (h x) -> h p j x", j=LANES, h=2)[half])
+        tw_row = tile("tw_row", [P, SLOTS])
+        gather_shared(tw_row, tw_window, idx_list, TW_SHARE)
+        parked = out_0[0:1, :SLOTS]
+        nc.sync.dma_start(parked, tw_row[0:1, :])
+        w_raw = tile("w_raw", [P, LANES, D])
+        nc.sync.dma_start(w_raw[:], W.rearrange("(p j) d -> p j d", j=LANES))
+        load_table(3)
+        tw_listed = tile("tw_listed", [P, SLOTS])
+        nc.sync.dma_start(tw_listed[:], parked[0].partition_broadcast(P))
 
-        def form_slope(t):
-            slope[t] = tile(f"slope{t}", [P, X])
-            nc.gpsimd.tensor_scalar(slope[t][:], h_squared[t][:], -1.0, 1.0, MULT, ADD)
+        gather_pairs(0)
+        gather_table(1)
+        gather_table(2)
+        pool(0)
+        gather_pairs(1)
+        gather_pairs(2)
+        square(0)
+        pool(1)
+        pool(2)
+        square(1)
 
-        def dense_backward():
-            w_bf = tile("w_bf", [P, LANES * D], BF16)
-            dz_bf = tile("dz_bf", [P, LANES * X], BF16)
-            w_codes = tile("w_codes", [P, D], U32)
-            w_scales = tile("w_scales", [P, D], U8)
-            dz_codes = tile("dz_codes", [P, X], U32)
-            dz_scales = tile("dz_scales", [P, X], U8)
-            for half in range(2):
-                nc.gpsimd.tensor_scalar(
-                    dz_bf[:].rearrange("p (x j) -> p x j", j=LANES)[:, half * X // 2 : (half + 1) * X // 2],
-                    dz_raw[half][:].rearrange("p j x -> p x j"),
-                    1.0,
-                    -0.0,
-                    MULT,
-                    ADD,
-                )
-            nc.vector.tensor_copy(
-                w_bf[:].rearrange("p (t q j) -> p q t j", t=LANES, j=LANES),
-                w_raw[:].rearrange("p j (q t) -> p q t j", t=LANES),
+        w_bf = tile("w_bf", [P, LANES * D], BF16)
+        dz_bf = tile("dz_bf", [P, LANES * X], BF16)
+        w_parts = pieces((0, P, D))
+        w_codes = [tile(f"w_codes{i}", [P, part.stop - part.start], U32) for i, part in enumerate(w_parts)]
+        w_scales = [tile(f"w_scales{i}", [P, part.stop - part.start], U8) for i, part in enumerate(w_parts)]
+        dz_codes = tile("dz_codes", [P, X], U32)
+        dz_scales = tile("dz_scales", [P, X], U8)
+        for half in range(2):
+            nc.gpsimd.tensor_scalar(
+                dz_bf[:].rearrange("p (x j) -> p x j", j=LANES)[:, half * X // 2 : (half + 1) * X // 2],
+                dz_raw[half][:].rearrange("p j x -> p x j"),
+                -1.0,
+                0.0,
+                MULT,
+                ADD,
             )
-            nc.vector.quantize_mx(dz_codes[:].bitcast(E5M2X4), dz_scales[:], dz_bf[:])
-            nc.vector.quantize_mx(w_codes[:].bitcast(E4M3X4), w_scales[:], w_bf[:])
-            for t in range(LANES):
-                cols = slice(t * P, (t + 1) * P)
-                dh[t] = psum.tile([P, X], F32, name=f"dh{t}", tag=f"dh{t}")
-                nc.tensor.matmul_mx(
-                    dh[t][:],
-                    lhsT=w_codes[:, cols].bitcast(E4M3X4),
-                    lhsT_scale=w_scales[:, cols],
-                    rhs=dz_codes[:].bitcast(E5M2X4),
-                    rhs_scale=dz_scales[:],
-                    start=True,
-                    stop=True,
-                )
+        nc.vector.tensor_copy(
+            w_bf[:].rearrange("p (t q j) -> p q t j", t=LANES, j=LANES),
+            w_raw[:].rearrange("p j (q t) -> p q t j", t=LANES),
+        )
+        nc.vector.quantize_mx(dz_codes[:].bitcast(E5M2X4), dz_scales[:], dz_bf[:])
+        for i, part in enumerate(w_parts):
+            nc.vector.quantize_mx(w_codes[i][:].bitcast(E4M3X4), w_scales[i][:], w_bf[:, LANES * part.start : LANES * part.stop])
+        for t in range(LANES):
+            i = min(t, 1)
+            cols = slice(t * P - w_parts[i].start, (t + 1) * P - w_parts[i].start)
+            dh[t] = psum.tile([P, X], F32, name=f"dh{t}", tag=f"dh{t}")
+            nc.tensor.matmul_mx(
+                dh[t][:],
+                lhsT=w_codes[i][:, cols].bitcast(E4M3X4),
+                lhsT_scale=w_scales[i][:, cols],
+                rhs=dz_codes[:].bitcast(E5M2X4),
+                rhs_scale=dz_scales[:],
+                start=True,
+                stop=True,
+            )
 
         def form_e(t):
-            nc.vector.tensor_tensor(e[t][:, :X], dh[t][:], slope[t][:], MULT)
+            nc.vector.scalar_tensor_tensor(e[t][:, :X], h_squared[t][:], 1.0, dh[t][:], SUBTRACT, MULT)
 
-        def gather_e(t, span, shares):
-            listed_e = tile(f"e_listed{t}_{span.start}", [P, span.stop - span.start])
-            e_listed[t, span.start] = listed_e
-            for move, part in shares:
-                move(listed_e[:, part.start - span.start : part.stop - span.start], e[t][:].indirect(entries(bag_list, part)))
+        def gather_e(move, t, part):
+            if t not in e_listed:
+                e_listed[t] = tile(f"e_listed{t}", [P, E_CUTS[t] if t == 1 else SLOTS])
+            gather(move, e_listed[t], e[t], bag_list, part)
 
         def weigh(t, piece):
             part = pieces(PRODUCTS[t])[piece]
             dv[t, piece] = tile(f"dv{t}{piece}", [P, part.stop - part.start])
-            first = max(start for lane, start in e_listed if lane == t and start <= part.start)
-            listed_e = e_listed[t, first][:, part.start - first : part.stop - first]
+            listed_e = e_rest1[:] if (t, piece) == (1, 1) else e_listed[t][:, part]
             nc.gpsimd.tensor_tensor(dv[t, piece][:], listed_e, tw_listed[:, part], MULT)
 
         def scatter(move, t, part):
@@ -269,64 +281,55 @@ def tile_attend_gfm_mlp_pl_kernel(tc, vT, W, dz, tw, offs, boffs, soffs, out_0, 
             at = part.start - PRODUCTS[t][piece]
             move(windows[t][:].indirect(entries(idx_list, part)), dv[t, piece][:, at : at + part.stop - part.start])
 
-        gather_table(0, shared(SLOTS // 2))
-        gather_pairs(0, shared(SLOTS // 2))
-        tw_listed = tile("tw_listed", [P, SLOTS])
-        gather(tw_listed, tw_all, idx_list, shared(TW_SHARE))
-        gather_table(1, shared(SHARE))
-        gather_table(2, shared(SHARE))
-        squash(0)
-        gather_pairs(1, shared(SHARE))
-        gather_pairs(2, shared(LAST_SHARE))
-        square(0)
-        squash(1)
-        dense_backward()
-        form_slope(0)
-        windows[3] = tile("window3", [P, T])
-        nc.gpsimd.memset(windows[3][:], 0.0)
-        gather_table(3, shared(LAST_SHARE))
-        form_e(0)
-        gather_pairs(3, shared(SLOTS // 2))
-        square(1)
-        form_slope(1)
-        squash(2)
-        whole = slice(0, SLOTS)
-        first_third, other_thirds = pieces((0, THIRDS[1], SLOTS))
-        form_e(1)
-        gather_e(0, whole, [(on_vector, half) for half in pieces(HALVES)])
-        gather_e(1, first_third, [(on_scalar, first_third)])
-        squash_and_square_last(3)
+        def head(t):
+            return slice(0, E_CUTS[t])
+
+        def rest(t):
+            return slice(E_CUTS[t], SLOTS)
+
+        gather_table(3)
+        for t in range(2, LANES):
+            open_e(t)
         square(2)
-        form_slope(2)
-        form_slope(3)
-        weigh(0, 0)
-        weigh(1, 0)
-        gather_e(1, other_thirds, [(on_scalar, other_thirds)])
-        scatter(on_vector, 0, pieces(PRODUCTS[0])[0])
-        scatter(on_scalar, 1, first_third)
+        form_e(0)
+        gather_pairs(3)
+        s_last = tile("s_last", [P, X])
+        nc.gpsimd.tensor_tensor(s_last[:], pairs[3][:, 0:SLOTS:2], pairs[3][:, 1:SLOTS:2], ADD)
+        form_e(1)
         form_e(2)
+        gather_e(on_scalar, 0, head(0))
+        gather_e(on_vector, 0, rest(0))
+        gather_e(on_vector, 1, head(1))
+        weigh(0, 1)
+        h_last = tile("h_last", [P, X])
+        nc.scalar.activation(h_last[:], s_last[:], ACT.Tanh)
+        e_rest1 = tile("e_rest1", [P, SLOTS - E_CUTS[1]])
+        on_scalar(e_rest1[:], e[1][:].indirect(entries(bag_list, rest(1))))
+        weigh(0, 0)
+        h_squared[3] = tile("h_squared3", [P, X])
+        nc.scalar.activation(h_squared[3][:], h_last[:], ACT.Square)
+        gather_e(on_scalar, 2, head(2))
+        gather_e(on_vector, 2, rest(2))
+        scatter(on_scalar, 0, pieces(THIRDS)[0])
         form_e(3)
-        gather_e(2, whole, shared(E_SHARES[0]))
-        gather_e(3, whole, shared(E_SHARES[1]))
-        for t, piece in ((0, 1), (1, 1), (3, 0), (1, 2), (2, 0), (3, 1)):
+        gather_e(on_scalar, 3, head(3))
+        for t, piece in ((1, 1), (1, 0), (2, 0), (3, 0), (0, 2), (3, 1)):
             weigh(t, piece)
-        scatter(on_vector, 0, pieces(PRODUCTS[0])[1])
-        scatter(on_vector, 2, whole)
-        for t, third in ((1, 1), (3, 0), (1, 2), (3, 1), (3, 2)):
-            scatter(on_scalar, t, pieces(THIRDS if t == 1 else LAST_THIRDS)[third])
-        for t in range(LANES):
+        for part in reversed(pieces(PRODUCTS[1])):
+            scatter(on_vector, 1, part)
+        scatter(on_vector, 2, slice(0, SLOTS))
+        for t, third in ((0, 1), (3, 0), (0, 2), (3, 1), (3, 2)):
+            scatter(on_scalar, t, pieces(THIRDS if t == 0 else LAST_THIRDS)[third])
+        for t in (1, 0, 2, 3):
             nc.sync.dma_start(out_lanes[t], windows[t][:])
 
-        early_words = tile("early_words", [P, GPSIMD_PIECES * PIECE * LANES], BF16)
-        late_words = tile("late_words", [P, (T // PIECE - GPSIMD_PIECES) * PIECE * LANES], BF16)
+        count = T // PIECE
+        early_words = tile("early_words", [P, (count - LATE_PIECES) * PIECE * LANES], BF16)
+        late_words = tile("late_words", [P, LATE_PIECES * PIECE * LANES], BF16)
+        late, early = pieces((0, LATE_PIECES, count))
 
         def pair_words(run):
-            if run.start < late.start:
-                words, first = early_words, 0
-            elif run.start < late.stop:
-                words, first = late_words, late.start
-            else:
-                words, first = early_words, late.stop - late.start
+            words, first = (late_words, 0) if run.start < late.stop else (early_words, late.stop)
             return words[:, (run.start - first) * PIECE * LANES : (run.stop - first) * PIECE * LANES]
 
         def round_lane(copy, t, run):
@@ -336,12 +339,9 @@ def tile_attend_gfm_mlp_pl_kernel(tc, vT, W, dz, tw, offs, boffs, soffs, out_0, 
         def on_gpsimd(out, in_):
             nc.gpsimd.tensor_scalar(out, in_, 1.0, -0.0, MULT, ADD)
 
-        first_run, late, last_run = pieces((0, VECTOR_PIECES, VECTOR_PIECES + T // PIECE - GPSIMD_PIECES, T // PIECE))
-        for t in range(2):
-            round_lane(on_gpsimd, t, first_run)
-            round_lane(on_gpsimd, t, last_run)
-        for run in (first_run, last_run):
-            round_lane(on_vector, 2, run)
+        for t in (1, 0):
+            round_lane(on_gpsimd, t, early)
+        round_lane(on_vector, 2, early)
         for t in range(3):
             round_lane(on_vector, t, late)
         rounded = tile("rounded", [P, T * LANES], BF16)
@@ -353,21 +353,21 @@ def tile_attend_gfm_mlp_pl_kernel(tc, vT, W, dz, tw, offs, boffs, soffs, out_0, 
 
         def quantize_and_store(cols):
             words = keep.tile([P, cols.stop - cols.start], U32, name=f"words{cols.start}", align_bytes=64)
-            for first in range(cols.start, cols.stop, PIECE):
+            for first in range(cols.start, cols.stop, CALL):
                 nc.vector.quantize_mx(
-                    words[:, first - cols.start : first - cols.start + PIECE].bitcast(E4M3X4),
-                    scales[4 * (first // 512) : P, first % 512 : first % 512 + PIECE],
-                    rounded[:, LANES * first : LANES * (first + PIECE)],
+                    words[:, first - cols.start : first - cols.start + CALL].bitcast(E4M3X4),
+                    scales[4 * (first // 512) : P, first % 512 : first % 512 + CALL],
+                    rounded[:, LANES * first : LANES * (first + CALL)],
                 )
             nc.sync.dma_start(out_words[:, cols], words[:].bitcast(I32))
 
-        for run in (late, first_run, slice(4, 6)):
+        for run in (slice(late.stop, 8), late, slice(8, 12)):
             round_lane(on_vector, 3, run)
-        weave(nc.vector.tensor_copy, I32, first_run)
-        round_lane(on_vector, 3, slice(6, 8))
+        weave(nc.vector.tensor_copy, I32, late)
+        round_lane(on_vector, 3, slice(12, count))
         quantize_and_store(pieces(STORES)[0])
-        for k in range(VECTOR_PIECES, T // PIECE):
-            weave(nc.scalar.copy, U32, slice(k, k + 1))
+        for k in range(late.stop, count, CALL // PIECE):
+            weave(nc.scalar.copy, U32, slice(k, k + CALL // PIECE))
         for cols in pieces(STORES)[1:]:
             quantize_and_store(cols)
         for q in range(4):

@@ -28,8 +28,8 @@ BLOCK = 32
 TW_SHARE = 512
 TABLE_SHARES = (512, 512, 512, 576)
 PAIR_SHARES = (512, 544, 512, 512)
-E_CUTS = (832, 704, 192, SLOTS)
-E_LONGEST = (832, 704, 832, SLOTS)
+E_CUTS = (832, 704, 64, SLOTS)
+E_LONGEST = (832, 704, 960, SLOTS)
 THIRDS = (0, 384, 768, SLOTS)
 LAST_THIRDS = (0, 256, 640, SLOTS)
 PRODUCTS = (THIRDS, (0, 704, SLOTS), (0, SLOTS), (0, 256, SLOTS))
@@ -74,7 +74,7 @@ def tile_attend_gfm_mlp_pl_kernel(tc, vT, W, dz, tw, offs, boffs, soffs, out_0, 
             "table3": 69632,
             "tw_window": 61440 + LINE,
             "h_squared2": 65536,
-            "e2": 45760,
+            "e2": 45248,
             "e3": 49152,
             "h_turned1": 45120,
             "pairs2": 57344,

@@ -28,14 +28,13 @@ BLOCK = 32
 TW_SHARE = 512
 TABLE_SHARES = (512, 512, 512, 576)
 PAIR_SHARES = (512, 544, 512, 512)
-E_CUTS = (832, 704, 64, SLOTS)
-E_LONGEST = (832, 704, 960, SLOTS)
-THIRDS = (0, 384, 768, SLOTS)
-LAST_THIRDS = (0, 256, 640, SLOTS)
-PRODUCTS = (THIRDS, (0, 704, SLOTS), (0, SLOTS), (0, 256, SLOTS))
+E_CUTS = (768, 640, 64, SLOTS)
+E_LONGEST = (768, 640, 960, SLOTS)
+THIRDS = (0, 256, 640, SLOTS)
+PRODUCTS = (THIRDS, (0, 640, SLOTS), (0, SLOTS), (0, 256, SLOTS))
 PIECE = 128
 CALL = 256
-LATE_PIECES = 4
+VECTOR_PIECES = 4
 STORES = (0, 512, 1024, 1536, 2048)
 LINE = 64
 
@@ -80,7 +79,7 @@ def tile_attend_gfm_mlp_pl_kernel(tc, vT, W, dz, tw, offs, boffs, soffs, out_0, 
             "pairs2": 57344,
             "w_codes0": 114176,
             "pairs3": 114176,
-                                    "dv10": 82240,
+                                    "dv10": 121088,
             "h_squared1": 85056 - LINE,
             "h_last": 85056 - LINE,
             "dv11": 85056,
@@ -90,10 +89,9 @@ def tile_attend_gfm_mlp_pl_kernel(tc, vT, W, dz, tw, offs, boffs, soffs, out_0, 
             "e_listed2": 125184,
             "e_listed1": 91712,
             "dv02": 91712,
-            "dv20": 118272,
-            "late_words": 118272,
+            "dv20": 80896,
             "tw_listed": 99840,
-            "early_words": 99840,
+            "pair_words": 99840,
             "pairs0": 103936,
             "pairs1": 108032,
         }
@@ -306,6 +304,7 @@ def tile_attend_gfm_mlp_pl_kernel(tc, vT, W, dz, tw, offs, boffs, soffs, out_0, 
         e_rest1 = tile("e_rest1", [P, SLOTS - E_CUTS[1]])
         on_scalar(e_rest1[:], e[1][:].indirect(entries(bag_list, rest(1))))
         weigh(0, 0)
+        weigh(1, 0)
         h_squared[3] = tile("h_squared3", [P, X])
         nc.scalar.activation(h_squared[3][:], h_last[:], ACT.Square)
         gather_e(on_scalar, 2, head(2))
@@ -313,43 +312,35 @@ def tile_attend_gfm_mlp_pl_kernel(tc, vT, W, dz, tw, offs, boffs, soffs, out_0, 
         scatter(on_scalar, 0, pieces(THIRDS)[0])
         form_e(3)
         gather_e(on_scalar, 3, head(3))
-        for t, piece in ((1, 1), (1, 0), (2, 0), (3, 0), (0, 2), (3, 1)):
+        for t, piece in ((1, 1), (2, 0), (3, 0), (0, 2), (3, 1)):
             weigh(t, piece)
-        for part in reversed(pieces(PRODUCTS[1])):
+        for part in pieces(PRODUCTS[1]):
             scatter(on_vector, 1, part)
         scatter(on_vector, 2, slice(0, SLOTS))
         for t, third in ((0, 1), (3, 0), (0, 2), (3, 1), (3, 2)):
-            scatter(on_scalar, t, pieces(THIRDS if t == 0 else LAST_THIRDS)[third])
+            scatter(on_scalar, t, pieces(THIRDS)[third])
         for t in (1, 0, 2, 3):
             nc.sync.dma_start(out_lanes[t], windows[t][:])
 
         count = T // PIECE
-        early_words = tile("early_words", [P, (count - LATE_PIECES) * PIECE * LANES], BF16)
-        late_words = tile("late_words", [P, LATE_PIECES * PIECE * LANES], BF16)
-        late, early = pieces((0, LATE_PIECES, count))
-
-        def pair_words(run):
-            words, first = (late_words, 0) if run.start < late.stop else (early_words, late.stop)
-            return words[:, (run.start - first) * PIECE * LANES : (run.stop - first) * PIECE * LANES]
+        pair_words = tile("pair_words", [P, T * LANES], BF16)
 
         def round_lane(copy, t, run):
-            halves = pair_words(run).rearrange("p (k u c l) -> p k u c l", u=2, c=PIECE, l=2)
-            copy(halves[:, :, t // 2, :, t % 2], windows[t][:].rearrange("p (k c) -> p k c", c=PIECE)[:, run, :])
+            halves = pair_words[:].rearrange("p (k u c l) -> p k u c l", u=2, c=PIECE, l=2)
+            copy(halves[:, run, t // 2, :, t % 2], windows[t][:].rearrange("p (k c) -> p k c", c=PIECE)[:, run, :])
 
         def on_gpsimd(out, in_):
             nc.gpsimd.tensor_scalar(out, in_, 1.0, -0.0, MULT, ADD)
 
         for t in (1, 0):
-            round_lane(on_gpsimd, t, early)
-        round_lane(on_vector, 2, early)
-        for t in range(3):
-            round_lane(on_vector, t, late)
+            round_lane(on_gpsimd, t, slice(0, count))
+        round_lane(on_vector, 2, slice(0, count))
         rounded = tile("rounded", [P, T * LANES], BF16)
         scales = tile("scales", [P, T // 4], U8)
 
         def weave(copy, dtype, run):
             out = rounded[:].bitcast(dtype).rearrange("p (k c u) -> p k c u", c=PIECE, u=2)
-            copy(out[:, run], pair_words(run).bitcast(dtype).rearrange("p (k u c) -> p k c u", u=2, c=PIECE))
+            copy(out[:, run], pair_words[:].bitcast(dtype).rearrange("p (k u c) -> p k c u", u=2, c=PIECE)[:, run])
 
         def quantize_and_store(cols):
             words = keep.tile([P, cols.stop - cols.start], U32, name=f"words{cols.start}", align_bytes=64)
@@ -361,12 +352,12 @@ def tile_attend_gfm_mlp_pl_kernel(tc, vT, W, dz, tw, offs, boffs, soffs, out_0, 
                 )
             nc.sync.dma_start(out_words[:, cols], words[:].bitcast(I32))
 
-        for run in (slice(late.stop, 8), late, slice(8, 12)):
+        for run in (slice(VECTOR_PIECES, 8), slice(0, VECTOR_PIECES), slice(8, 12)):
             round_lane(on_vector, 3, run)
-        weave(nc.vector.tensor_copy, I32, late)
+        weave(nc.vector.tensor_copy, I32, slice(0, VECTOR_PIECES))
         round_lane(on_vector, 3, slice(12, count))
         quantize_and_store(pieces(STORES)[0])
-        for k in range(late.stop, count, CALL // PIECE):
+        for k in range(VECTOR_PIECES, count, CALL // PIECE):
             weave(nc.scalar.copy, U32, slice(k, k + CALL // PIECE))
         for cols in pieces(STORES)[1:]:
             quantize_and_store(cols)

@@ -25,18 +25,23 @@ T = 2048
 PER_COL = 16
 MARGIN = 16
 BLOCK = 32
+GROUP = 512
+LINE = 64
+
 TW_SHARE = 512
 TABLE_SHARES = (512, 512, 512, 576)
 PAIR_SHARES = (512, 544, 512, 512)
-E_CUTS = (768, 640, 64, SLOTS)
-E_LONGEST = (768, 640, 960, SLOTS)
-THIRDS = (0, 256, 640, SLOTS)
-PRODUCTS = (THIRDS, (0, 640, SLOTS), (0, SLOTS), (0, 256, SLOTS))
+E_CUTS = (768, 896, 384, SLOTS)
+E_LONGEST = (768, 896, 640, SLOTS)
+THIRDS = (0, 384, 768, SLOTS)
+LAST_THIRDS = (0, 256, 640, SLOTS)
+PRODUCTS = (THIRDS, (0, 384, SLOTS), (0, SLOTS), (0, 256, SLOTS))
 PIECE = 128
 CALL = 256
-VECTOR_PIECES = 4
+FIRST_PIECES = 4
+LATE_PIECES = 2
+LAST_RUN = 12
 STORES = (0, 512, 1024, 1536, 2048)
-LINE = 64
 
 FLOPS = 2 * M * D * X
 
@@ -56,42 +61,42 @@ def tile_attend_gfm_mlp_pl_kernel(tc, vT, W, dz, tw, offs, boffs, soffs, out_0, 
         vT_lanes = vT.rearrange("(p t) c -> t p c", t=LANES)
         out_lanes = out_0.rearrange("(p t) c -> t p c", t=LANES)
         out_words = out_1.rearrange("a p c l -> p (a c l)").bitcast(I32)
-        out_scales = out_2.rearrange("a (q r) (j c) -> (a q) j r c", r=4, j=4).bitcast(I32)
+        out_scales = out_2.rearrange("a (q r) (j c) -> (a q) j r c", r=4, j=T // GROUP).bitcast(I32)
 
         places = {
             "table1": 32768,
-            "table2": 40960,
             "ones": 40960 - LINE,
-            "listed3": 61440 - LINE,
-            "w_bf": 49152 - LINE,
-            "dz_codes": 43072,
+            "table2": 40960,
             "h_turned0": 40960 + LINE,
+            "dz_codes": 43072,
+            "h_turned1": 45120,
+            "w_bf": 49152 - LINE,
+            "table0": 49152 + LINE,
             "dz_raw1": 49152,
             "dz_raw0": 53248,
-            "table0": 49152 + LINE,
+            "tw_window": 61440 + LINE,
             "w_raw": 61440,
             "table3": 69632,
-            "tw_window": 61440 + LINE,
-            "h_squared2": 65536,
-            "e2": 45248,
+            "e2": 46528,
             "e3": 49152,
-            "h_turned1": 45120,
             "pairs2": 57344,
+            "listed3": 61440 - LINE,
+            "h_squared2": 65536,
             "w_codes0": 114176,
             "pairs3": 114176,
-                                    "dv10": 121088,
             "h_squared1": 85056 - LINE,
             "h_last": 85056 - LINE,
             "dv11": 85056,
-            "e_rest1": 114176,
+            "dv10": 122112,
             "s_last": 123648 - LINE,
             "dv00": 123648,
             "e_listed2": 125184,
             "e_listed1": 91712,
             "dv02": 91712,
             "dv20": 80896,
+            "late_words": 80896,
             "tw_listed": 99840,
-            "pair_words": 99840,
+            "early_words": 99840,
             "pairs0": 103936,
             "pairs1": 108032,
         }
@@ -131,7 +136,7 @@ def tile_attend_gfm_mlp_pl_kernel(tc, vT, W, dz, tw, offs, boffs, soffs, out_0, 
             nc.gpsimd.memset(windows[t][:], 0.0)
 
         def open_e(t):
-            e[t] = tile(f"e{t}", [P, max(E_LONGEST[t], X) + MARGIN])
+            e[t] = tile(f"e{t}", [P, E_LONGEST[t] + MARGIN])
             nc.gpsimd.memset(e[t][:, X:], 0.0)
 
         nc.sync.dma_start(idx_list[:], offs)
@@ -265,19 +270,18 @@ def tile_attend_gfm_mlp_pl_kernel(tc, vT, W, dz, tw, offs, boffs, soffs, out_0, 
 
         def gather_e(move, t, part):
             if t not in e_listed:
-                e_listed[t] = tile(f"e_listed{t}", [P, E_CUTS[t] if t == 1 else SLOTS])
+                e_listed[t] = tile(f"e_listed{t}", [P, SLOTS])
             gather(move, e_listed[t], e[t], bag_list, part)
 
-        def weigh(t, piece):
-            part = pieces(PRODUCTS[t])[piece]
-            dv[t, piece] = tile(f"dv{t}{piece}", [P, part.stop - part.start])
-            listed_e = e_rest1[:] if (t, piece) == (1, 1) else e_listed[t][:, part]
-            nc.gpsimd.tensor_tensor(dv[t, piece][:], listed_e, tw_listed[:, part], MULT)
+        def weigh(t, nr):
+            part = pieces(PRODUCTS[t])[nr]
+            dv[t, nr] = tile(f"dv{t}{nr}", [P, part.stop - part.start])
+            nc.gpsimd.tensor_tensor(dv[t, nr][:], e_listed[t][:, part], tw_listed[:, part], MULT)
 
         def scatter(move, t, part):
-            piece = sum(edge <= part.start for edge in PRODUCTS[t][1:])
-            at = part.start - PRODUCTS[t][piece]
-            move(windows[t][:].indirect(entries(idx_list, part)), dv[t, piece][:, at : at + part.stop - part.start])
+            nr = sum(edge <= part.start for edge in PRODUCTS[t][1:])
+            at = part.start - PRODUCTS[t][nr]
+            move(windows[t][:].indirect(entries(idx_list, part)), dv[t, nr][:, at : at + part.stop - part.start])
 
         def head(t):
             return slice(0, E_CUTS[t])
@@ -296,13 +300,12 @@ def tile_attend_gfm_mlp_pl_kernel(tc, vT, W, dz, tw, offs, boffs, soffs, out_0, 
         form_e(1)
         form_e(2)
         gather_e(on_scalar, 0, head(0))
-        gather_e(on_vector, 0, rest(0))
         gather_e(on_vector, 1, head(1))
+        gather_e(on_scalar, 1, rest(1))
+        gather_e(on_vector, 0, rest(0))
         weigh(0, 1)
         h_last = tile("h_last", [P, X])
         nc.scalar.activation(h_last[:], s_last[:], ACT.Tanh)
-        e_rest1 = tile("e_rest1", [P, SLOTS - E_CUTS[1]])
-        on_scalar(e_rest1[:], e[1][:].indirect(entries(bag_list, rest(1))))
         weigh(0, 0)
         weigh(1, 0)
         h_squared[3] = tile("h_squared3", [P, X])
@@ -312,55 +315,70 @@ def tile_attend_gfm_mlp_pl_kernel(tc, vT, W, dz, tw, offs, boffs, soffs, out_0, 
         scatter(on_scalar, 0, pieces(THIRDS)[0])
         form_e(3)
         gather_e(on_scalar, 3, head(3))
-        for t, piece in ((1, 1), (2, 0), (3, 0), (0, 2), (3, 1)):
-            weigh(t, piece)
+        for t, nr in ((1, 1), (2, 0), (3, 0), (0, 2), (3, 1)):
+            weigh(t, nr)
         for part in pieces(PRODUCTS[1]):
             scatter(on_vector, 1, part)
         scatter(on_vector, 2, slice(0, SLOTS))
         for t, third in ((0, 1), (3, 0), (0, 2), (3, 1), (3, 2)):
-            scatter(on_scalar, t, pieces(THIRDS)[third])
+            scatter(on_scalar, t, pieces(THIRDS if t == 0 else LAST_THIRDS)[third])
         for t in (1, 0, 2, 3):
             nc.sync.dma_start(out_lanes[t], windows[t][:])
 
         count = T // PIECE
-        pair_words = tile("pair_words", [P, T * LANES], BF16)
+        early_words = tile("early_words", [P, (count - LATE_PIECES) * PIECE * LANES], BF16)
+        late_words = tile("late_words", [P, LATE_PIECES * PIECE * LANES], BF16)
+        first_run, late, last_run = pieces((0, FIRST_PIECES, FIRST_PIECES + LATE_PIECES, count))
+
+        def pair_words(run):
+            if run.start < late.start:
+                pair_tile, first = early_words, 0
+            elif run.start < late.stop:
+                pair_tile, first = late_words, late.start
+            else:
+                pair_tile, first = early_words, LATE_PIECES
+            return pair_tile[:, (run.start - first) * PIECE * LANES : (run.stop - first) * PIECE * LANES]
 
         def round_lane(copy, t, run):
-            halves = pair_words[:].rearrange("p (k u c l) -> p k u c l", u=2, c=PIECE, l=2)
-            copy(halves[:, run, t // 2, :, t % 2], windows[t][:].rearrange("p (k c) -> p k c", c=PIECE)[:, run, :])
+            halves = pair_words(run).rearrange("p (k u c l) -> p k u c l", u=2, c=PIECE, l=2)
+            copy(halves[:, :, t // 2, :, t % 2], windows[t][:].rearrange("p (k c) -> p k c", c=PIECE)[:, run, :])
 
         def on_gpsimd(out, in_):
             nc.gpsimd.tensor_scalar(out, in_, 1.0, -0.0, MULT, ADD)
 
         for t in (1, 0):
-            round_lane(on_gpsimd, t, slice(0, count))
-        round_lane(on_vector, 2, slice(0, count))
+            round_lane(on_gpsimd, t, first_run)
+            round_lane(on_gpsimd, t, last_run)
+        for run in (first_run, last_run):
+            round_lane(on_vector, 2, run)
+        for t in range(LANES - 1):
+            round_lane(on_vector, t, late)
         rounded = tile("rounded", [P, T * LANES], BF16)
-        scales = tile("scales", [P, T // 4], U8)
+        scales = tile("scales", [P, GROUP], U8)
 
         def weave(copy, dtype, run):
             out = rounded[:].bitcast(dtype).rearrange("p (k c u) -> p k c u", c=PIECE, u=2)
-            copy(out[:, run], pair_words[:].bitcast(dtype).rearrange("p (k u c) -> p k c u", u=2, c=PIECE)[:, run])
+            copy(out[:, run], pair_words(run).bitcast(dtype).rearrange("p (k u c) -> p k c u", u=2, c=PIECE))
 
         def quantize_and_store(cols):
-            words = keep.tile([P, cols.stop - cols.start], U32, name=f"words{cols.start}", align_bytes=64)
+            words = tile(f"words{cols.start}", [P, cols.stop - cols.start], U32)
             for first in range(cols.start, cols.stop, CALL):
                 nc.vector.quantize_mx(
                     words[:, first - cols.start : first - cols.start + CALL].bitcast(E4M3X4),
-                    scales[4 * (first // 512) : P, first % 512 : first % 512 + CALL],
+                    scales[4 * (first // GROUP) : P, first % GROUP : first % GROUP + CALL],
                     rounded[:, LANES * first : LANES * (first + CALL)],
                 )
             nc.sync.dma_start(out_words[:, cols], words[:].bitcast(I32))
 
-        for run in (slice(VECTOR_PIECES, 8), slice(0, VECTOR_PIECES), slice(8, 12)):
+        for run in (late, first_run, slice(late.stop, LAST_RUN)):
             round_lane(on_vector, 3, run)
-        weave(nc.vector.tensor_copy, I32, slice(0, VECTOR_PIECES))
-        round_lane(on_vector, 3, slice(12, count))
+        weave(nc.vector.tensor_copy, I32, first_run)
+        round_lane(on_vector, 3, slice(LAST_RUN, count))
         quantize_and_store(pieces(STORES)[0])
-        for k in range(VECTOR_PIECES, count, CALL // PIECE):
+        for k in range(FIRST_PIECES, count, CALL // PIECE):
             weave(nc.scalar.copy, U32, slice(k, k + CALL // PIECE))
         for cols in pieces(STORES)[1:]:
             quantize_and_store(cols)
-        for q in range(4):
+        for q in range(P // BLOCK):
             queue = nc.sync if q % 2 == 0 else nc.scalar
-            queue.dma_start(out_scales[q], scales[32 * q : 32 * q + 16, :].bitcast(I32))
+            queue.dma_start(out_scales[q], scales[BLOCK * q : BLOCK * q + 16, :].bitcast(I32))

@@ -41,7 +41,7 @@ CALL = 256
 FIRST_PIECES = 4
 LATE_PIECES = 2
 LAST_RUN = 12
-STORES = (0, 512, 1024, 1536, 2048)
+STORES = (0, 768, 1280, 1792, 2048)
 
 FLOPS = 2 * M * D * X
 
@@ -360,25 +360,28 @@ def tile_attend_gfm_mlp_pl_kernel(tc, vT, W, dz, tw, offs, boffs, soffs, out_0, 
             out = rounded[:].bitcast(dtype).rearrange("p (k c u) -> p k c u", c=PIECE, u=2)
             copy(out[:, run], pair_words(run).bitcast(dtype).rearrange("p (k u c) -> p k c u", u=2, c=PIECE))
 
-        def quantize_and_store(cols):
-            words = tile(f"words{cols.start}", [P, cols.stop - cols.start], U32)
-            for first in range(cols.start, cols.stop, CALL):
-                nc.vector.quantize_mx(
-                    words[:, first - cols.start : first - cols.start + CALL].bitcast(E4M3X4),
-                    scales[4 * (first // GROUP) : P, first % GROUP : first % GROUP + CALL],
-                    rounded[:, LANES * first : LANES * (first + CALL)],
-                )
-            nc.sync.dma_start(out_words[:, cols], words[:].bitcast(I32))
+        stores = [(cols, tile(f"words{cols.start}", [P, cols.stop - cols.start], U32)) for cols in pieces(STORES)]
+
+        def quantize_and_store(first):
+            cols, words = [store for store in stores if store[0].start <= first][-1]
+            nc.vector.quantize_mx(
+                words[:, first - cols.start : first - cols.start + CALL].bitcast(E4M3X4),
+                scales[4 * (first // GROUP) : P, first % GROUP : first % GROUP + CALL],
+                rounded[:, LANES * first : LANES * (first + CALL)],
+            )
+            if first + CALL == cols.stop:
+                nc.sync.dma_start(out_words[:, cols], words[:].bitcast(I32))
 
         for run in (late, first_run, slice(late.stop, LAST_RUN)):
             round_lane(on_vector, 3, run)
         weave(nc.vector.tensor_copy, I32, first_run)
         round_lane(on_vector, 3, slice(LAST_RUN, count))
-        quantize_and_store(pieces(STORES)[0])
+        for first in range(0, FIRST_PIECES * PIECE, CALL):
+            quantize_and_store(first)
         for k in range(FIRST_PIECES, count, CALL // PIECE):
             weave(nc.scalar.copy, U32, slice(k, k + CALL // PIECE))
-        for cols in pieces(STORES)[1:]:
-            quantize_and_store(cols)
+        for first in range(FIRST_PIECES * PIECE, T, CALL):
+            quantize_and_store(first)
         for q in range(P // BLOCK):
             queue = nc.sync if q % 2 == 0 else nc.scalar
             queue.dma_start(out_scales[q], scales[BLOCK * q : BLOCK * q + 16, :].bitcast(I32))

@@ -31,14 +31,15 @@ LINE = 64
 TW_SHARE = 512
 TABLE_SHARES = (512, 512, 512, 576)
 PAIR_SHARES = (512, 544, 512, 512)
-E_CUTS = (768, 896, 384, SLOTS)
+E_CUTS = (768, 896, 512, SLOTS)
 E_LONGEST = (768, 896, 640, SLOTS)
 THIRDS = (0, 384, 768, SLOTS)
 LAST_THIRDS = (0, 256, 640, SLOTS)
 PRODUCTS = (THIRDS, (0, 384, SLOTS), (0, SLOTS), (0, 256, SLOTS))
 PIECE = 128
 CALL = 256
-FIRST_PIECES = 4
+FIRST_PIECES = 6
+SCALAR_PIECES = 6
 LATE_PIECES = 2
 LAST_RUN = 12
 STORES = (0, 768, 1280, 1792, 2048)
@@ -64,6 +65,9 @@ def tile_attend_gfm_mlp_pl_kernel(tc, vT, W, dz, tw, offs, boffs, soffs, out_0, 
         out_scales = out_2.rearrange("a (q r) (j c) -> (a q) j r c", r=4, j=T // GROUP).bitcast(I32)
 
         places = {
+            "one": 0,
+            "after_lane_2": 0,
+            "rounded": 0,
             "table1": 32768,
             "ones": 40960 - LINE,
             "table2": 40960,
@@ -165,6 +169,8 @@ def tile_attend_gfm_mlp_pl_kernel(tc, vT, W, dz, tw, offs, boffs, soffs, out_0, 
         for first in range(0, P, BLOCK):
             block = slice(first, first + BLOCK)
             nc.vector.tensor_tensor(identity_wide[block, block], row[block, :], column[block, :], mybir.AluOpType.is_equal)
+        one = tile("one", [P, 1])
+        nc.vector.memset(one[:], 1.0)
         load_table(1)
         load_table(2)
         for t in range(LANES):
@@ -349,10 +355,15 @@ def tile_attend_gfm_mlp_pl_kernel(tc, vT, W, dz, tw, offs, boffs, soffs, out_0, 
         for t in (1, 0):
             round_lane(on_gpsimd, t, first_run)
             round_lane(on_gpsimd, t, last_run)
-        for run in (first_run, last_run):
-            round_lane(on_vector, 2, run)
+        def on_vector_times_one(out, in_):
+            nc.vector.tensor_scalar_mul(out, in_, one[:])
+
+        round_lane(on_vector_times_one, 2, first_run)
+        after_lane_2 = tile("after_lane_2", [P, 1])
+        nc.gpsimd.memset(after_lane_2[:], 1.0)
         for t in range(LANES - 1):
             round_lane(on_vector, t, late)
+        round_lane(on_vector, 2, last_run)
         rounded = tile("rounded", [P, T * LANES], BF16)
         scales = tile("scales", [P, GROUP], U8)
 
@@ -372,10 +383,14 @@ def tile_attend_gfm_mlp_pl_kernel(tc, vT, W, dz, tw, offs, boffs, soffs, out_0, 
             if first + CALL == cols.stop:
                 nc.sync.dma_start(out_words[:, cols], words[:].bitcast(I32))
 
-        for run in (late, first_run, slice(late.stop, LAST_RUN)):
+        def on_scalar_in_turn(out, in_):
+            nc.scalar.activation(out, in_, ACT.Copy, scale=after_lane_2[:])
+
+        round_lane(on_scalar_in_turn, 3, slice(0, SCALAR_PIECES))
+        for run in (late, slice(late.stop, LAST_RUN)):
             round_lane(on_vector, 3, run)
-        weave(nc.vector.tensor_copy, I32, first_run)
         round_lane(on_vector, 3, slice(LAST_RUN, count))
+        weave(nc.vector.tensor_copy, I32, first_run)
         for first in range(0, FIRST_PIECES * PIECE, CALL):
             quantize_and_store(first)
         for k in range(FIRST_PIECES, count, CALL // PIECE):

@@ -31,7 +31,7 @@ LINE = 64
 TW_SHARE = 512
 TABLE_SHARES = (512, 512, 512, 576)
 PAIR_SHARES = (512, 544, 512, 512)
-E_CUTS = (768, 896, 512, SLOTS)
+E_CUTS = (768, 896, 384, SLOTS)
 E_LONGEST = (768, 896, 640, SLOTS)
 THIRDS = (0, 384, 768, SLOTS)
 LAST_THIRDS = (0, 256, 640, SLOTS)
@@ -39,7 +39,7 @@ PRODUCTS = (THIRDS, (0, 384, SLOTS), (0, SLOTS), (0, 256, SLOTS))
 PIECE = 128
 CALL = 256
 FIRST_PIECES = 6
-SCALAR_PIECES = 6
+SCALAR_PIECES = 4
 LATE_PIECES = 2
 LAST_RUN = 12
 STORES = (0, 768, 1280, 1792, 2048)
@@ -67,6 +67,7 @@ def tile_attend_gfm_mlp_pl_kernel(tc, vT, W, dz, tw, offs, boffs, soffs, out_0, 
         places = {
             "one": 0,
             "after_lane_2": 0,
+            "dv31": LINE,
             "rounded": 0,
             "table1": 32768,
             "ones": 40960 - LINE,
@@ -171,6 +172,8 @@ def tile_attend_gfm_mlp_pl_kernel(tc, vT, W, dz, tw, offs, boffs, soffs, out_0, 
             nc.vector.tensor_tensor(identity_wide[block, block], row[block, :], column[block, :], mybir.AluOpType.is_equal)
         one = tile("one", [P, 1])
         nc.vector.memset(one[:], 1.0)
+        other_one = tile("other_one", [P, 1])
+        nc.vector.memset(other_one[:], 1.0)
         load_table(1)
         load_table(2)
         for t in range(LANES):
@@ -358,9 +361,10 @@ def tile_attend_gfm_mlp_pl_kernel(tc, vT, W, dz, tw, offs, boffs, soffs, out_0, 
         def on_vector_times_one(out, in_):
             nc.vector.tensor_scalar_mul(out, in_, one[:])
 
-        round_lane(on_vector_times_one, 2, first_run)
-        after_lane_2 = tile("after_lane_2", [P, 1])
-        nc.gpsimd.memset(after_lane_2[:], 1.0)
+        round_lane(on_vector_times_one, 2, slice(0, SCALAR_PIECES))
+        round_lane(on_vector, 2, slice(SCALAR_PIECES, FIRST_PIECES))
+        after_lane_2 = tile("after_lane_2", [P, 2 * MARGIN])
+        nc.scalar.activation(after_lane_2[:, 0:1], other_one[:], ACT.Copy)
         for t in range(LANES - 1):
             round_lane(on_vector, t, late)
         round_lane(on_vector, 2, last_run)
@@ -384,10 +388,10 @@ def tile_attend_gfm_mlp_pl_kernel(tc, vT, W, dz, tw, offs, boffs, soffs, out_0, 
                 nc.sync.dma_start(out_words[:, cols], words[:].bitcast(I32))
 
         def on_scalar_in_turn(out, in_):
-            nc.scalar.activation(out, in_, ACT.Copy, scale=after_lane_2[:])
+            nc.scalar.activation(out, in_, ACT.Copy, scale=after_lane_2[:, 0:1])
 
         round_lane(on_scalar_in_turn, 3, slice(0, SCALAR_PIECES))
-        for run in (late, slice(late.stop, LAST_RUN)):
+        for run in (late, slice(SCALAR_PIECES, FIRST_PIECES), slice(late.stop, LAST_RUN)):
             round_lane(on_vector, 3, run)
         round_lane(on_vector, 3, slice(LAST_RUN, count))
         weave(nc.vector.tensor_copy, I32, first_run)

@@ -38,8 +38,7 @@ LAST_THIRDS = (0, 256, 640, SLOTS)
 PRODUCTS = (THIRDS, (0, 384, SLOTS), (0, SLOTS), (0, 256, SLOTS))
 PIECE = 128
 CALL = 256
-FIRST_PIECES = 6
-SCALAR_PIECES = 4
+FIRST_PIECES = 4
 LATE_PIECES = 2
 LAST_RUN = 12
 STORES = (0, 768, 1280, 1792, 2048)
@@ -361,8 +360,7 @@ def tile_attend_gfm_mlp_pl_kernel(tc, vT, W, dz, tw, offs, boffs, soffs, out_0, 
         def on_vector_times_one(out, in_):
             nc.vector.tensor_scalar_mul(out, in_, one[:])
 
-        round_lane(on_vector_times_one, 2, slice(0, SCALAR_PIECES))
-        round_lane(on_vector, 2, slice(SCALAR_PIECES, FIRST_PIECES))
+        round_lane(on_vector_times_one, 2, first_run)
         after_lane_2 = tile("after_lane_2", [P, 2 * MARGIN])
         nc.scalar.activation(after_lane_2[:, 0:1], other_one[:], ACT.Copy)
         for t in range(LANES - 1):
@@ -390,8 +388,8 @@ def tile_attend_gfm_mlp_pl_kernel(tc, vT, W, dz, tw, offs, boffs, soffs, out_0, 
         def on_scalar_in_turn(out, in_):
             nc.scalar.activation(out, in_, ACT.Copy, scale=after_lane_2[:, 0:1])
 
-        round_lane(on_scalar_in_turn, 3, slice(0, SCALAR_PIECES))
-        for run in (late, slice(SCALAR_PIECES, FIRST_PIECES), slice(late.stop, LAST_RUN)):
+        round_lane(on_scalar_in_turn, 3, first_run)
+        for run in (late, slice(late.stop, LAST_RUN)):
             round_lane(on_vector, 3, run)
         round_lane(on_vector, 3, slice(LAST_RUN, count))
         weave(nc.vector.tensor_copy, I32, first_run)

from contextlib import ExitStack

import concourse.mybir as mybir

F32 = mybir.dt.float32
BF16 = mybir.dt.bfloat16
I32 = mybir.dt.int32
U32 = mybir.dt.uint32
U16 = mybir.dt.uint16
U8 = mybir.dt.uint8
E4M3X4 = mybir.dt.float8_e4m3fn_x4
E5M2X4 = mybir.dt.float8_e5m2_x4
ACT = mybir.ActivationFunctionType
MULT = mybir.AluOpType.mult
ADD = mybir.AluOpType.add
SUBTRACT = mybir.AluOpType.subtract

P = 128
LANES = 4
D = 512
M = 512
X = 512
SLOTS = 1024
T = 2048
PER_COL = 16
MARGIN = 16
BLOCK = 32
GROUP = 512
LINE = 64

TW_SHARE = 512
TABLE_SHARES = (512, 512, 512, 576)
PAIR_SHARES = (512, 544, 512, 512)
E_CUTS = (768, 896, 384, SLOTS)
E_LONGEST = (768, 896, 640, SLOTS)
THIRDS = (0, 384, 768, SLOTS)
LAST_THIRDS = (0, 256, 640, SLOTS)
PRODUCTS = (THIRDS, (0, 384, SLOTS), (0, SLOTS), (0, 256, SLOTS))
PIECE = 128
CALL = 256
FIRST_PIECES = 4
LATE_PIECES = 2
LAST_RUN = 12
STORES = (0, 768, 1280, 1792, 2048)

FLOPS = 2 * M * D * X


def pieces(edges):
    return [slice(a, b) for a, b in zip(edges, edges[1:])]


def tile_attend_gfm_mlp_pl_kernel(tc, vT, W, dz, tw, offs, boffs, soffs, out_0, out_1, out_2):
    nc = tc.nc
    with ExitStack() as ctx:
        lists = ctx.enter_context(tc.tile_pool(name="lists", bufs=1))
        keep = ctx.enter_context(tc.tile_pool(name="keep", bufs=1))
        reused = ctx.enter_context(tc.tile_pool(name="reused", bufs=1))
        psum = ctx.enter_context(tc.psum_pool(name="psum", bufs=1))

        vT_lanes = vT.rearrange("(p t) c -> t p c", t=LANES)
        out_lanes = out_0.rearrange("(p t) c -> t p c", t=LANES)
        out_words = out_1.rearrange("a p c l -> p (a c l)").bitcast(I32)
        out_scales = out_2.rearrange("a (q r) (j c) -> (a q) j r c", r=4, j=T // GROUP).bitcast(I32)

        places = {
            "one": 0,
            "after_lane_2": 0,
            "dv31": LINE,
            "rounded": 0,
            "table1": 32768,
            "ones": 40960 - LINE,
            "table2": 40960,
            "h_turned0": 40960 + LINE,
            "dz_codes": 43072,
            "h_turned1": 45120,
            "w_bf": 49152 - LINE,
            "table0": 49152 + LINE,
            "dz_raw1": 49152,
            "dz_raw0": 53248,
            "tw_window": 61440 + LINE,
            "w_raw": 61440,
            "table3": 69632,
            "e2": 46528,
            "e3": 49152,
            "pairs2": 57344,
            "listed3": 61440 - LINE,
            "h_squared2": 65536,
            "w_codes0": 114176,
            "pairs3": 114176,
            "h_squared1": 85056 - LINE,
            "h_last": 85056 - LINE,
            "dv11": 85056,
            "dv10": 122112,
            "s_last": 123648 - LINE,
            "dv00": 123648,
            "e_listed2": 125184,
            "e_listed1": 91712,
            "dv02": 91712,
            "dv20": 80896,
            "late_words": 80896,
            "tw_listed": 99840,
            "early_words": 99840,
            "pairs0": 103936,
            "pairs1": 108032,
        }

        def tile(name, shape, dtype=F32):
            if name in places:
                return reused.tile(shape, dtype, name=name, offset=places[name], align_bytes=64)
            return keep.tile(shape, dtype, name=name, align_bytes=64)

        def entries(a_list, part):
            return a_list[:, part.start // PER_COL : part.stop // PER_COL]

        def on_vector(out, in_):
            nc.vector.tensor_copy(out, in_)

        def on_scalar(out, in_):
            nc.scalar.activation(out, in_, ACT.Copy)

        def gather(move, out, window, a_list, part):
            move(out[:, part], window[:].indirect(entries(a_list, part)))

        def gather_shared(out, window, a_list, vector_share):
            gather(on_vector, out, window, a_list, slice(0, vector_share))
            gather(on_scalar, out, window, a_list, slice(vector_share, SLOTS))

        idx_list = lists.tile([P, SLOTS // PER_COL], U16, name="idx_list")
        bag_list = lists.tile([P, SLOTS // PER_COL], U16, name="bag_list")
        slot_list = lists.tile([P, SLOTS // PER_COL], U16, name="slot_list")
        table, listed, pairs, h_turned, h_squared, dh, e, e_listed, dv, windows = {}, {}, {}, {}, {}, {}, {}, {}, {}, {}

        def load_table(t):
            table[t] = tile(f"table{t}", [P, T])
            nc.sync.dma_start(table[t][:], vT_lanes[t])

        def zero_window(t):
            windows[t] = tile(f"window{t}", [P, T])
            nc.gpsimd.memset(windows[t][:], 0.0)

        def open_e(t):
            e[t] = tile(f"e{t}", [P, E_LONGEST[t] + MARGIN])
            nc.gpsimd.memset(e[t][:, X:], 0.0)

        nc.sync.dma_start(idx_list[:], offs)
        load_table(0)
        nc.sync.dma_start(slot_list[:], soffs)
        nc.sync.dma_start(bag_list[:], boffs)

        tw_window = tile("tw_window", [P, T])
        nc.gpsimd.memset(tw_window[:, : T // 2], 0.0)
        for part in pieces((T // 2, 3 * T // 4 - 1, T)):
            nc.vector.memset(tw_window[:, part], 0.0)
        nc.scalar.dma_start(tw_window[0:1, :], tw[0:1, :])
        warm = tile("warm", [P, 2])
        nc.vector.memset(warm[:, 0:1], 0.0)
        nc.scalar.activation(warm[:, 1:2], warm[:, 0:1], ACT.Tanh)

        identity_wide = tile("identity", [P, P + 1])
        identity = identity_wide[:, :P]
        ones = tile("ones", [P, BLOCK + 1])
        column = tile("column", [P, BLOCK])
        row = tile("row", [P, BLOCK])
        nc.vector.memset(ones[:], 1.0)
        nc.vector.memset(identity_wide[:], 0.0)
        nc.vector.tensor_tensor_scan(column[:], ones[:, :BLOCK], ones[:, :BLOCK], 0.0, MULT, ADD)
        nc.vector.transpose(row[:], column[:])
        for first in range(0, P, BLOCK):
            block = slice(first, first + BLOCK)
            nc.vector.tensor_tensor(identity_wide[block, block], row[block, :], column[block, :], mybir.AluOpType.is_equal)
        one = tile("one", [P, 1])
        nc.vector.memset(one[:], 1.0)
        other_one = tile("other_one", [P, 1])
        nc.vector.memset(other_one[:], 1.0)
        load_table(1)
        load_table(2)
        for t in range(LANES):
            zero_window(t)
        for t in range(2):
            open_e(t)

        def gather_table(t):
            listed[t] = tile(f"listed{t}", [P, SLOTS])
            gather_shared(listed[t], table[t], idx_list, TABLE_SHARES[t])

        def gather_pairs(t):
            pairs[t] = tile(f"pairs{t}", [P, SLOTS])
            gather_shared(pairs[t], listed[t], slot_list, PAIR_SHARES[t])

        def pool(t):
            s_turned = psum.tile([P, X], F32, name=f"s_turned{t}", tag=f"sum{t % 2}")
            for blk in range(X // P):
                for j in range(2):
                    nc.tensor.matmul(
                        s_turned[:, blk * P : (blk + 1) * P],
                        lhsT=pairs[t][:, 2 * P * blk + j : 2 * P * (blk + 1) : 2],
                        rhs=identity,
                        is_transpose=True,
                        start=(j == 0),
                        stop=(j == 1),
                    )
            h_turned[t] = tile(f"h_turned{t}", [P, X])
            nc.scalar.activation(h_turned[t][:], s_turned[:], ACT.Tanh)

        def square(t):
            h = psum.tile([P, X], F32, name=f"h{t}", tag=f"h{t % 2}")
            for blk in range(X // P):
                cols = slice(blk * P, (blk + 1) * P)
                nc.tensor.transpose(h[:, cols], h_turned[t][:, cols], identity)
            h_squared[t] = tile(f"h_squared{t}", [P, X])
            nc.scalar.activation(h_squared[t][:], h[:], ACT.Square)

        gather_table(0)
        dz_raw = [tile(f"dz_raw{half}", [P, LANES, X // 2]) for half in range(2)]
        for half in range(2):
            nc.sync.dma_start(dz_raw[half][:], dz.rearrange("(p j) (h x) -> h p j x", j=LANES, h=2)[half])
        tw_row = tile("tw_row", [P, SLOTS])
        gather_shared(tw_row, tw_window, idx_list, TW_SHARE)
        parked = out_0[0:1, :SLOTS]
        nc.sync.dma_start(parked, tw_row[0:1, :])
        w_raw = tile("w_raw", [P, LANES, D])
        nc.sync.dma_start(w_raw[:], W.rearrange("(p j) d -> p j d", j=LANES))
        load_table(3)
        tw_listed = tile("tw_listed", [P, SLOTS])
        nc.sync.dma_start(tw_listed[:], parked[0].partition_broadcast(P))

        gather_pairs(0)
        gather_table(1)
        gather_table(2)
        pool(0)
        gather_pairs(1)
        gather_pairs(2)
        square(0)
        pool(1)
        pool(2)
        square(1)

        w_bf = tile("w_bf", [P, LANES * D], BF16)
        dz_bf = tile("dz_bf", [P, LANES * X], BF16)
        w_parts = pieces((0, P, D))
        w_codes = [tile(f"w_codes{i}", [P, part.stop - part.start], U32) for i, part in enumerate(w_parts)]
        w_scales = [tile(f"w_scales{i}", [P, part.stop - part.start], U8) for i, part in enumerate(w_parts)]
        dz_codes = tile("dz_codes", [P, X], U32)
        dz_scales = tile("dz_scales", [P, X], U8)
        for half in range(2):
            nc.gpsimd.tensor_scalar(
                dz_bf[:].rearrange("p (x j) -> p x j", j=LANES)[:, half * X // 2 : (half + 1) * X // 2],
                dz_raw[half][:].rearrange("p j x -> p x j"),
                -1.0,
                0.0,
                MULT,
                ADD,
            )
        nc.vector.tensor_copy(
            w_bf[:].rearrange("p (t q j) -> p q t j", t=LANES, j=LANES),
            w_raw[:].rearrange("p j (q t) -> p q t j", t=LANES),
        )
        nc.vector.quantize_mx(dz_codes[:].bitcast(E5M2X4), dz_scales[:], dz_bf[:])
        for i, part in enumerate(w_parts):
            nc.vector.quantize_mx(w_codes[i][:].bitcast(E4M3X4), w_scales[i][:], w_bf[:, LANES * part.start : LANES * part.stop])
        for t in range(LANES):
            i = min(t, 1)
            cols = slice(t * P - w_parts[i].start, (t + 1) * P - w_parts[i].start)
            dh[t] = psum.tile([P, X], F32, name=f"dh{t}", tag=f"dh{t}")
            nc.tensor.matmul_mx(
                dh[t][:],
                lhsT=w_codes[i][:, cols].bitcast(E4M3X4),
                lhsT_scale=w_scales[i][:, cols],
                rhs=dz_codes[:].bitcast(E5M2X4),
                rhs_scale=dz_scales[:],
                start=True,
                stop=True,
            )

        def form_e(t):
            nc.vector.scalar_tensor_tensor(e[t][:, :X], h_squared[t][:], 1.0, dh[t][:], SUBTRACT, MULT)

        def gather_e(move, t, part):
            if t not in e_listed:
                e_listed[t] = tile(f"e_listed{t}", [P, SLOTS])
            gather(move, e_listed[t], e[t], bag_list, part)

        def weigh(t, nr):
            part = pieces(PRODUCTS[t])[nr]
            dv[t, nr] = tile(f"dv{t}{nr}", [P, part.stop - part.start])
            nc.gpsimd.tensor_tensor(dv[t, nr][:], e_listed[t][:, part], tw_listed[:, part], MULT)

        def scatter(move, t, part):
            nr = sum(edge <= part.start for edge in PRODUCTS[t][1:])
            at = part.start - PRODUCTS[t][nr]
            move(windows[t][:].indirect(entries(idx_list, part)), dv[t, nr][:, at : at + part.stop - part.start])

        def head(t):
            return slice(0, E_CUTS[t])

        def rest(t):
            return slice(E_CUTS[t], SLOTS)

        gather_table(3)
        for t in range(2, LANES):
            open_e(t)
        square(2)
        form_e(0)
        gather_pairs(3)
        s_last = tile("s_last", [P, X])
        nc.gpsimd.tensor_tensor(s_last[:], pairs[3][:, 0:SLOTS:2], pairs[3][:, 1:SLOTS:2], ADD)
        form_e(1)
        form_e(2)
        gather_e(on_scalar, 0, head(0))
        gather_e(on_vector, 1, head(1))
        gather_e(on_scalar, 1, rest(1))
        gather_e(on_vector, 0, rest(0))
        weigh(0, 1)
        h_last = tile("h_last", [P, X])
        nc.scalar.activation(h_last[:], s_last[:], ACT.Tanh)
        weigh(0, 0)
        weigh(1, 0)
        h_squared[3] = tile("h_squared3", [P, X])
        nc.scalar.activation(h_squared[3][:], h_last[:], ACT.Square)
        gather_e(on_scalar, 2, head(2))
        gather_e(on_vector, 2, rest(2))
        scatter(on_scalar, 0, pieces(THIRDS)[0])
        form_e(3)
        gather_e(on_scalar, 3, head(3))
        for t, nr in ((1, 1), (2, 0), (3, 0), (0, 2), (3, 1)):
            weigh(t, nr)
        for part in pieces(PRODUCTS[1]):
            scatter(on_vector, 1, part)
        scatter(on_vector, 2, slice(0, SLOTS))
        for t, third in ((0, 1), (3, 0), (0, 2), (3, 1), (3, 2)):
            scatter(on_scalar, t, pieces(THIRDS if t == 0 else LAST_THIRDS)[third])
        for t in (1, 0, 2, 3):
            nc.sync.dma_start(out_lanes[t], windows[t][:])

        count = T // PIECE
        early_words = tile("early_words", [P, (count - LATE_PIECES) * PIECE * LANES], BF16)
        late_words = tile("late_words", [P, LATE_PIECES * PIECE * LANES], BF16)
        first_run, late, last_run = pieces((0, FIRST_PIECES, FIRST_PIECES + LATE_PIECES, count))

        def pair_words(run):
            if run.start < late.start:
                pair_tile, first = early_words, 0
            elif run.start < late.stop:
                pair_tile, first = late_words, late.start
            else:
                pair_tile, first = early_words, LATE_PIECES
            return pair_tile[:, (run.start - first) * PIECE * LANES : (run.stop - first) * PIECE * LANES]

        def round_lane(copy, t, run):
            halves = pair_words(run).rearrange("p (k u c l) -> p k u c l", u=2, c=PIECE, l=2)
            copy(halves[:, :, t // 2, :, t % 2], windows[t][:].rearrange("p (k c) -> p k c", c=PIECE)[:, run, :])

        def on_gpsimd(out, in_):
            nc.gpsimd.tensor_scalar(out, in_, 1.0, -0.0, MULT, ADD)

        for t in (1, 0):
            round_lane(on_gpsimd, t, first_run)
            round_lane(on_gpsimd, t, last_run)
        def on_vector_times_one(out, in_):
            nc.vector.tensor_scalar_mul(out, in_, one[:])

        round_lane(on_vector_times_one, 2, first_run)
        after_lane_2 = tile("after_lane_2", [P, 2 * MARGIN])
        nc.scalar.activation(after_lane_2[:, 0:1], other_one[:], ACT.Copy)
        for t in range(LANES - 1):
            round_lane(on_vector, t, late)
        round_lane(on_vector, 2, last_run)
        rounded = tile("rounded", [P, T * LANES], BF16)
        scales = tile("scales", [P, GROUP], U8)

        def weave(copy, dtype, run):
            out = rounded[:].bitcast(dtype).rearrange("p (k c u) -> p k c u", c=PIECE, u=2)
            copy(out[:, run], pair_words(run).bitcast(dtype).rearrange("p (k u c) -> p k c u", u=2, c=PIECE))

        stores = [(cols, tile(f"words{cols.start}", [P, cols.stop - cols.start], U32)) for cols in pieces(STORES)]

        def quantize_and_store(first):
            cols, words = [store for store in stores if store[0].start <= first][-1]
            nc.vector.quantize_mx(
                words[:, first - cols.start : first - cols.start + CALL].bitcast(E4M3X4),
                scales[4 * (first // GROUP) : P, first % GROUP : first % GROUP + CALL],
                rounded[:, LANES * first : LANES * (first + CALL)],
            )
            if first + CALL == cols.stop:
                nc.sync.dma_start(out_words[:, cols], words[:].bitcast(I32))

        def on_scalar_in_turn(out, in_):
            nc.scalar.activation(out, in_, ACT.Copy, scale=after_lane_2[:, 0:1])

        round_lane(on_scalar_in_turn, 3, first_run)
        for run in (late, slice(late.stop, LAST_RUN)):
            round_lane(on_vector, 3, run)
        round_lane(on_vector, 3, slice(LAST_RUN, count))
        weave(nc.vector.tensor_copy, I32, first_run)
        for first in range(0, FIRST_PIECES * PIECE, CALL):
            quantize_and_store(first)
        for k in range(FIRST_PIECES, count, CALL // PIECE):
            weave(nc.scalar.copy, U32, slice(k, k + CALL // PIECE))
        for first in range(FIRST_PIECES * PIECE, T, CALL):
            quantize_and_store(first)
        for q in range(P // BLOCK):
            queue = nc.sync if q % 2 == 0 else nc.scalar
            queue.dma_start(out_scales[q], scales[BLOCK * q : BLOCK * q + 16, :].bitcast(I32))
